import numpy as np
import ml_dtypes


def mxq(x, axis, fmt="e4m3"):
    dtype, down = {"e4m3": (ml_dtypes.float8_e4m3fn, 7), "e5m2": (ml_dtypes.float8_e5m2, 14)}[fmt]
    v = np.moveaxis(np.asarray(x, np.float32).astype(ml_dtypes.bfloat16).astype(np.float64), axis, -1)
    blocks = v.reshape(v.shape[:-1] + (-1, 32))
    amax = np.abs(blocks).max(-1, keepdims=True)
    byte = np.maximum(np.where(amax > 0, np.frexp(amax)[1] - 1 + 127, 0) - down, 1)
    scale = np.exp2(byte - 127.0)
    codes = (blocks / scale).astype(np.float32).astype(dtype).astype(np.float64)
    return np.moveaxis((codes * scale).reshape(v.shape), -1, axis)


WIDE = False


def mx_kscale(k):
    if not WIDE:
        return np.ones(k)
    levels = np.array([10, -10, 5, -5, 0])
    if k % 512:
        return np.exp2(np.random.permutation(np.resize(levels, k // 32))).repeat(32)
    a = np.empty((k // 512, 16))
    for p in range(k // 512):
        a[p, :8] = np.random.permutation(np.resize(levels, 8))
        for g in range(8):
            far = levels[np.abs(levels - a[p, g]) >= 10]
            a[p, g + 8] = far[np.random.randint(len(far))]
    return np.exp2(a.ravel()).repeat(32)


def f64(x):
    return np.asarray(x).astype(np.float64)


def striped(idx):
    return np.tile(idx.reshape(-1, 16).T, (8, 1)).astype(np.uint16)


def unstriped(offs):
    return offs[:16].T.reshape(-1).astype(np.int64)


def silu(v):
    return v / (1.0 + np.exp(-np.maximum(v, -700.0)))


K, T, E, C, H, N = 512, 768, 12, 128, 1024, 128


def by_expert(wq, xq):
    return np.concatenate([wq[e].T @ xq[:, e * C:(e + 1) * C] for e in range(E)], axis=1)


def setup_inputs():
    n = np.random.standard_normal
    s = mx_kscale(K)[:, None]
    u = mx_kscale(H)
    first = np.random.permutation(np.repeat(np.arange(E), T // E))
    second = (first + 1 + np.random.permutation(np.repeat(np.arange(E - 1), -(-T // (E - 1)))[:T])) % E
    while np.bincount(second, minlength=E).max() != T // E:
        load = np.bincount(second, minlength=E); hi, lo = int(load.argmax()), int(load.argmin())
        t = np.flatnonzero((second == hi) & (first != lo))[0]; second[t] = lo
    slot_token = np.empty(E * C, np.int64); pos = np.empty((2, T), np.int64); fill = np.zeros(E, np.int64)
    place = np.stack([np.random.permutation(C) for _ in range(E)])
    for r, deal in enumerate((first, second)):
        for t in np.random.permutation(T):
            e = deal[t]; j = e * C + place[e, fill[e]]; fill[e] += 1; slot_token[j] = t; pos[r, t] = j
    g = np.random.uniform(0.2, 0.8, T)
    return {
        "xT": (n((K, T)) * s).astype(np.float32),
        "w1": (n((E, K, H)) / np.sqrt(K) / s[None] * u[None, None, :]).astype(np.float32),
        "w2": (n((E, H, N)) / np.sqrt(H) / u[None, :, None]).astype(np.float32),
        "gate": np.stack([np.tile(g, (N, 1)), np.tile(1.0 - g, (N, 1))]).astype(np.float32),
        "offs": striped(slot_token),
        "pos1": striped(pos[0]),
        "pos2": striped(pos[1]),
    }


def reference(xT, w1, w2, gate, offs, pos1, pos2):
    idx = unstriped(offs)
    xq = mxq(f64(xT)[:, idx], 0, "e4m3")
    h = silu(by_expert(mxq(f64(w1), 1, "e4m3"), xq))
    y = by_expert(mxq(f64(w2), 1, "e4m3"), mxq(h, 0, "e4m3"))
    return f64(gate[0]) * y[:, unstriped(pos1)] + f64(gate[1]) * y[:, unstriped(pos2)]

@@ -1,0 +1,208 @@
+from contextlib import ExitStack
+
+import concourse.mybir as mybir
+
+K, T, E, C, H, N = 512, 768, 12, 128, 1024, 128
+FLOPS = 2 * E * C * H * (K + N)
+
+F32 = mybir.dt.float32
+BF16 = mybir.dt.bfloat16
+U32 = mybir.dt.uint32
+I32 = mybir.dt.int32
+U16 = mybir.dt.uint16
+U8 = mybir.dt.uint8
+FP8X4 = mybir.dt.float8_e4m3fn_x4
+SILU = mybir.ActivationFunctionType.Silu
+MULT = mybir.AluOpType.mult
+ADD = mybir.AluOpType.add
+
+P = 128
+J = 4
+G = H // 512
+X_CHUNKS = ((0, 512), (512, 768))
+GATHERS = (512, 512, 512)
+V_SHARE = [(96, 0)] * 3 + [(128, 0)] * 7 + [(96, 16), (128, 32)]
+Y_BANKS = ((0, 1, 2, 3), (4, 5, 6, 7), (8, 9, 10), (11,))
+W2_SHARE = {(0, 1): 3, (2, 3): 4, (4, 5): 3, (6, 7): 2, (8, 9): 4, (10,): 0, (11,): 1}
+W1_GROUPS = ((0, 1), (2, 3), (4, 5), (6, 7), (8, 9), (10,), (11,))
+ORDER = [("w1", (0, 1)), ("w1", (2, 3)), ("w1", (4, 5)), ("w1", (6, 7)), ("w2", (0, 1)), ("w1", (8, 9)), ("w2", (2, 3)), ("w2", (4, 5)),
+         ("w1", (10,)), ("w2", (6, 7)), ("w1", (11,)), ("w2", (8, 9)), ("w2", (10,)), ("w2", (11,))]
+OUT_CHUNKS = (512, 256)
+RAW_BUFS = 4
+
+
+def tile_routed_moe_kernel(tc, xT, w1, w2, gate, offs, pos1, pos2, out):
+    nc = tc.nc
+    with ExitStack() as ctx:
+        keep = ctx.enter_context(tc.tile_pool(name="keep", bufs=1))
+        ring = ctx.enter_context(tc.tile_pool(name="ring", bufs=2))
+        psum = ctx.enter_context(tc.psum_pool(name="psum", bufs=2))
+
+        offs_t = keep.tile([P, E * C // 16], U16, name="offs_t")
+        pos1_t = keep.tile([P, T // 16], U16, name="pos1_t")
+        pos2_t = keep.tile([P, T // 16], U16, name="pos2_t")
+        y_all = keep.tile([P, E * C], F32, name="y_all")
+        warm = keep.tile([P, 2], F32, name="warm")
+
+        nc.vector.memset(warm[:], 0.0)
+        nc.scalar.activation(warm[:, 1:2], warm[:, 0:1], SILU)
+
+        def raw_tile(shape):
+            return ring.tile(shape, F32, name="raw", tag="raw", bufs=RAW_BUFS, align_bytes=64)
+
+        x_raw = raw_tile([P, J, T])
+        nc.sync.dma_start(out=x_raw[:], in_=xT.rearrange("(p j) n -> p j n", j=J))
+        nc.sync.dma_start(out=offs_t[:], in_=offs)
+        raw = {}
+        for i, (kind, group) in enumerate(ORDER):
+            n = len(group)
+            if kind == "w1":
+                t = raw_tile([P, n, J, H])
+                nc.sync.dma_start(out=t[:], in_=w1[group[0]:group[0] + n].rearrange("e (p j) h -> p e j h", j=J))
+            else:
+                t = raw_tile([P, n * G, J, N])
+                nc.sync.dma_start(out=t[:], in_=w2[group[0]:group[0] + n].rearrange("e (g p j) n -> p (e g) j n", p=P, j=J))
+            raw[kind, group] = t
+            if i == RAW_BUFS - 2:
+                nc.sync.dma_start(out=pos1_t[:], in_=pos1)
+                nc.sync.dma_start(out=pos2_t[:], in_=pos2)
+        gate_t = raw_tile([P, 2, T])
+        nc.sync.dma_start(out=gate_t[:], in_=gate.rearrange("r p t -> p r t"))
+
+        x_codes = keep.tile([P, T], U32, name="x_codes", align_bytes=64)
+        x_scales = keep.tile([P, T], U8, name="x_scales", align_bytes=64)
+        nc.gpsimd.memset(x_scales[:], 0)
+        x_grouped = []
+        for a, b in X_CHUNKS:
+            t = ring.tile([P, b - a, J], BF16, name="hg", tag="hg", bufs=3, align_bytes=64)
+            nc.vector.tensor_copy(out=t[:].rearrange("p (c i) j -> p c j i", i=4),
+                                  in_=x_raw[:, :, a:b].rearrange("p j (c i) -> p c j i", i=4))
+            x_grouped.append(t)
+        for (a, b), t in zip(X_CHUNKS, x_grouped):
+            nc.vector.quantize_mx(out=x_codes[:, a:b].bitcast(FP8X4), scales=x_scales[:, a:b],
+                                  in_=t[:].rearrange("p n j -> p (n j)"))
+        slot_codes = {}
+        at = 0
+        for i, n in enumerate(GATHERS):
+            codes = keep.tile([P, n], U32, name="g_codes%d" % i, align_bytes=64)
+            scales = keep.tile([P, n], U8, name="g_scales%d" % i, align_bytes=64)
+            part = offs_t[:, at // 16:(at + n) // 16]
+            nc.vector.tensor_copy(out=codes[:], in_=x_codes[:].indirect(part))
+            nc.vector.tensor_copy(out=scales[:], in_=x_scales[:].indirect(part))
+            for q in range(n // C):
+                slot_codes[(at + q * C) // C] = (codes[:, q * C:(q + 1) * C], scales[:, q * C:(q + 1) * C])
+            at += n
+
+        w1_grouped = {}
+        w1_q = {}
+        w2_q = {}
+        h_grouped = {}
+        h_q = {}
+
+        def group_w1(e, raw_e):
+            w1_grouped[e] = [ring.tile([P, 4, 128, J], BF16, name="wg", tag="wg", bufs=5, align_bytes=64) for g in range(G)]
+            for g in (1, 0):
+                dst = w1_grouped[e][g][:].rearrange("p t m j -> p m j t")
+                src = raw_e[:, :, g * 512:(g + 1) * 512].rearrange("p j (m t) -> p m j t", t=4)
+                m = V_SHARE[e][g]
+                if m > 0:
+                    nc.vector.tensor_copy(out=dst[:, 0:m], in_=src[:, 0:m])
+                if m < 128:
+                    nc.scalar.copy(out=dst[:, m:128], in_=src[:, m:128])
+
+        def quant_w1(e, g):
+            codes = ring.tile([P, 512], U32, name="wc", tag="wc", bufs=6, align_bytes=64)[:]
+            scales = ring.tile([P, 512], U8, name="ws", tag="ws", bufs=6, align_bytes=64)[:]
+            nc.vector.quantize_mx(out=codes.bitcast(FP8X4), scales=scales,
+                                  in_=w1_grouped[e][g][:].rearrange("p t m j -> p (t m j)"))
+            w1_q[e, g] = (codes, scales)
+
+        def hidden(e, g):
+            xc, xs = slot_codes[e]
+            group = [b for b in W1_GROUPS if e in b][0]
+            if group not in h_grouped:
+                h_grouped[group] = ring.tile([P, 2, G, C, J], BF16, name="hg", tag="hg", bufs=3, align_bytes=64)
+            codes, scales = w1_q[e, g]
+            acc = psum.tile([P, 4, C], F32, name="acc", tag="acc", bufs=4)
+            for q in range(4):
+                s = slice(q * 128, (q + 1) * 128)
+                nc.tensor.matmul_mx(out=acc[:, q, :], lhsT=codes[:, s].bitcast(FP8X4), lhsT_scale=scales[:, s],
+                                    rhs=xc.bitcast(FP8X4), rhs_scale=xs, start=True, stop=True)
+            nc.scalar.activation(h_grouped[group][:, e - group[0], g, :, :], acc[:].rearrange("p t n -> p n t"), SILU)
+
+        def quant_h(group):
+            n = len(group)
+            codes = keep.tile([P, n, G * C], U32, name="hc%d" % group[0], align_bytes=64)
+            scales = keep.tile([P, n, G * C], U8, name="hs%d" % group[0], align_bytes=64)
+            nc.vector.quantize_mx(out=codes[:].rearrange("p e n -> p (e n)").bitcast(FP8X4),
+                                  scales=scales[:].rearrange("p e n -> p (e n)"),
+                                  in_=h_grouped[group][:, 0:n].rearrange("p e g n j -> p (e g n j)"))
+            for e in group:
+                h_q[e] = (codes[:, e - group[0]], scales[:, e - group[0]])
+
+        def prepare_w2(group):
+            total = len(group) * G
+            t = ring.tile([P, total, N, J], BF16, name="vg", tag="vg", bufs=2, align_bytes=64)
+            dst = t[:].rearrange("p g (c i) j -> p g c j i", i=4)
+            src = raw["w2", group][:].rearrange("p g j (c i) -> p g c j i", i=4)
+            n = W2_SHARE[group]
+            if n > 0:
+                nc.vector.tensor_copy(out=dst[:, 0:n], in_=src[:, 0:n])
+            for g in range(n, total):
+                nc.scalar.copy(out=dst[:, g], in_=src[:, g])
+            codes = ring.tile([P, total, N], U32, name="vc", tag="vc", bufs=2, align_bytes=64)
+            scales = ring.tile([P, total, N], U8, name="vs", tag="vs", bufs=2, align_bytes=64)
+            nc.vector.quantize_mx(out=codes[:].rearrange("p g n -> p (g n)").bitcast(FP8X4),
+                                  scales=scales[:].rearrange("p g n -> p (g n)"),
+                                  in_=t[:].rearrange("p g n j -> p (g n j)"))
+            for i, e in enumerate(group):
+                w2_q[e] = (codes[:, i * G:(i + 1) * G], scales[:, i * G:(i + 1) * G])
+
+        y_bank = {}
+
+        def second(e):
+            wc, ws = w2_q[e]
+            hc, hs = h_q[e]
+            bank = [b for b in Y_BANKS if e in b][0]
+            if e == bank[0]:
+                y_bank[bank] = psum.tile([N, 4, C], F32, name="acc_y", tag="acc_y", bufs=4)
+            acc = y_bank[bank]
+            for g in range(G):
+                s = slice(g * C, (g + 1) * C)
+                nc.tensor.matmul_mx(out=acc[:, e - bank[0], :], lhsT=wc[:, g, :].bitcast(FP8X4), lhsT_scale=ws[:, g, :],
+                                    rhs=hc[:, s].bitcast(FP8X4), rhs_scale=hs[:, s],
+                                    start=(g == 0), stop=(g == G - 1))
+            if e == bank[-1]:
+                n = len(bank)
+                dst = y_all[:, bank[0] * C:(e + 1) * C]
+                src = acc[:, 0:n, :].rearrange("p a n -> p (a n)")
+                if e == E - 1:
+                    nc.vector.tensor_copy(out=dst, in_=src)
+                else:
+                    nc.scalar.copy(out=dst, in_=src)
+
+        for kind, group in ORDER:
+            if kind == "w1":
+                for i, e in enumerate(group):
+                    group_w1(e, raw[kind, group][:, i])
+                for e in group:
+                    for g in range(G):
+                        quant_w1(e, g)
+                        hidden(e, g)
+                quant_h(group)
+            else:
+                prepare_w2(group)
+                for e in group:
+                    second(e)
+
+        at = 0
+        for i, n in enumerate(OUT_CHUNKS):
+            s = slice(at, at + n)
+            part = slice(at // 16, (at + n) // 16)
+            a = ring.tile([P, n], F32, name="hg", tag="hg", bufs=3, align_bytes=64)
+            b = ring.tile([P, n], F32, name="hg", tag="hg", bufs=3, align_bytes=64)
+            nc.vector.tensor_tensor(a[:], y_all[:].indirect(pos1_t[:, part]), gate_t[:, 0, s], MULT)
+            nc.vector.tensor_tensor(b[:], y_all[:].indirect(pos2_t[:, part]), gate_t[:, 1, s], MULT)
+            nc.vector.tensor_tensor(a[:], a[:], b[:], ADD)
+            nc.sync.dma_start(out=out[:, s], in_=a[:])
+            at += n

@@ -8,7 +8,6 @@ FLOPS = 2 * E * C * H * (K + N)
 F32 = mybir.dt.float32
 BF16 = mybir.dt.bfloat16
 U32 = mybir.dt.uint32
-I32 = mybir.dt.int32
 U16 = mybir.dt.uint16
 U8 = mybir.dt.uint8
 FP8X4 = mybir.dt.float8_e4m3fn_x4
@@ -19,16 +18,15 @@ ADD = mybir.AluOpType.add
 P = 128
 J = 4
 G = H // 512
-X_CHUNKS = ((0, 512), (512, 768))
-GATHERS = (512, 512, 512)
-V_SHARE = [(96, 0)] * 3 + [(128, 0)] * 7 + [(96, 16), (128, 32)]
-Y_BANKS = ((0, 1, 2, 3), (4, 5, 6, 7), (8, 9, 10), (11,))
-W2_SHARE = {(0, 1): 3, (2, 3): 4, (4, 5): 3, (6, 7): 2, (8, 9): 4, (10,): 0, (11,): 1}
-W1_GROUPS = ((0, 1), (2, 3), (4, 5), (6, 7), (8, 9), (10,), (11,))
-ORDER = [("w1", (0, 1)), ("w1", (2, 3)), ("w1", (4, 5)), ("w1", (6, 7)), ("w2", (0, 1)), ("w1", (8, 9)), ("w2", (2, 3)), ("w2", (4, 5)),
-         ("w1", (10,)), ("w2", (6, 7)), ("w1", (11,)), ("w2", (8, 9)), ("w2", (10,)), ("w2", (11,))]
+UNIT = 128 * J
+HALF = 4 * UNIT
+X_SPLIT = 512
+GATHER = 512
+W1_VECTOR_COLS = 32
+W2_LOADS = (4, 4, 4, 4, 2, 2, 2, 1, 1)
+Y_BANKS = ((0, 1, 2, 3), (4, 6, 8, 10), (5, 7, 9), (11,))
 OUT_CHUNKS = (512, 256)
-RAW_BUFS = 4
+RAW_BUFS = 8
 
 
 def tile_routed_moe_kernel(tc, xT, w1, w2, gate, offs, pos1, pos2, out):
@@ -50,159 +48,188 @@ def tile_routed_moe_kernel(tc, xT, w1, w2, gate, offs, pos1, pos2, out):
         def raw_tile(shape):
             return ring.tile(shape, F32, name="raw", tag="raw", bufs=RAW_BUFS, align_bytes=64)
 
+        def grouped_tile(shape):
+            return ring.tile(shape, BF16, name="grouped", tag="grouped", bufs=3, align_bytes=64)
+
         x_raw = raw_tile([P, J, T])
         nc.sync.dma_start(out=x_raw[:], in_=xT.rearrange("(p j) n -> p j n", j=J))
         nc.sync.dma_start(out=offs_t[:], in_=offs)
-        raw = {}
-        for i, (kind, group) in enumerate(ORDER):
-            n = len(group)
-            if kind == "w1":
-                t = raw_tile([P, n, J, H])
-                nc.sync.dma_start(out=t[:], in_=w1[group[0]:group[0] + n].rearrange("e (p j) h -> p e j h", j=J))
-            else:
-                t = raw_tile([P, n * G, J, N])
-                nc.sync.dma_start(out=t[:], in_=w2[group[0]:group[0] + n].rearrange("e (g p j) n -> p (e g) j n", p=P, j=J))
-            raw[kind, group] = t
-            if i == RAW_BUFS - 2:
+        w1_raw = []
+        for e in range(E):
+            t = raw_tile([P, J, H])
+            nc.sync.dma_start(out=t[:], in_=w1[e].rearrange("(p j) h -> p j h", j=J))
+            w1_raw.append(t)
+            if e == RAW_BUFS - 2:
                 nc.sync.dma_start(out=pos1_t[:], in_=pos1)
                 nc.sync.dma_start(out=pos2_t[:], in_=pos2)
+        w2_blocks = w2.rearrange("e (g p j) n -> p (e g) j n", p=P, j=J)
+        w2_raw = []
+        load_start = []
+        for n in W2_LOADS:
+            t = raw_tile([P, n, J, N])
+            nc.sync.dma_start(out=t[:], in_=w2_blocks[:, len(w2_raw):len(w2_raw) + n])
+            load_start.append(len(w2_raw))
+            w2_raw.extend([t[:, i] for i in range(n)])
         gate_t = raw_tile([P, 2, T])
         nc.sync.dma_start(out=gate_t[:], in_=gate.rearrange("r p t -> p r t"))
 
         x_codes = keep.tile([P, T], U32, name="x_codes", align_bytes=64)
         x_scales = keep.tile([P, T], U8, name="x_scales", align_bytes=64)
         nc.gpsimd.memset(x_scales[:], 0)
-        x_grouped = []
-        for a, b in X_CHUNKS:
-            t = ring.tile([P, b - a, J], BF16, name="hg", tag="hg", bufs=3, align_bytes=64)
-            nc.vector.tensor_copy(out=t[:].rearrange("p (c i) j -> p c j i", i=4),
-                                  in_=x_raw[:, :, a:b].rearrange("p j (c i) -> p c j i", i=4))
-            x_grouped.append(t)
-        for (a, b), t in zip(X_CHUNKS, x_grouped):
+        x_parts = []
+        for a, b, copy in ((0, X_SPLIT, nc.vector.tensor_copy), (X_SPLIT, T, nc.scalar.copy)):
+            t = grouped_tile([P, b - a, J])
+            copy(out=t[:].rearrange("p (c i) j -> p c j i", i=4), in_=x_raw[:, :, a:b].rearrange("p j (c i) -> p c j i", i=4))
+            x_parts.append((a, b, t))
+        for a, b, t in x_parts:
             nc.vector.quantize_mx(out=x_codes[:, a:b].bitcast(FP8X4), scales=x_scales[:, a:b],
                                   in_=t[:].rearrange("p n j -> p (n j)"))
         slot_codes = {}
-        at = 0
-        for i, n in enumerate(GATHERS):
-            codes = keep.tile([P, n], U32, name="g_codes%d" % i, align_bytes=64)
-            scales = keep.tile([P, n], U8, name="g_scales%d" % i, align_bytes=64)
-            part = offs_t[:, at // 16:(at + n) // 16]
+        for at in range(0, E * C, GATHER):
+            codes = keep.tile([P, GATHER], U32, name="g_codes%d" % at, align_bytes=64)
+            scales = keep.tile([P, GATHER], U8, name="g_scales%d" % at, align_bytes=64)
+            part = offs_t[:, at // 16:(at + GATHER) // 16]
             nc.vector.tensor_copy(out=codes[:], in_=x_codes[:].indirect(part))
             nc.vector.tensor_copy(out=scales[:], in_=x_scales[:].indirect(part))
-            for q in range(n // C):
-                slot_codes[(at + q * C) // C] = (codes[:, q * C:(q + 1) * C], scales[:, q * C:(q + 1) * C])
-            at += n
+            for q in range(GATHER // C):
+                slot_codes[at // C + q] = (codes[:, q * C:(q + 1) * C], scales[:, q * C:(q + 1) * C])
 
-        w1_grouped = {}
-        w1_q = {}
-        w2_q = {}
-        h_grouped = {}
+        def quantise(values, codes, scales):
+            n = values.shape[1]
+            at = 0
+            while at < n:
+                width = 4096
+                while width > n - at:
+                    width //= 2
+                words = slice(at // J, (at + width) // J)
+                nc.vector.quantize_mx(out=codes[:, words].bitcast(FP8X4), scales=scales[:, words], in_=values[:, at:at + width])
+                at += width
+
+        last_pair = (E - 2, E - 1)
+        hidden_of = [[(e, g) for e, g in ((k - 1, 0), (k - 2, 1)) if e >= 0 and e not in last_pair] for k in range(E + 1)]
+        weights_of = [[(e, g) for e, g in ((k - 1, 1), (k, 0)) if 0 <= e < E] for k in range(E + 1)]
+        batch = {}
+        late = keep.tile([P, 2 * HALF], BF16, name="late", align_bytes=64)
+
+        def batch_tile(k):
+            if k not in batch:
+                batch[k] = grouped_tile([P, len(hidden_of[k]) * UNIT + len(weights_of[k]) * HALF])
+            return batch[k]
+
+        def weights_view(e, g):
+            k = e + g
+            at = len(hidden_of[k]) * UNIT + weights_of[k].index((e, g)) * HALF
+            dst = batch_tile(k)[:, at:at + HALF].rearrange("p (t m j) -> p m j t", t=4, j=J)
+            src = w1_raw[e][:, :, g * 512:(g + 1) * 512].rearrange("p j (m t) -> p m j t", t=4)
+            return dst, src
+
+        def hidden_view(e, g):
+            if e in last_pair:
+                at = HALF + ((e - last_pair[0]) * G + g) * UNIT
+                host = late
+            else:
+                at = hidden_of[e + 1 + g].index((e, g)) * UNIT
+                host = batch_tile(e + 1 + g)
+            return host[:, at:at + UNIT].rearrange("p (n j) -> p n j", j=J)
+
+        code_words = (E // 2 - 1) * G * C + 2 * 512
+        w1_codes = [keep.tile([P, code_words], U32, name="w1_codes%d" % i, align_bytes=64) for i in range(2)]
+        w1_scales = [keep.tile([P, code_words], U8, name="w1_scales%d" % i, align_bytes=64) for i in range(2)]
+        kept = [0, 0]
         h_q = {}
+        for k in range(E + 1):
+            if k == 0:
+                for g in range(G):
+                    dst, src = weights_view(0, g)
+                    nc.scalar.copy(out=dst, in_=src)
+            elif k < E:
+                m = W1_VECTOR_COLS
+                dst, src = weights_view(k, 0)
+                nc.vector.tensor_copy(out=dst, in_=src)
+                dst, src = weights_view(k, 1)
+                nc.vector.tensor_copy(out=dst[:, 0:m], in_=src[:, 0:m])
+                nc.scalar.copy(out=dst[:, m:128], in_=src[:, m:128])
+            t = batch_tile(k)
+            words = slice(kept[k % 2], kept[k % 2] + t.shape[1] // J)
+            codes, scales = w1_codes[k % 2][:, words], w1_scales[k % 2][:, words]
+            quantise(t[:], codes, scales)
+            for i, key in enumerate(hidden_of[k]):
+                h_q[key] = (codes[:, i * C:(i + 1) * C], scales[:, i * C:(i + 1) * C])
+            kept[k % 2] += len(hidden_of[k]) * C
+            for i, (e, g) in enumerate(weights_of[k]):
+                xc, xs = slot_codes[e]
+                acc = psum.tile([P, 4, C], F32, name="acc", tag="acc", bufs=4)
+                for q in range(4):
+                    at = len(hidden_of[k]) * C + (4 * i + q) * 128
+                    s = slice(at, at + 128)
+                    nc.tensor.matmul_mx(out=acc[:, q, :], lhsT=codes[:, s].bitcast(FP8X4), lhsT_scale=scales[:, s],
+                                        rhs=xc.bitcast(FP8X4), rhs_scale=xs, start=True, stop=True)
+                nc.scalar.activation(hidden_view(e, g), acc[:].rearrange("p t n -> p n t"), SILU)
 
-        def group_w1(e, raw_e):
-            w1_grouped[e] = [ring.tile([P, 4, 128, J], BF16, name="wg", tag="wg", bufs=5, align_bytes=64) for g in range(G)]
-            for g in (1, 0):
-                dst = w1_grouped[e][g][:].rearrange("p t m j -> p m j t")
-                src = raw_e[:, :, g * 512:(g + 1) * 512].rearrange("p j (m t) -> p m j t", t=4)
-                m = V_SHARE[e][g]
-                if m > 0:
-                    nc.vector.tensor_copy(out=dst[:, 0:m], in_=src[:, 0:m])
-                if m < 128:
-                    nc.scalar.copy(out=dst[:, m:128], in_=src[:, m:128])
+        ends = [b + 1 for b in load_start]
+        batches = [range(a, b) for a, b in zip([0] + ends[:-1], ends)]
+        late_batch = 3
+        w2_tile = {late_batch: late}
 
-        def quant_w1(e, g):
-            codes = ring.tile([P, 512], U32, name="wc", tag="wc", bufs=6, align_bytes=64)[:]
-            scales = ring.tile([P, 512], U8, name="ws", tag="ws", bufs=6, align_bytes=64)[:]
-            nc.vector.quantize_mx(out=codes.bitcast(FP8X4), scales=scales,
-                                  in_=w1_grouped[e][g][:].rearrange("p t m j -> p (t m j)"))
-            w1_q[e, g] = (codes, scales)
-
-        def hidden(e, g):
-            xc, xs = slot_codes[e]
-            group = [b for b in W1_GROUPS if e in b][0]
-            if group not in h_grouped:
-                h_grouped[group] = ring.tile([P, 2, G, C, J], BF16, name="hg", tag="hg", bufs=3, align_bytes=64)
-            codes, scales = w1_q[e, g]
-            acc = psum.tile([P, 4, C], F32, name="acc", tag="acc", bufs=4)
-            for q in range(4):
-                s = slice(q * 128, (q + 1) * 128)
-                nc.tensor.matmul_mx(out=acc[:, q, :], lhsT=codes[:, s].bitcast(FP8X4), lhsT_scale=scales[:, s],
-                                    rhs=xc.bitcast(FP8X4), rhs_scale=xs, start=True, stop=True)
-            nc.scalar.activation(h_grouped[group][:, e - group[0], g, :, :], acc[:].rearrange("p t n -> p n t"), SILU)
-
-        def quant_h(group):
-            n = len(group)
-            codes = keep.tile([P, n, G * C], U32, name="hc%d" % group[0], align_bytes=64)
-            scales = keep.tile([P, n, G * C], U8, name="hs%d" % group[0], align_bytes=64)
-            nc.vector.quantize_mx(out=codes[:].rearrange("p e n -> p (e n)").bitcast(FP8X4),
-                                  scales=scales[:].rearrange("p e n -> p (e n)"),
-                                  in_=h_grouped[group][:, 0:n].rearrange("p e g n j -> p (e g n j)"))
-            for e in group:
-                h_q[e] = (codes[:, e - group[0]], scales[:, e - group[0]])
-
-        def prepare_w2(group):
-            total = len(group) * G
-            t = ring.tile([P, total, N, J], BF16, name="vg", tag="vg", bufs=2, align_bytes=64)
-            dst = t[:].rearrange("p g (c i) j -> p g c j i", i=4)
-            src = raw["w2", group][:].rearrange("p g j (c i) -> p g c j i", i=4)
-            n = W2_SHARE[group]
-            if n > 0:
-                nc.vector.tensor_copy(out=dst[:, 0:n], in_=src[:, 0:n])
-            for g in range(n, total):
-                nc.scalar.copy(out=dst[:, g], in_=src[:, g])
-            codes = ring.tile([P, total, N], U32, name="vc", tag="vc", bufs=2, align_bytes=64)
-            scales = ring.tile([P, total, N], U8, name="vs", tag="vs", bufs=2, align_bytes=64)
-            nc.vector.quantize_mx(out=codes[:].rearrange("p g n -> p (g n)").bitcast(FP8X4),
-                                  scales=scales[:].rearrange("p g n -> p (g n)"),
-                                  in_=t[:].rearrange("p g n j -> p (g n j)"))
-            for i, e in enumerate(group):
-                w2_q[e] = (codes[:, i * G:(i + 1) * G], scales[:, i * G:(i + 1) * G])
+        def group_w2(block, copy):
+            b = [i for i, blocks in enumerate(batches) if block in blocks][0]
+            if b not in w2_tile:
+                w2_tile[b] = grouped_tile([P, len(batches[b]) * UNIT])
+            at = (block - batches[b].start) * UNIT
+            copy(out=w2_tile[b][:, at:at + UNIT].rearrange("p (c i j) -> p c j i", i=4, j=J),
+                 in_=w2_raw[block].rearrange("p j (c i) -> p c j i", i=4))
 
         y_bank = {}
-
-        def second(e):
-            wc, ws = w2_q[e]
-            hc, hs = h_q[e]
-            bank = [b for b in Y_BANKS if e in b][0]
-            if e == bank[0]:
-                y_bank[bank] = psum.tile([N, 4, C], F32, name="acc_y", tag="acc_y", bufs=4)
-            acc = y_bank[bank]
-            for g in range(G):
-                s = slice(g * C, (g + 1) * C)
-                nc.tensor.matmul_mx(out=acc[:, e - bank[0], :], lhsT=wc[:, g, :].bitcast(FP8X4), lhsT_scale=ws[:, g, :],
-                                    rhs=hc[:, s].bitcast(FP8X4), rhs_scale=hs[:, s],
-                                    start=(g == 0), stop=(g == G - 1))
-            if e == bank[-1]:
-                n = len(bank)
-                dst = y_all[:, bank[0] * C:(e + 1) * C]
-                src = acc[:, 0:n, :].rearrange("p a n -> p (a n)")
-                if e == E - 1:
-                    nc.vector.tensor_copy(out=dst, in_=src)
-                else:
-                    nc.scalar.copy(out=dst, in_=src)
-
-        for kind, group in ORDER:
-            if kind == "w1":
-                for i, e in enumerate(group):
-                    group_w1(e, raw[kind, group][:, i])
-                for e in group:
-                    for g in range(G):
-                        quant_w1(e, g)
-                        hidden(e, g)
-                quant_h(group)
+        for b, n in enumerate(W2_LOADS):
+            on_vector = 0 if b == len(W2_LOADS) - 2 else (n + 1) // 2
+            for i in range(n):
+                group_w2(load_start[b] + i, nc.vector.tensor_copy if i < on_vector else nc.scalar.copy)
+            t = w2_tile[b]
+            words = t.shape[1] // J
+            if b == late_batch:
+                codes = keep.tile([P, words], U32, name="late_codes", align_bytes=64)
+                scales = keep.tile([P, words], U8, name="late_scales", align_bytes=64)
+                for i in range(2 * G):
+                    s = slice(512 + i * C, 512 + (i + 1) * C)
+                    h_q[last_pair[0] + i // G, i % G] = (codes[:, s], scales[:, s])
             else:
-                prepare_w2(group)
-                for e in group:
-                    second(e)
+                codes = ring.tile([P, words], U32, name="codes", tag="codes", bufs=3, align_bytes=64)
+                scales = ring.tile([P, words], U8, name="scales", tag="scales", bufs=3, align_bytes=64)
+            quantise(t[:], codes[:], scales[:])
+            for i, block in enumerate(batches[b]):
+                e, g = divmod(block, G)
+                bank = [bk for bk in Y_BANKS if e in bk][0]
+                if bank not in y_bank:
+                    y_bank[bank] = psum.tile([N, len(bank), C], F32, name="acc_y", tag="acc_y", bufs=4)
+                acc = y_bank[bank]
+                hc, hs = h_q[e, g]
+                w = slice(i * N, (i + 1) * N)
+                nc.tensor.matmul_mx(out=acc[:, bank.index(e), :], lhsT=codes[:, w].bitcast(FP8X4), lhsT_scale=scales[:, w],
+                                    rhs=hc.bitcast(FP8X4), rhs_scale=hs, start=(g == 0), stop=(g == G - 1))
+                if e == bank[-1] and g == G - 1:
+                    step = bank[1] - bank[0] if len(bank) > 1 else 1
+                    dst = y_all[:].rearrange("p (e n) -> p e n", n=C)[:, bank[0]:e + 1:step]
+                    copy = nc.vector.tensor_copy if e == E - 1 else nc.scalar.copy
+                    copy(out=dst, in_=acc[:])
 
+        parts = []
         at = 0
-        for i, n in enumerate(OUT_CHUNKS):
-            s = slice(at, at + n)
-            part = slice(at // 16, (at + n) // 16)
-            a = ring.tile([P, n], F32, name="hg", tag="hg", bufs=3, align_bytes=64)
-            b = ring.tile([P, n], F32, name="hg", tag="hg", bufs=3, align_bytes=64)
-            nc.vector.tensor_tensor(a[:], y_all[:].indirect(pos1_t[:, part]), gate_t[:, 0, s], MULT)
-            nc.vector.tensor_tensor(b[:], y_all[:].indirect(pos2_t[:, part]), gate_t[:, 1, s], MULT)
+        for n in OUT_CHUNKS:
+            parts.append((slice(at, at + n), slice(at // 16, (at + n) // 16), raw_tile([P, n]), raw_tile([P, n])))
+            at += n
+
+        def fetch(i, r):
+            s, part, a, b = parts[i]
+            nc.vector.tensor_tensor((a, b)[r][:], y_all[:].indirect((pos1_t, pos2_t)[r][:, part]), gate_t[:, r, s], MULT)
+
+        def finish(i):
+            s, part, a, b = parts[i]
             nc.vector.tensor_tensor(a[:], a[:], b[:], ADD)
             nc.sync.dma_start(out=out[:, s], in_=a[:])
-            at += n
+
+        fetch(0, 0)
+        fetch(0, 1)
+        fetch(1, 0)
+        finish(0)
+        fetch(1, 1)
+        finish(1)

@@ -79,7 +79,7 @@ def tile_routed_moe_kernel(tc, xT, w1, w2, gate, offs, pos1, pos2, out):
         x_parts = []
         for a, b, copy in ((0, X_SPLIT, nc.vector.tensor_copy), (X_SPLIT, T, nc.scalar.copy)):
             t = grouped_tile([P, b - a, J])
-            copy(out=t[:].rearrange("p (c i) j -> p c j i", i=4), in_=x_raw[:, :, a:b].rearrange("p j (c i) -> p c j i", i=4))
+            copy(out=t[:].rearrange("p (c i) j -> p c j i", i=2), in_=x_raw[:, :, a:b].rearrange("p j (c i) -> p c j i", i=2))
             x_parts.append((a, b, t))
         for a, b, t in x_parts:
             nc.vector.quantize_mx(out=x_codes[:, a:b].bitcast(FP8X4), scales=x_scales[:, a:b],
@@ -119,8 +119,8 @@ def tile_routed_moe_kernel(tc, xT, w1, w2, gate, offs, pos1, pos2, out):
         def weights_view(e, g):
             k = e + g
             at = len(hidden_of[k]) * UNIT + weights_of[k].index((e, g)) * HALF
-            dst = batch_tile(k)[:, at:at + HALF].rearrange("p (t m j) -> p m j t", t=4, j=J)
-            src = w1_raw[e][:, :, g * 512:(g + 1) * 512].rearrange("p j (m t) -> p m j t", t=4)
+            dst = batch_tile(k)[:, at:at + HALF].rearrange("p (t m u j) -> p m u t j", t=4, u=2, j=2)
+            src = w1_raw[e][:, :, g * 512:(g + 1) * 512].rearrange("p (u j) (m t) -> p m u t j", t=4, j=2)
             return dst, src
 
         def hidden_view(e, g):
@@ -176,8 +176,8 @@ def tile_routed_moe_kernel(tc, xT, w1, w2, gate, offs, pos1, pos2, out):
             if b not in w2_tile:
                 w2_tile[b] = grouped_tile([P, len(batches[b]) * UNIT])
             at = (block - batches[b].start) * UNIT
-            copy(out=w2_tile[b][:, at:at + UNIT].rearrange("p (c i j) -> p c j i", i=4, j=J),
-                 in_=w2_raw[block].rearrange("p j (c i) -> p c j i", i=4))
+            copy(out=w2_tile[b][:, at:at + UNIT].rearrange("p (c i j) -> p c j i", i=2, j=J),
+                 in_=w2_raw[block].rearrange("p j (c i) -> p c j i", i=2))
 
         y_bank = {}
         for b, n in enumerate(W2_LOADS):

@@ -24,9 +24,10 @@ X_SPLIT = 512
 GATHER = 512
 W1_VECTOR_COLS = 32
 W2_LOADS = (4, 4, 4, 4, 2, 2, 2, 1, 1)
-Y_BANKS = ((0, 1, 2, 3), (4, 6, 8, 10), (5, 7, 9), (11,))
-OUT_CHUNKS = (512, 256)
-RAW_BUFS = 8
+Y_BANKS = ((0, 1, 2), (3, 4, 5), (6, 8, 10), (7, 9, 11))
+OUT_CHUNK = 384
+W1_LOADS = (1, 2, 2, 2, 1, 1, 1, 1, 1)
+RAW_BYTES = 4 * J * (T + 7 * H)
 
 
 def tile_routed_moe_kernel(tc, xT, w1, w2, gate, offs, pos1, pos2, out):
@@ -34,6 +35,7 @@ def tile_routed_moe_kernel(tc, xT, w1, w2, gate, offs, pos1, pos2, out):
     with ExitStack() as ctx:
         keep = ctx.enter_context(tc.tile_pool(name="keep", bufs=1))
         ring = ctx.enter_context(tc.tile_pool(name="ring", bufs=2))
+        landing = ctx.enter_context(tc.tile_pool(name="landing", bufs=1))
         psum = ctx.enter_context(tc.psum_pool(name="psum", bufs=2))
 
         offs_t = keep.tile([P, E * C // 16], U16, name="offs_t")
@@ -45,8 +47,15 @@ def tile_routed_moe_kernel(tc, xT, w1, w2, gate, offs, pos1, pos2, out):
         nc.vector.memset(warm[:], 0.0)
         nc.scalar.activation(warm[:, 1:2], warm[:, 0:1], SILU)
 
+        placed = [0]
+
         def raw_tile(shape):
-            return ring.tile(shape, F32, name="raw", tag="raw", bufs=RAW_BUFS, align_bytes=64)
+            size = 4
+            for d in shape[1:]:
+                size *= d
+            at = placed[-1] if placed[-1] + size <= RAW_BYTES else 0
+            placed.append(at + size)
+            return landing.tile(shape, F32, name="raw%d" % len(placed), offset=at)
 
         def grouped_tile(shape):
             return ring.tile(shape, BF16, name="grouped", tag="grouped", bufs=3, align_bytes=64)
@@ -55,11 +64,11 @@ def tile_routed_moe_kernel(tc, xT, w1, w2, gate, offs, pos1, pos2, out):
         nc.sync.dma_start(out=x_raw[:], in_=xT.rearrange("(p j) n -> p j n", j=J))
         nc.sync.dma_start(out=offs_t[:], in_=offs)
         w1_raw = []
-        for e in range(E):
-            t = raw_tile([P, J, H])
-            nc.sync.dma_start(out=t[:], in_=w1[e].rearrange("(p j) h -> p j h", j=J))
-            w1_raw.append(t)
-            if e == RAW_BUFS - 2:
+        for n in W1_LOADS:
+            t = raw_tile([P, n, J, H])
+            nc.sync.dma_start(out=t[:], in_=w1[len(w1_raw):len(w1_raw) + n].rearrange("e (p j) h -> p e j h", j=J))
+            w1_raw.extend([t[:, i] for i in range(n)])
+            if len(w1_raw) == 7:
                 nc.sync.dma_start(out=pos1_t[:], in_=pos1)
                 nc.sync.dma_start(out=pos2_t[:], in_=pos2)
         w2_blocks = w2.rearrange("e (g p j) n -> p (e g) j n", p=P, j=J)
@@ -166,9 +175,9 @@ def tile_routed_moe_kernel(tc, xT, w1, w2, gate, offs, pos1, pos2, out):
                                         rhs=xc.bitcast(FP8X4), rhs_scale=xs, start=True, stop=True)
                 nc.scalar.activation(hidden_view(e, g), acc[:].rearrange("p t n -> p n t"), SILU)
 
-        ends = [b + 1 for b in load_start]
+        ends = [b + 1 for b in load_start[:-2]] + [load_start[-2], E * G]
         batches = [range(a, b) for a, b in zip([0] + ends[:-1], ends)]
-        late_batch = 3
+        late_batch = 1
         w2_tile = {late_batch: late}
 
         def group_w2(block, copy):
@@ -180,10 +189,14 @@ def tile_routed_moe_kernel(tc, xT, w1, w2, gate, offs, pos1, pos2, out):
                  in_=w2_raw[block].rearrange("p j (c i) -> p c j i", i=2))
 
         y_bank = {}
-        for b, n in enumerate(W2_LOADS):
-            on_vector = 0 if b == len(W2_LOADS) - 2 else (n + 1) // 2
-            for i in range(n):
-                group_w2(load_start[b] + i, nc.vector.tensor_copy if i < on_vector else nc.scalar.copy)
+        for b in range(len(batches)):
+            if b < len(W2_LOADS) - 2:
+                n = W2_LOADS[b]
+                for i in range(n):
+                    group_w2(load_start[b] + i, nc.vector.tensor_copy if i < n // 2 else nc.scalar.copy)
+            elif b == len(batches) - 1:
+                group_w2(E * G - 2, nc.scalar.copy)
+                group_w2(E * G - 1, nc.vector.tensor_copy)
             t = w2_tile[b]
             words = t.shape[1] // J
             if b == late_batch:
@@ -207,29 +220,18 @@ def tile_routed_moe_kernel(tc, xT, w1, w2, gate, offs, pos1, pos2, out):
                 nc.tensor.matmul_mx(out=acc[:, bank.index(e), :], lhsT=codes[:, w].bitcast(FP8X4), lhsT_scale=scales[:, w],
                                     rhs=hc.bitcast(FP8X4), rhs_scale=hs, start=(g == 0), stop=(g == G - 1))
                 if e == bank[-1] and g == G - 1:
-                    step = bank[1] - bank[0] if len(bank) > 1 else 1
+                    step = bank[1] - bank[0]
                     dst = y_all[:].rearrange("p (e n) -> p e n", n=C)[:, bank[0]:e + 1:step]
-                    copy = nc.vector.tensor_copy if e == E - 1 else nc.scalar.copy
-                    copy(out=dst, in_=acc[:])
+                    nc.scalar.copy(out=dst, in_=acc[:])
 
+        first = raw_tile([P, T])
+        nc.vector.tensor_tensor(first[:], y_all[:].indirect(pos1_t[:]), gate_t[:, 0, :], MULT)
         parts = []
-        at = 0
-        for n in OUT_CHUNKS:
-            parts.append((slice(at, at + n), slice(at // 16, (at + n) // 16), raw_tile([P, n]), raw_tile([P, n])))
-            at += n
-
-        def fetch(i, r):
-            s, part, a, b = parts[i]
-            nc.vector.tensor_tensor((a, b)[r][:], y_all[:].indirect((pos1_t, pos2_t)[r][:, part]), gate_t[:, r, s], MULT)
-
-        def finish(i):
-            s, part, a, b = parts[i]
-            nc.vector.tensor_tensor(a[:], a[:], b[:], ADD)
-            nc.sync.dma_start(out=out[:, s], in_=a[:])
-
-        fetch(0, 0)
-        fetch(0, 1)
-        fetch(1, 0)
-        finish(0)
-        fetch(1, 1)
-        finish(1)
+        for at in range(0, T, OUT_CHUNK):
+            s = slice(at, at + OUT_CHUNK)
+            second = raw_tile([P, OUT_CHUNK])
+            nc.vector.tensor_tensor(second[:], y_all[:].indirect(pos2_t[:, at // 16:(at + OUT_CHUNK) // 16]), gate_t[:, 1, s], MULT)
+            parts.append((s, second))
+        for s, second in parts:
+            nc.vector.tensor_tensor(second[:], second[:], first[:, s], ADD)
+            nc.sync.dma_start(out=out[:, s], in_=second[:])

@@ -23,10 +23,11 @@ HALF = 4 * UNIT
 X_SPLIT = 512
 GATHER = 512
 W1_VECTOR_COLS = 32
-W2_LOADS = (4, 4, 4, 4, 2, 2, 2, 1, 1)
-Y_BANKS = ((0, 1, 2), (3, 4, 5), (6, 8, 10), (7, 9, 11))
+W2_LOADS = (2, 2, 4, 4, 4, 2, 2, 2, 1, 1)
+BANKS = 3
+W2_ORDER = [(e, g) for e in range(E - BANKS) for g in range(G)] + [(e, g) for g in range(G) for e in range(E - BANKS, E)]
 OUT_CHUNK = 384
-W1_LOADS = (1, 2, 2, 2, 1, 1, 1, 1, 1)
+W1_LOADS = (1,) * E
 RAW_BYTES = 4 * J * (T + 7 * H)
 
 
@@ -58,7 +59,7 @@ def tile_routed_moe_kernel(tc, xT, w1, w2, gate, offs, pos1, pos2, out):
             return landing.tile(shape, F32, name="raw%d" % len(placed), offset=at)
 
         def grouped_tile(shape):
-            return ring.tile(shape, BF16, name="grouped", tag="grouped", bufs=3, align_bytes=64)
+            return ring.tile(shape, BF16, name="grouped", tag="grouped", bufs=4, align_bytes=64)
 
         x_raw = raw_tile([P, J, T])
         nc.sync.dma_start(out=x_raw[:], in_=xT.rearrange("(p j) n -> p j n", j=J))
@@ -68,17 +69,19 @@ def tile_routed_moe_kernel(tc, xT, w1, w2, gate, offs, pos1, pos2, out):
             t = raw_tile([P, n, J, H])
             nc.sync.dma_start(out=t[:], in_=w1[len(w1_raw):len(w1_raw) + n].rearrange("e (p j) h -> p e j h", j=J))
             w1_raw.extend([t[:, i] for i in range(n)])
-            if len(w1_raw) == 7:
-                nc.sync.dma_start(out=pos1_t[:], in_=pos1)
-                nc.sync.dma_start(out=pos2_t[:], in_=pos2)
         w2_blocks = w2.rearrange("e (g p j) n -> p (e g) j n", p=P, j=J)
         w2_raw = []
         load_start = []
         for n in W2_LOADS:
             t = raw_tile([P, n, J, N])
-            nc.sync.dma_start(out=t[:], in_=w2_blocks[:, len(w2_raw):len(w2_raw) + n])
+            blocks = [e * G + g for e, g in W2_ORDER[len(w2_raw):len(w2_raw) + n]]
+            rising = sorted(blocks)
+            step = rising[1] - rising[0] if n > 1 else 1
+            nc.sync.dma_start(out=t[:], in_=w2_blocks[:, rising[0]:rising[-1] + 1:step])
             load_start.append(len(w2_raw))
-            w2_raw.extend([t[:, i] for i in range(n)])
+            w2_raw.extend([t[:, rising.index(block)] for block in blocks])
+        nc.sync.dma_start(out=pos1_t[:], in_=pos1)
+        nc.sync.dma_start(out=pos2_t[:], in_=pos2)
         gate_t = raw_tile([P, 2, T])
         nc.sync.dma_start(out=gate_t[:], in_=gate.rearrange("r p t -> p r t"))
 
@@ -115,7 +118,7 @@ def tile_routed_moe_kernel(tc, xT, w1, w2, gate, offs, pos1, pos2, out):
                 at += width
 
         last_pair = (E - 2, E - 1)
-        hidden_of = [[(e, g) for e, g in ((k - 1, 0), (k - 2, 1)) if e >= 0 and e not in last_pair] for k in range(E + 1)]
+        hidden_of = [[(e, g) for e, g in ((k - 2, 0), (k - 3, 1)) if e >= 0 and e not in last_pair] for k in range(E + 1)]
         weights_of = [[(e, g) for e, g in ((k - 1, 1), (k, 0)) if 0 <= e < E] for k in range(E + 1)]
         batch = {}
         late = keep.tile([P, 2 * HALF], BF16, name="late", align_bytes=64)
@@ -137,8 +140,8 @@ def tile_routed_moe_kernel(tc, xT, w1, w2, gate, offs, pos1, pos2, out):
                 at = HALF + ((e - last_pair[0]) * G + g) * UNIT
                 host = late
             else:
-                at = hidden_of[e + 1 + g].index((e, g)) * UNIT
-                host = batch_tile(e + 1 + g)
+                at = hidden_of[e + 2 + g].index((e, g)) * UNIT
+                host = batch_tile(e + 2 + g)
             return host[:, at:at + UNIT].rearrange("p (n j) -> p n j", j=J)
 
         code_words = (E // 2 - 1) * G * C + 2 * 512
@@ -175,9 +178,9 @@ def tile_routed_moe_kernel(tc, xT, w1, w2, gate, offs, pos1, pos2, out):
                                         rhs=xc.bitcast(FP8X4), rhs_scale=xs, start=True, stop=True)
                 nc.scalar.activation(hidden_view(e, g), acc[:].rearrange("p t n -> p n t"), SILU)
 
-        ends = [b + 1 for b in load_start[:-2]] + [load_start[-2], E * G]
+        ends = [1] + [b + 1 for b in load_start[2:-2]] + [load_start[-2], E * G]
         batches = [range(a, b) for a, b in zip([0] + ends[:-1], ends)]
-        late_batch = 1
+        late_batch = 2
         w2_tile = {late_batch: late}
 
         def group_w2(block, copy):
@@ -189,14 +192,14 @@ def tile_routed_moe_kernel(tc, xT, w1, w2, gate, offs, pos1, pos2, out):
                  in_=w2_raw[block].rearrange("p j (c i) -> p c j i", i=2))
 
         y_bank = {}
+        grouped = 0
         for b in range(len(batches)):
-            if b < len(W2_LOADS) - 2:
-                n = W2_LOADS[b]
-                for i in range(n):
-                    group_w2(load_start[b] + i, nc.vector.tensor_copy if i < n // 2 else nc.scalar.copy)
-            elif b == len(batches) - 1:
-                group_w2(E * G - 2, nc.scalar.copy)
-                group_w2(E * G - 1, nc.vector.tensor_copy)
+            for at, n in zip(load_start, W2_LOADS):
+                if grouped <= at < max(batches[b].stop, 4):
+                    on_vector = 0 if at in (0, load_start[-2]) else n if at == load_start[1] else (n + 1) // 2
+                    for i in range(n):
+                        group_w2(at + i, nc.vector.tensor_copy if i < on_vector else nc.scalar.copy)
+                    grouped = at + n
             t = w2_tile[b]
             words = t.shape[1] // J
             if b == late_batch:
@@ -210,19 +213,19 @@ def tile_routed_moe_kernel(tc, xT, w1, w2, gate, offs, pos1, pos2, out):
                 scales = ring.tile([P, words], U8, name="scales", tag="scales", bufs=3, align_bytes=64)
             quantise(t[:], codes[:], scales[:])
             for i, block in enumerate(batches[b]):
-                e, g = divmod(block, G)
-                bank = [bk for bk in Y_BANKS if e in bk][0]
+                e, g = W2_ORDER[block]
+                bank, place = e % BANKS, e // BANKS
                 if bank not in y_bank:
-                    y_bank[bank] = psum.tile([N, len(bank), C], F32, name="acc_y", tag="acc_y", bufs=4)
+                    y_bank[bank] = psum.tile([N, E // BANKS, C], F32, name="acc_y", tag="acc_y", bufs=BANKS)
                 acc = y_bank[bank]
                 hc, hs = h_q[e, g]
                 w = slice(i * N, (i + 1) * N)
-                nc.tensor.matmul_mx(out=acc[:, bank.index(e), :], lhsT=codes[:, w].bitcast(FP8X4), lhsT_scale=scales[:, w],
+                nc.tensor.matmul_mx(out=acc[:, place, :], lhsT=codes[:, w].bitcast(FP8X4), lhsT_scale=scales[:, w],
                                     rhs=hc.bitcast(FP8X4), rhs_scale=hs, start=(g == 0), stop=(g == G - 1))
-                if e == bank[-1] and g == G - 1:
-                    step = bank[1] - bank[0]
-                    dst = y_all[:].rearrange("p (e n) -> p e n", n=C)[:, bank[0]:e + 1:step]
-                    nc.scalar.copy(out=dst, in_=acc[:])
+                if e >= E - BANKS and g == G - 1:
+                    dst = y_all[:].rearrange("p (e n) -> p e n", n=C)[:, bank:E:BANKS]
+                    copy = nc.vector.tensor_copy if e == E - 2 else nc.scalar.copy
+                    copy(out=dst, in_=acc[:])
 
         first = raw_tile([P, T])
         nc.vector.tensor_tensor(first[:], y_all[:].indirect(pos1_t[:]), gate_t[:, 0, :], MULT)

@@ -26,9 +26,8 @@ W1_VECTOR_COLS = 32
 W2_LOADS = (2, 2, 4, 4, 4, 2, 2, 2, 1, 1)
 BANKS = 3
 W2_ORDER = [(e, g) for e in range(E - BANKS) for g in range(G)] + [(e, g) for g in range(G) for e in range(E - BANKS, E)]
-OUT_CHUNK = 384
-W1_LOADS = (1,) * E
-RAW_BYTES = 4 * J * (T + 7 * H)
+OUT_CHUNKS = (512, 256)
+RAW_BUFS = 8
 
 
 def tile_routed_moe_kernel(tc, xT, w1, w2, gate, offs, pos1, pos2, out):
@@ -36,7 +35,6 @@ def tile_routed_moe_kernel(tc, xT, w1, w2, gate, offs, pos1, pos2, out):
     with ExitStack() as ctx:
         keep = ctx.enter_context(tc.tile_pool(name="keep", bufs=1))
         ring = ctx.enter_context(tc.tile_pool(name="ring", bufs=2))
-        landing = ctx.enter_context(tc.tile_pool(name="landing", bufs=1))
         psum = ctx.enter_context(tc.psum_pool(name="psum", bufs=2))
 
         offs_t = keep.tile([P, E * C // 16], U16, name="offs_t")
@@ -48,15 +46,8 @@ def tile_routed_moe_kernel(tc, xT, w1, w2, gate, offs, pos1, pos2, out):
         nc.vector.memset(warm[:], 0.0)
         nc.scalar.activation(warm[:, 1:2], warm[:, 0:1], SILU)
 
-        placed = [0]
-
         def raw_tile(shape):
-            size = 4
-            for d in shape[1:]:
-                size *= d
-            at = placed[-1] if placed[-1] + size <= RAW_BYTES else 0
-            placed.append(at + size)
-            return landing.tile(shape, F32, name="raw%d" % len(placed), offset=at)
+            return ring.tile(shape, F32, name="raw", tag="raw", bufs=RAW_BUFS, align_bytes=64)
 
         def grouped_tile(shape):
             return ring.tile(shape, BF16, name="grouped", tag="grouped", bufs=4, align_bytes=64)
@@ -65,10 +56,13 @@ def tile_routed_moe_kernel(tc, xT, w1, w2, gate, offs, pos1, pos2, out):
         nc.sync.dma_start(out=x_raw[:], in_=xT.rearrange("(p j) n -> p j n", j=J))
         nc.sync.dma_start(out=offs_t[:], in_=offs)
         w1_raw = []
-        for n in W1_LOADS:
-            t = raw_tile([P, n, J, H])
-            nc.sync.dma_start(out=t[:], in_=w1[len(w1_raw):len(w1_raw) + n].rearrange("e (p j) h -> p e j h", j=J))
-            w1_raw.extend([t[:, i] for i in range(n)])
+        for e in range(E):
+            t = raw_tile([P, J, H])
+            nc.sync.dma_start(out=t[:], in_=w1[e].rearrange("(p j) h -> p j h", j=J))
+            w1_raw.append(t)
+            if e == RAW_BUFS - 2:
+                nc.sync.dma_start(out=pos1_t[:], in_=pos1)
+                nc.sync.dma_start(out=pos2_t[:], in_=pos2)
         w2_blocks = w2.rearrange("e (g p j) n -> p (e g) j n", p=P, j=J)
         w2_raw = []
         load_start = []
@@ -80,8 +74,6 @@ def tile_routed_moe_kernel(tc, xT, w1, w2, gate, offs, pos1, pos2, out):
             nc.sync.dma_start(out=t[:], in_=w2_blocks[:, rising[0]:rising[-1] + 1:step])
             load_start.append(len(w2_raw))
             w2_raw.extend([t[:, rising.index(block)] for block in blocks])
-        nc.sync.dma_start(out=pos1_t[:], in_=pos1)
-        nc.sync.dma_start(out=pos2_t[:], in_=pos2)
         gate_t = raw_tile([P, 2, T])
         nc.sync.dma_start(out=gate_t[:], in_=gate.rearrange("r p t -> p r t"))
 
@@ -227,14 +219,24 @@ def tile_routed_moe_kernel(tc, xT, w1, w2, gate, offs, pos1, pos2, out):
                     copy = nc.vector.tensor_copy if e == E - 2 else nc.scalar.copy
                     copy(out=dst, in_=acc[:])
 
-        first = raw_tile([P, T])
-        nc.vector.tensor_tensor(first[:], y_all[:].indirect(pos1_t[:]), gate_t[:, 0, :], MULT)
         parts = []
-        for at in range(0, T, OUT_CHUNK):
-            s = slice(at, at + OUT_CHUNK)
-            second = raw_tile([P, OUT_CHUNK])
-            nc.vector.tensor_tensor(second[:], y_all[:].indirect(pos2_t[:, at // 16:(at + OUT_CHUNK) // 16]), gate_t[:, 1, s], MULT)
-            parts.append((s, second))
-        for s, second in parts:
-            nc.vector.tensor_tensor(second[:], second[:], first[:, s], ADD)
-            nc.sync.dma_start(out=out[:, s], in_=second[:])
+        at = 0
+        for n in OUT_CHUNKS:
+            parts.append((slice(at, at + n), slice(at // 16, (at + n) // 16), raw_tile([P, n]), raw_tile([P, n])))
+            at += n
+
+        def fetch(i, r):
+            s, part, a, b = parts[i]
+            nc.vector.tensor_tensor((a, b)[r][:], y_all[:].indirect((pos1_t, pos2_t)[r][:, part]), gate_t[:, r, s], MULT)
+
+        def finish(i):
+            s, part, a, b = parts[i]
+            nc.vector.tensor_tensor(a[:], a[:], b[:], ADD)
+            nc.sync.dma_start(out=out[:, s], in_=a[:])
+
+        fetch(0, 0)
+        fetch(0, 1)
+        fetch(1, 0)
+        finish(0)
+        fetch(1, 1)
+        finish(1)

@@ -41,13 +41,9 @@ def tile_routed_moe_kernel(tc, xT, w1, w2, gate, offs, pos1, pos2, out):
         pos1_t = keep.tile([P, T // 16], U16, name="pos1_t")
         pos2_t = keep.tile([P, T // 16], U16, name="pos2_t")
         y_all = keep.tile([P, E * C], F32, name="y_all")
-        warm = keep.tile([P, 2], F32, name="warm")
-
-        nc.vector.memset(warm[:], 0.0)
-        nc.scalar.activation(warm[:, 1:2], warm[:, 0:1], SILU)
 
         def raw_tile(shape):
-            return ring.tile(shape, F32, name="raw", tag="raw", bufs=RAW_BUFS, align_bytes=64)
+            return ring.tile(shape, F32, name="raw", tag="raw", bufs=RAW_BUFS, align_bytes=256)
 
         def grouped_tile(shape):
             return ring.tile(shape, BF16, name="grouped", tag="grouped", bufs=4, align_bytes=64)

@@ -17,17 +17,25 @@ ADD = mybir.AluOpType.add
 
 P = 128
 J = 4
-G = H // 512
-UNIT = 128 * J
-HALF = 4 * UNIT
+PASS = P * J
+G = H // PASS
+LIST_ROWS = 16
+OPERAND = 128 * J
+HALF = J * OPERAND
+WIDEST = 4096
+
 X_SPLIT = 512
 GATHER = 512
 W1_VECTOR_COLS = 32
-W2_LOADS = (2, 2, 4, 4, 4, 2, 2, 2, 1, 1)
+W1_LOADS = (2,) * 4 + (1,) * 4
+RAW_BUFS = 3
+GROUPED_BUFS = 4
 BANKS = 3
 W2_ORDER = [(e, g) for e in range(E - BANKS) for g in range(G)] + [(e, g) for g in range(G) for e in range(E - BANKS, E)]
+W2_LOADS = (2, 6, 4, 4, 2, 2, 2, 1, 1)
+W2_BORROWS = 3
+LATE_BATCH = 2
 OUT_CHUNKS = (512, 256)
-RAW_BUFS = 8
 
 
 def tile_routed_moe_kernel(tc, xT, w1, w2, gate, offs, pos1, pos2, out):
@@ -37,33 +45,35 @@ def tile_routed_moe_kernel(tc, xT, w1, w2, gate, offs, pos1, pos2, out):
         ring = ctx.enter_context(tc.tile_pool(name="ring", bufs=2))
         psum = ctx.enter_context(tc.psum_pool(name="psum", bufs=2))
 
-        offs_t = keep.tile([P, E * C // 16], U16, name="offs_t")
-        pos1_t = keep.tile([P, T // 16], U16, name="pos1_t")
-        pos2_t = keep.tile([P, T // 16], U16, name="pos2_t")
+        offs_t = keep.tile([P, E * C // LIST_ROWS], U16, name="offs_t")
+        pos1_t = keep.tile([P, T // LIST_ROWS], U16, name="pos1_t")
+        pos2_t = keep.tile([P, T // LIST_ROWS], U16, name="pos2_t")
         y_all = keep.tile([P, E * C], F32, name="y_all")
 
         def raw_tile(shape):
             return ring.tile(shape, F32, name="raw", tag="raw", bufs=RAW_BUFS, align_bytes=256)
 
-        def grouped_tile(shape):
-            return ring.tile(shape, BF16, name="grouped", tag="grouped", bufs=4, align_bytes=64)
+        def grouped_tile(shape, dtype):
+            return ring.tile(shape, dtype, name="grouped", tag="grouped", bufs=GROUPED_BUFS, align_bytes=64)
 
         x_raw = raw_tile([P, J, T])
         nc.sync.dma_start(out=x_raw[:], in_=xT.rearrange("(p j) n -> p j n", j=J))
         nc.sync.dma_start(out=offs_t[:], in_=offs)
+        nc.sync.dma_start(out=pos1_t[:], in_=pos1)
+        nc.sync.dma_start(out=pos2_t[:], in_=pos2)
         w1_raw = []
-        for e in range(E):
-            t = raw_tile([P, J, H])
-            nc.sync.dma_start(out=t[:], in_=w1[e].rearrange("(p j) h -> p j h", j=J))
-            w1_raw.append(t)
-            if e == RAW_BUFS - 2:
-                nc.sync.dma_start(out=pos1_t[:], in_=pos1)
-                nc.sync.dma_start(out=pos2_t[:], in_=pos2)
+        for n in W1_LOADS:
+            t = raw_tile([P, n, J, H])
+            nc.sync.dma_start(out=t[:], in_=w1[len(w1_raw):len(w1_raw) + n].rearrange("e (p j) h -> p e j h", j=J))
+            w1_raw.extend([t[:, i] for i in range(n)])
         w2_blocks = w2.rearrange("e (g p j) n -> p (e g) j n", p=P, j=J)
         w2_raw = []
         load_start = []
         for n in W2_LOADS:
-            t = raw_tile([P, n, J, N])
+            if len(load_start) == W2_BORROWS:
+                t = raw_tile([P, n, J, N])
+            else:
+                t = keep.tile([P, n, J, N], F32, name="w2_raw%d" % len(w2_raw), align_bytes=256)
             blocks = [e * G + g for e, g in W2_ORDER[len(w2_raw):len(w2_raw) + n]]
             rising = sorted(blocks)
             step = rising[1] - rising[0] if n > 1 else 1
@@ -78,27 +88,27 @@ def tile_routed_moe_kernel(tc, xT, w1, w2, gate, offs, pos1, pos2, out):
         nc.gpsimd.memset(x_scales[:], 0)
         x_parts = []
         for a, b, copy in ((0, X_SPLIT, nc.vector.tensor_copy), (X_SPLIT, T, nc.scalar.copy)):
-            t = grouped_tile([P, b - a, J])
+            t = grouped_tile([P, b - a, J], BF16)
             copy(out=t[:].rearrange("p (c i) j -> p c j i", i=2), in_=x_raw[:, :, a:b].rearrange("p j (c i) -> p c j i", i=2))
             x_parts.append((a, b, t))
         for a, b, t in x_parts:
             nc.vector.quantize_mx(out=x_codes[:, a:b].bitcast(FP8X4), scales=x_scales[:, a:b],
                                   in_=t[:].rearrange("p n j -> p (n j)"))
-        slot_codes = {}
+        slot_q = {}
         for at in range(0, E * C, GATHER):
-            codes = keep.tile([P, GATHER], U32, name="g_codes%d" % at, align_bytes=64)
-            scales = keep.tile([P, GATHER], U8, name="g_scales%d" % at, align_bytes=64)
-            part = offs_t[:, at // 16:(at + GATHER) // 16]
+            codes = keep.tile([P, GATHER], U32, name="slot_codes%d" % at, align_bytes=64)
+            scales = keep.tile([P, GATHER], U8, name="slot_scales%d" % at, align_bytes=64)
+            part = offs_t[:, at // LIST_ROWS:(at + GATHER) // LIST_ROWS]
             nc.vector.tensor_copy(out=codes[:], in_=x_codes[:].indirect(part))
             nc.vector.tensor_copy(out=scales[:], in_=x_scales[:].indirect(part))
             for q in range(GATHER // C):
-                slot_codes[at // C + q] = (codes[:, q * C:(q + 1) * C], scales[:, q * C:(q + 1) * C])
+                slot_q[at // C + q] = (codes[:, q * C:(q + 1) * C], scales[:, q * C:(q + 1) * C])
 
         def quantise(values, codes, scales):
             n = values.shape[1]
             at = 0
             while at < n:
-                width = 4096
+                width = WIDEST
                 while width > n - at:
                     width //= 2
                 words = slice(at // J, (at + width) // J)
@@ -106,129 +116,129 @@ def tile_routed_moe_kernel(tc, xT, w1, w2, gate, offs, pos1, pos2, out):
                 at += width
 
         last_pair = (E - 2, E - 1)
-        hidden_of = [[(e, g) for e, g in ((k - 2, 0), (k - 3, 1)) if e >= 0 and e not in last_pair] for k in range(E + 1)]
-        weights_of = [[(e, g) for e, g in ((k - 1, 1), (k, 0)) if 0 <= e < E] for k in range(E + 1)]
-        batch = {}
+        hidden_of = [[(e, g) for e, g in ((b - 2, 0), (b - 3, 1)) if e >= 0 and e not in last_pair] for b in range(E + 1)]
+        weights_of = [[(e, g) for e, g in ((b - 1, 1), (b, 0)) if 0 <= e < E] for b in range(E + 1)]
+        w1_batch = {}
         late = keep.tile([P, 2 * HALF], BF16, name="late", align_bytes=64)
 
-        def batch_tile(k):
-            if k not in batch:
-                batch[k] = grouped_tile([P, len(hidden_of[k]) * UNIT + len(weights_of[k]) * HALF])
-            return batch[k]
+        def w1_batch_tile(b):
+            if b not in w1_batch:
+                w1_batch[b] = grouped_tile([P, len(hidden_of[b]) * OPERAND + len(weights_of[b]) * HALF], BF16)
+            return w1_batch[b]
 
         def weights_view(e, g):
-            k = e + g
-            at = len(hidden_of[k]) * UNIT + weights_of[k].index((e, g)) * HALF
-            dst = batch_tile(k)[:, at:at + HALF].rearrange("p (t m u j) -> p m u t j", t=4, u=2, j=2)
-            src = w1_raw[e][:, :, g * 512:(g + 1) * 512].rearrange("p (u j) (m t) -> p m u t j", t=4, j=2)
+            b = e + g
+            at = len(hidden_of[b]) * OPERAND + weights_of[b].index((e, g)) * HALF
+            dst = w1_batch_tile(b)[:, at:at + HALF].rearrange("p (t m u j) -> p m u t j", t=J, u=2, j=2)
+            src = w1_raw[e][:, :, g * PASS:(g + 1) * PASS].rearrange("p (u j) (m t) -> p m u t j", t=J, j=2)
             return dst, src
 
         def hidden_view(e, g):
             if e in last_pair:
-                at = HALF + ((e - last_pair[0]) * G + g) * UNIT
+                at = HALF + ((e - last_pair[0]) * G + g) * OPERAND
                 host = late
             else:
-                at = hidden_of[e + 2 + g].index((e, g)) * UNIT
-                host = batch_tile(e + 2 + g)
-            return host[:, at:at + UNIT].rearrange("p (n j) -> p n j", j=J)
+                at = hidden_of[e + 2 + g].index((e, g)) * OPERAND
+                host = w1_batch_tile(e + 2 + g)
+            return host[:, at:at + OPERAND].rearrange("p (n j) -> p n j", j=J)
 
-        code_words = (E // 2 - 1) * G * C + 2 * 512
+        code_words = (E // 2 - 1) * G * C + G * HALF // J
         w1_codes = [keep.tile([P, code_words], U32, name="w1_codes%d" % i, align_bytes=64) for i in range(2)]
         w1_scales = [keep.tile([P, code_words], U8, name="w1_scales%d" % i, align_bytes=64) for i in range(2)]
         kept = [0, 0]
         h_q = {}
-        for k in range(E + 1):
-            if k == 0:
-                for g in range(G):
-                    dst, src = weights_view(0, g)
-                    nc.scalar.copy(out=dst, in_=src)
-            elif k < E:
+        for b in range(E + 1):
+            if b < E:
                 m = W1_VECTOR_COLS
-                dst, src = weights_view(k, 0)
+                dst, src = weights_view(b, 0)
                 nc.vector.tensor_copy(out=dst, in_=src)
-                dst, src = weights_view(k, 1)
+                dst, src = weights_view(b, 1)
                 nc.vector.tensor_copy(out=dst[:, 0:m], in_=src[:, 0:m])
                 nc.scalar.copy(out=dst[:, m:128], in_=src[:, m:128])
-            t = batch_tile(k)
-            words = slice(kept[k % 2], kept[k % 2] + t.shape[1] // J)
-            codes, scales = w1_codes[k % 2][:, words], w1_scales[k % 2][:, words]
+            t = w1_batch_tile(b)
+            words = slice(kept[b % 2], kept[b % 2] + t.shape[1] // J)
+            codes, scales = w1_codes[b % 2][:, words], w1_scales[b % 2][:, words]
             quantise(t[:], codes, scales)
-            for i, key in enumerate(hidden_of[k]):
+            for i, key in enumerate(hidden_of[b]):
                 h_q[key] = (codes[:, i * C:(i + 1) * C], scales[:, i * C:(i + 1) * C])
-            kept[k % 2] += len(hidden_of[k]) * C
-            for i, (e, g) in enumerate(weights_of[k]):
-                xc, xs = slot_codes[e]
-                acc = psum.tile([P, 4, C], F32, name="acc", tag="acc", bufs=4)
-                for q in range(4):
-                    at = len(hidden_of[k]) * C + (4 * i + q) * 128
+            kept[b % 2] += len(hidden_of[b]) * C
+            for i, (e, g) in enumerate(weights_of[b]):
+                xc, xs = slot_q[e]
+                acc = psum.tile([P, J, C], F32, name="acc", tag="acc", bufs=2 * G)
+                for q in range(J):
+                    at = len(hidden_of[b]) * C + (J * i + q) * 128
                     s = slice(at, at + 128)
                     nc.tensor.matmul_mx(out=acc[:, q, :], lhsT=codes[:, s].bitcast(FP8X4), lhsT_scale=scales[:, s],
                                         rhs=xc.bitcast(FP8X4), rhs_scale=xs, start=True, stop=True)
                 nc.scalar.activation(hidden_view(e, g), acc[:].rearrange("p t n -> p n t"), SILU)
 
-        ends = [1] + [b + 1 for b in load_start[2:-2]] + [load_start[-2], E * G]
-        batches = [range(a, b) for a, b in zip([0] + ends[:-1], ends)]
-        late_batch = 2
-        w2_tile = {late_batch: late}
+        ends = [1, 5] + [at + 1 for at in load_start[2:-2]] + [load_start[-2], E * G]
+        w2_batches = [range(a, z) for a, z in zip([0] + ends[:-1], ends)]
+        w2_batch = {LATE_BATCH: late}
 
-        def group_w2(block, copy):
-            b = [i for i, blocks in enumerate(batches) if block in blocks][0]
-            if b not in w2_tile:
-                w2_tile[b] = grouped_tile([P, len(batches[b]) * UNIT])
-            at = (block - batches[b].start) * UNIT
-            copy(out=w2_tile[b][:, at:at + UNIT].rearrange("p (c i j) -> p c j i", i=2, j=J),
-                 in_=w2_raw[block].rearrange("p j (c i) -> p c j i", i=2))
+        def group_w2(place, copy):
+            b = [i for i, places in enumerate(w2_batches) if place in places][0]
+            if b not in w2_batch:
+                w2_batch[b] = grouped_tile([P, len(w2_batches[b]) * OPERAND], BF16)
+            at = (place - w2_batches[b].start) * OPERAND
+            copy(out=w2_batch[b][:, at:at + OPERAND].rearrange("p (c i j) -> p c j i", i=2, j=J),
+                 in_=w2_raw[place].rearrange("p j (c i) -> p c j i", i=2))
+
+        def vector_blocks(load):
+            if load in (0, len(W2_LOADS) - 2):
+                return 0
+            if load == 1:
+                return W2_LOADS[load] - 2
+            return (W2_LOADS[load] + 1) // 2
 
         y_bank = {}
-        grouped = 0
-        for b in range(len(batches)):
-            for at, n in zip(load_start, W2_LOADS):
-                if grouped <= at < max(batches[b].stop, 4):
-                    on_vector = 0 if at in (0, load_start[-2]) else n if at == load_start[1] else (n + 1) // 2
-                    for i in range(n):
-                        group_w2(at + i, nc.vector.tensor_copy if i < on_vector else nc.scalar.copy)
-                    grouped = at + n
-            t = w2_tile[b]
+        load = 0
+        for b, places in enumerate(w2_batches):
+            while load < len(W2_LOADS) and (load_start[load] < places.stop or load < 2):
+                for i in range(W2_LOADS[load]):
+                    group_w2(load_start[load] + i, nc.vector.tensor_copy if i < vector_blocks(load) else nc.scalar.copy)
+                load += 1
+            t = w2_batch[b]
             words = t.shape[1] // J
-            if b == late_batch:
+            if b == LATE_BATCH:
                 codes = keep.tile([P, words], U32, name="late_codes", align_bytes=64)
                 scales = keep.tile([P, words], U8, name="late_scales", align_bytes=64)
                 for i in range(2 * G):
-                    s = slice(512 + i * C, 512 + (i + 1) * C)
+                    s = slice(HALF // J + i * C, HALF // J + (i + 1) * C)
                     h_q[last_pair[0] + i // G, i % G] = (codes[:, s], scales[:, s])
             else:
                 codes = ring.tile([P, words], U32, name="codes", tag="codes", bufs=3, align_bytes=64)
                 scales = ring.tile([P, words], U8, name="scales", tag="scales", bufs=3, align_bytes=64)
             quantise(t[:], codes[:], scales[:])
-            for i, block in enumerate(batches[b]):
-                e, g = W2_ORDER[block]
-                bank, place = e % BANKS, e // BANKS
+            for i, place in enumerate(places):
+                e, g = W2_ORDER[place]
+                bank = e % BANKS
                 if bank not in y_bank:
                     y_bank[bank] = psum.tile([N, E // BANKS, C], F32, name="acc_y", tag="acc_y", bufs=BANKS)
-                acc = y_bank[bank]
                 hc, hs = h_q[e, g]
                 w = slice(i * N, (i + 1) * N)
-                nc.tensor.matmul_mx(out=acc[:, place, :], lhsT=codes[:, w].bitcast(FP8X4), lhsT_scale=scales[:, w],
+                nc.tensor.matmul_mx(out=y_bank[bank][:, e // BANKS, :], lhsT=codes[:, w].bitcast(FP8X4), lhsT_scale=scales[:, w],
                                     rhs=hc.bitcast(FP8X4), rhs_scale=hs, start=(g == 0), stop=(g == G - 1))
                 if e >= E - BANKS and g == G - 1:
                     dst = y_all[:].rearrange("p (e n) -> p e n", n=C)[:, bank:E:BANKS]
                     copy = nc.vector.tensor_copy if e == E - 2 else nc.scalar.copy
-                    copy(out=dst, in_=acc[:])
+                    copy(out=dst, in_=y_bank[bank][:])
 
-        parts = []
+        chunks = []
         at = 0
         for n in OUT_CHUNKS:
-            parts.append((slice(at, at + n), slice(at // 16, (at + n) // 16), raw_tile([P, n]), raw_tile([P, n])))
+            terms = (grouped_tile([P, n], F32), grouped_tile([P, n], F32))
+            chunks.append((slice(at, at + n), slice(at // LIST_ROWS, (at + n) // LIST_ROWS), terms))
             at += n
 
-        def fetch(i, r):
-            s, part, a, b = parts[i]
-            nc.vector.tensor_tensor((a, b)[r][:], y_all[:].indirect((pos1_t, pos2_t)[r][:, part]), gate_t[:, r, s], MULT)
+        def fetch(chunk, r):
+            tokens, columns, terms = chunks[chunk]
+            nc.vector.tensor_tensor(terms[r][:], y_all[:].indirect((pos1_t, pos2_t)[r][:, columns]), gate_t[:, r, tokens], MULT)
 
-        def finish(i):
-            s, part, a, b = parts[i]
-            nc.vector.tensor_tensor(a[:], a[:], b[:], ADD)
-            nc.sync.dma_start(out=out[:, s], in_=a[:])
+        def finish(chunk):
+            tokens, columns, terms = chunks[chunk]
+            nc.vector.tensor_tensor(terms[0][:], terms[0][:], terms[1][:], ADD)
+            nc.sync.dma_start(out=out[:, tokens], in_=terms[0][:])
 
         fetch(0, 0)
         fetch(0, 1)

@@ -27,14 +27,15 @@ WIDEST = 4096
 X_SPLIT = 512
 GATHER = 512
 W1_VECTOR_COLS = 32
-W1_LOADS = (2,) * 4 + (1,) * 4
-RAW_BUFS = 3
+W1_LOADS = (2, 2, 2, 1, 1, 1, 1, 1, 1)
+W1_SHARE = (96, 96) + (160,) * 10
+W1_LAST_VECTOR_COLS = 64
+LANDING = 7 * J * H
 GROUPED_BUFS = 4
-BANKS = 3
-W2_ORDER = [(e, g) for e in range(E - BANKS) for g in range(G)] + [(e, g) for g in range(G) for e in range(E - BANKS, E)]
-W2_LOADS = (2, 6, 4, 4, 2, 2, 2, 1, 1)
-W2_BORROWS = 3
-LATE_BATCH = 2
+W2_LOADS = ((0, 0, 2), (3, 1, 2), (1, 1, 2), (1, 1, 2), (1, 0, 1), (1, 0, 1), (1, 0, 1), (1, 0, 1))
+LATE_HIDDEN = 4
+LATE_BATCH = 1
+Y_BANKS = ((0, 4), (4, 8), (8, 10), (10, 11), (11, 12))
 OUT_CHUNKS = (512, 256)
 
 
@@ -48,40 +49,68 @@ def tile_routed_moe_kernel(tc, xT, w1, w2, gate, offs, pos1, pos2, out):
         offs_t = keep.tile([P, E * C // LIST_ROWS], U16, name="offs_t")
         pos1_t = keep.tile([P, T // LIST_ROWS], U16, name="pos1_t")
         pos2_t = keep.tile([P, T // LIST_ROWS], U16, name="pos2_t")
-        y_all = keep.tile([P, E * C], F32, name="y_all")
+        y_all = keep.tile([P, E * C], F32, name="y_all", align_bytes=256)
+        landing = keep.tile([P, LANDING], F32, name="landing", align_bytes=256)
+        tenant = [-1] * (LANDING // (J * H))
+        cursor = [0]
+        stream = []
 
-        def raw_tile(shape):
-            return ring.tile(shape, F32, name="raw", tag="raw", bufs=RAW_BUFS, align_bytes=256)
+        def land(n, expert=None):
+            if cursor[0] + n > LANDING:
+                cursor[0] = 0
+            places = range(cursor[0] // (J * H), (cursor[0] + n - 1) // (J * H) + 1)
+            t = landing[:, cursor[0]:cursor[0] + n]
+            after = max(tenant[i] for i in places)
+            for i in places:
+                if expert is not None:
+                    tenant[i] = expert + i - places.start
+            cursor[0] += n
+            return after, t
+
+        def issue(copied):
+            while stream and stream[0][0] <= copied:
+                after, dst, src = stream.pop(0)
+                nc.sync.dma_start(out=dst, in_=src)
 
         def grouped_tile(shape, dtype):
             return ring.tile(shape, dtype, name="grouped", tag="grouped", bufs=GROUPED_BUFS, align_bytes=64)
 
-        x_raw = raw_tile([P, J, T])
+        x_raw = keep.tile([P, J, T], F32, name="x_raw", tag="first_last", align_bytes=256)
         nc.sync.dma_start(out=x_raw[:], in_=xT.rearrange("(p j) n -> p j n", j=J))
         nc.sync.dma_start(out=offs_t[:], in_=offs)
         nc.sync.dma_start(out=pos1_t[:], in_=pos1)
         nc.sync.dma_start(out=pos2_t[:], in_=pos2)
-        w1_raw = []
+        w1_raw = {}
+        e = 0
         for n in W1_LOADS:
-            t = raw_tile([P, n, J, H])
-            nc.sync.dma_start(out=t[:], in_=w1[len(w1_raw):len(w1_raw) + n].rearrange("e (p j) h -> p e j h", j=J))
-            w1_raw.extend([t[:, i] for i in range(n)])
+            after, t = land(n * J * H, e)
+            t = t.rearrange("p (e j h) -> p e j h", j=J, h=H)
+            stream.append((after, t, w1[e:e + n].rearrange("e (p j) h -> p e j h", j=J)))
+            for i in range(n):
+                for g in range(G):
+                    w1_raw[e + i, g] = t[:, i, :, g * PASS:(g + 1) * PASS]
+            e += n
+        for e in range(e, E):
+            for g in range(G):
+                after, t = land(J * PASS)
+                w1_raw[e, g] = t.rearrange("p (j h) -> p j h", j=J)
+                stream.append((after, w1_raw[e, g], w1[e, :, g * PASS:(g + 1) * PASS].rearrange("(p j) h -> p j h", j=J)))
         w2_blocks = w2.rearrange("e (g p j) n -> p (e g) j n", p=P, j=J)
         w2_raw = []
-        load_start = []
-        for n in W2_LOADS:
-            if len(load_start) == W2_BORROWS:
-                t = raw_tile([P, n, J, N])
+        block = 0
+        for shares in W2_LOADS:
+            n = sum(shares)
+            if block + n == E * G:
+                t = y_all[:, 2 * C:2 * C + n * OPERAND]
             else:
-                t = keep.tile([P, n, J, N], F32, name="w2_raw%d" % len(w2_raw), align_bytes=256)
-            blocks = [e * G + g for e, g in W2_ORDER[len(w2_raw):len(w2_raw) + n]]
-            rising = sorted(blocks)
-            step = rising[1] - rising[0] if n > 1 else 1
-            nc.sync.dma_start(out=t[:], in_=w2_blocks[:, rising[0]:rising[-1] + 1:step])
-            load_start.append(len(w2_raw))
-            w2_raw.extend([t[:, rising.index(block)] for block in blocks])
-        gate_t = raw_tile([P, 2, T])
-        nc.sync.dma_start(out=gate_t[:], in_=gate.rearrange("r p t -> p r t"))
+                after, t = land(n * OPERAND)
+            t = t.rearrange("p (b j n) -> p b j n", j=J, n=N)
+            stream.append((after, t, w2_blocks[:, block:block + n]))
+            w2_raw.append(t)
+            block += n
+        gate_t = keep.tile([P, 2, T], F32, name="gate_t", tag="first_last", align_bytes=256)
+        stream.append((after, gate_t[:], gate.rearrange("r p t -> p r t")))
+        issue(-1)
 
         x_codes = keep.tile([P, T], U32, name="x_codes", align_bytes=64)
         x_scales = keep.tile([P, T], U8, name="x_scales", align_bytes=64)
@@ -115,11 +144,19 @@ def tile_routed_moe_kernel(tc, xT, w1, w2, gate, offs, pos1, pos2, out):
                 nc.vector.quantize_mx(out=codes[:, words].bitcast(FP8X4), scales=scales[:, words], in_=values[:, at:at + width])
                 at += width
 
-        last_pair = (E - 2, E - 1)
-        hidden_of = [[(e, g) for e, g in ((b - 2, 0), (b - 3, 1)) if e >= 0 and e not in last_pair] for b in range(E + 1)]
+        late_hidden = [(e, g) for e in range(E) for g in range(G)][-LATE_HIDDEN:]
+        hidden_of = [[key for key in ((b - 2, 0), (b - 3, 1)) if key[0] >= 0 and key not in late_hidden] for b in range(E + 1)]
         weights_of = [[(e, g) for e, g in ((b - 1, 1), (b, 0)) if 0 <= e < E] for b in range(E + 1)]
         w1_batch = {}
-        late = keep.tile([P, 2 * HALF], BF16, name="late", align_bytes=64)
+        ends = []
+        block = 0
+        for shares in W2_LOADS:
+            ends.append(block + shares[0])
+            block += sum(shares)
+        ends = [z for z in ends if z > 0] + [E * G]
+        w2_batches = [range(a, z) for a, z in zip([0] + ends[:-1], ends)]
+        late_blocks = len(w2_batches[LATE_BATCH])
+        late = keep.tile([P, (late_blocks + len(late_hidden)) * OPERAND], BF16, name="late", align_bytes=64)
 
         def w1_batch_tile(b):
             if b not in w1_batch:
@@ -130,31 +167,33 @@ def tile_routed_moe_kernel(tc, xT, w1, w2, gate, offs, pos1, pos2, out):
             b = e + g
             at = len(hidden_of[b]) * OPERAND + weights_of[b].index((e, g)) * HALF
             dst = w1_batch_tile(b)[:, at:at + HALF].rearrange("p (t m u j) -> p m u t j", t=J, u=2, j=2)
-            src = w1_raw[e][:, :, g * PASS:(g + 1) * PASS].rearrange("p (u j) (m t) -> p m u t j", t=J, j=2)
+            src = w1_raw[e, g].rearrange("p (u j) (m t) -> p m u t j", t=J, j=2)
             return dst, src
 
         def hidden_view(e, g):
-            if e in last_pair:
-                at = HALF + ((e - last_pair[0]) * G + g) * OPERAND
+            if (e, g) in late_hidden:
+                at = (late_blocks + late_hidden.index((e, g))) * OPERAND
                 host = late
             else:
                 at = hidden_of[e + 2 + g].index((e, g)) * OPERAND
                 host = w1_batch_tile(e + 2 + g)
             return host[:, at:at + OPERAND].rearrange("p (n j) -> p n j", j=J)
 
-        code_words = (E // 2 - 1) * G * C + G * HALF // J
+        code_words = (E // 2) * G * C + G * HALF // J
         w1_codes = [keep.tile([P, code_words], U32, name="w1_codes%d" % i, align_bytes=64) for i in range(2)]
         w1_scales = [keep.tile([P, code_words], U8, name="w1_scales%d" % i, align_bytes=64) for i in range(2)]
         kept = [0, 0]
         h_q = {}
         for b in range(E + 1):
             if b < E:
-                m = W1_VECTOR_COLS
-                dst, src = weights_view(b, 0)
-                nc.vector.tensor_copy(out=dst, in_=src)
-                dst, src = weights_view(b, 1)
-                nc.vector.tensor_copy(out=dst[:, 0:m], in_=src[:, 0:m])
-                nc.scalar.copy(out=dst[:, m:128], in_=src[:, m:128])
+                for g in range(G):
+                    m = min(128, max(0, W1_SHARE[b] - 128 * g))
+                    dst, src = weights_view(b, g)
+                    if m > 0:
+                        nc.vector.tensor_copy(out=dst[:, 0:m], in_=src[:, 0:m])
+                    if m < 128:
+                        nc.scalar.copy(out=dst[:, m:128], in_=src[:, m:128])
+                issue(b)
             t = w1_batch_tile(b)
             words = slice(kept[b % 2], kept[b % 2] + t.shape[1] // J)
             codes, scales = w1_codes[b % 2][:, words], w1_scales[b % 2][:, words]
@@ -172,57 +211,56 @@ def tile_routed_moe_kernel(tc, xT, w1, w2, gate, offs, pos1, pos2, out):
                                         rhs=xc.bitcast(FP8X4), rhs_scale=xs, start=True, stop=True)
                 nc.scalar.activation(hidden_view(e, g), acc[:].rearrange("p t n -> p n t"), SILU)
 
-        ends = [1, 5] + [at + 1 for at in load_start[2:-2]] + [load_start[-2], E * G]
-        w2_batches = [range(a, z) for a, z in zip([0] + ends[:-1], ends)]
         w2_batch = {LATE_BATCH: late}
 
-        def group_w2(place, copy):
-            b = [i for i, places in enumerate(w2_batches) if place in places][0]
+        def group_w2(load, first, n, block, copy):
+            b = [i for i, blocks in enumerate(w2_batches) if block in blocks][0]
             if b not in w2_batch:
                 w2_batch[b] = grouped_tile([P, len(w2_batches[b]) * OPERAND], BF16)
-            at = (place - w2_batches[b].start) * OPERAND
-            copy(out=w2_batch[b][:, at:at + OPERAND].rearrange("p (c i j) -> p c j i", i=2, j=J),
-                 in_=w2_raw[place].rearrange("p j (c i) -> p c j i", i=2))
-
-        def vector_blocks(load):
-            if load in (0, len(W2_LOADS) - 2):
-                return 0
-            if load == 1:
-                return W2_LOADS[load] - 2
-            return (W2_LOADS[load] + 1) // 2
+            at = (block - w2_batches[b].start) * OPERAND
+            copy(out=w2_batch[b][:, at:at + n * OPERAND].rearrange("p (b c i j) -> p b c j i", b=n, i=2, j=J),
+                 in_=w2_raw[load][:, first:first + n].rearrange("p b j (c i) -> p b c j i", i=2))
 
         y_bank = {}
         load = 0
-        for b, places in enumerate(w2_batches):
-            while load < len(W2_LOADS) and (load_start[load] < places.stop or load < 2):
-                for i in range(W2_LOADS[load]):
-                    group_w2(load_start[load] + i, nc.vector.tensor_copy if i < vector_blocks(load) else nc.scalar.copy)
+        block = 0
+        for b, blocks in enumerate(w2_batches):
+            while load < len(W2_LOADS) and block < blocks.stop:
+                first = 0
+                for n, copy in zip(W2_LOADS[load], (nc.vector.tensor_copy, nc.vector.tensor_copy, nc.scalar.copy)):
+                    if n > 1:
+                        group_w2(load, first, n - n % 2, block, copy)
+                    if n % 2:
+                        group_w2(load, first + n - 1, 1, block + n - 1, copy)
+                    first += n
+                    block += n
                 load += 1
             t = w2_batch[b]
             words = t.shape[1] // J
             if b == LATE_BATCH:
                 codes = keep.tile([P, words], U32, name="late_codes", align_bytes=64)
                 scales = keep.tile([P, words], U8, name="late_scales", align_bytes=64)
-                for i in range(2 * G):
-                    s = slice(HALF // J + i * C, HALF // J + (i + 1) * C)
-                    h_q[last_pair[0] + i // G, i % G] = (codes[:, s], scales[:, s])
+                for i, key in enumerate(late_hidden):
+                    s = slice((late_blocks + i) * C, (late_blocks + i + 1) * C)
+                    h_q[key] = (codes[:, s], scales[:, s])
             else:
                 codes = ring.tile([P, words], U32, name="codes", tag="codes", bufs=3, align_bytes=64)
                 scales = ring.tile([P, words], U8, name="scales", tag="scales", bufs=3, align_bytes=64)
             quantise(t[:], codes[:], scales[:])
-            for i, place in enumerate(places):
-                e, g = W2_ORDER[place]
-                bank = e % BANKS
+            for i, number in enumerate(blocks):
+                e, g = divmod(number, G)
+                bank = [q for q, (a, z) in enumerate(Y_BANKS) if a <= e < z][0]
+                a, z = Y_BANKS[bank]
                 if bank not in y_bank:
-                    y_bank[bank] = psum.tile([N, E // BANKS, C], F32, name="acc_y", tag="acc_y", bufs=BANKS)
+                    tag = "acc_y" if bank < 4 else "acc"
+                    y_bank[bank] = psum.tile([N, z - a, C], F32, name="acc_y", tag=tag, bufs=4)
                 hc, hs = h_q[e, g]
                 w = slice(i * N, (i + 1) * N)
-                nc.tensor.matmul_mx(out=y_bank[bank][:, e // BANKS, :], lhsT=codes[:, w].bitcast(FP8X4), lhsT_scale=scales[:, w],
+                nc.tensor.matmul_mx(out=y_bank[bank][:, e - a, :], lhsT=codes[:, w].bitcast(FP8X4), lhsT_scale=scales[:, w],
                                     rhs=hc.bitcast(FP8X4), rhs_scale=hs, start=(g == 0), stop=(g == G - 1))
-                if e >= E - BANKS and g == G - 1:
-                    dst = y_all[:].rearrange("p (e n) -> p e n", n=C)[:, bank:E:BANKS]
-                    copy = nc.vector.tensor_copy if e == E - 2 else nc.scalar.copy
-                    copy(out=dst, in_=y_bank[bank][:])
+        for bank, (a, z) in enumerate(Y_BANKS):
+            copy = nc.vector.tensor_copy if bank in (1, 4) else nc.scalar.copy
+            copy(out=y_all[:, a * C:z * C], in_=y_bank[bank][:].rearrange("p e n -> p (e n)"))
 
         chunks = []
         at = 0

@@ -27,15 +27,13 @@ WIDEST = 4096
 X_SPLIT = 512
 GATHER = 512
 W1_VECTOR_COLS = 32
-W1_LOADS = (2, 2, 2, 1, 1, 1, 1, 1, 1)
-W1_SHARE = (96, 96) + (160,) * 10
-W1_LAST_VECTOR_COLS = 64
-LANDING = 7 * J * H
+W1_LOADS = (3, 2, 2, 1, 1, 1, 1, 1)
+PLACES = 7
+PLACE = J * H
 GROUPED_BUFS = 4
-W2_LOADS = ((0, 0, 2), (3, 1, 2), (1, 1, 2), (1, 1, 2), (1, 0, 1), (1, 0, 1), (1, 0, 1), (1, 0, 1))
-LATE_HIDDEN = 4
+W2_LOADS = ((0, 0, 2), (3, 1, 2), (1, 1, 2), (1, 1, 2), (1, 1, 1), (1, 1, 1), (0, 1, 1))
 LATE_BATCH = 1
-Y_BANKS = ((0, 4), (4, 8), (8, 10), (10, 11), (11, 12))
+Y_BANKS = ((0, 4), (4, 8), (8, 11), (11, 12))
 OUT_CHUNKS = (512, 256)
 
 
@@ -50,26 +48,20 @@ def tile_routed_moe_kernel(tc, xT, w1, w2, gate, offs, pos1, pos2, out):
         pos1_t = keep.tile([P, T // LIST_ROWS], U16, name="pos1_t")
         pos2_t = keep.tile([P, T // LIST_ROWS], U16, name="pos2_t")
         y_all = keep.tile([P, E * C], F32, name="y_all", align_bytes=256)
-        landing = keep.tile([P, LANDING], F32, name="landing", align_bytes=256)
-        tenant = [-1] * (LANDING // (J * H))
+        landing = keep.tile([P, PLACES * PLACE], F32, name="landing", align_bytes=256)
+        tenant = [-1] * PLACES
         cursor = [0]
         stream = []
 
-        def land(n, expert=None):
-            if cursor[0] + n > LANDING:
+        def land(n):
+            if cursor[0] + n > PLACES * PLACE:
                 cursor[0] = 0
-            places = range(cursor[0] // (J * H), (cursor[0] + n - 1) // (J * H) + 1)
-            t = landing[:, cursor[0]:cursor[0] + n]
-            after = max(tenant[i] for i in places)
-            for i in places:
-                if expert is not None:
-                    tenant[i] = expert + i - places.start
             cursor[0] += n
-            return after, t
+            return landing[:, cursor[0] - n:cursor[0]], range((cursor[0] - n) // PLACE, (cursor[0] - 1) // PLACE + 1)
 
         def issue(copied):
             while stream and stream[0][0] <= copied:
-                after, dst, src = stream.pop(0)
+                dst, src = stream.pop(0)[1:]
                 nc.sync.dma_start(out=dst, in_=src)
 
         def grouped_tile(shape, dtype):
@@ -78,38 +70,31 @@ def tile_routed_moe_kernel(tc, xT, w1, w2, gate, offs, pos1, pos2, out):
         x_raw = keep.tile([P, J, T], F32, name="x_raw", tag="first_last", align_bytes=256)
         nc.sync.dma_start(out=x_raw[:], in_=xT.rearrange("(p j) n -> p j n", j=J))
         nc.sync.dma_start(out=offs_t[:], in_=offs)
-        nc.sync.dma_start(out=pos1_t[:], in_=pos1)
-        nc.sync.dma_start(out=pos2_t[:], in_=pos2)
-        w1_raw = {}
-        e = 0
+        w1_raw = []
         for n in W1_LOADS:
-            after, t = land(n * J * H, e)
+            t, places = land(n * PLACE)
             t = t.rearrange("p (e j h) -> p e j h", j=J, h=H)
-            stream.append((after, t, w1[e:e + n].rearrange("e (p j) h -> p e j h", j=J)))
+            e = len(w1_raw)
+            stream.append((max(tenant[i] for i in places), t, w1[e:e + n].rearrange("e (p j) h -> p e j h", j=J)))
             for i in range(n):
-                for g in range(G):
-                    w1_raw[e + i, g] = t[:, i, :, g * PASS:(g + 1) * PASS]
-            e += n
-        for e in range(e, E):
-            for g in range(G):
-                after, t = land(J * PASS)
-                w1_raw[e, g] = t.rearrange("p (j h) -> p j h", j=J)
-                stream.append((after, w1_raw[e, g], w1[e, :, g * PASS:(g + 1) * PASS].rearrange("(p j) h -> p j h", j=J)))
-        w2_blocks = w2.rearrange("e (g p j) n -> p (e g) j n", p=P, j=J)
+                tenant[places[i]] = e + i
+                w1_raw.append(t[:, i])
+        w2_slabs = w2.rearrange("e (g p j) n -> p (e g) j n", p=P, j=J)
         w2_raw = []
-        block = 0
+        slab = 0
         for shares in W2_LOADS:
             n = sum(shares)
-            if block + n == E * G:
-                t = y_all[:, 2 * C:2 * C + n * OPERAND]
+            if slab + n < E * G:
+                t, places = land(n * OPERAND)
             else:
-                after, t = land(n * OPERAND)
-            t = t.rearrange("p (b j n) -> p b j n", j=J, n=N)
-            stream.append((after, t, w2_blocks[:, block:block + n]))
+                t = y_all[:, (E - 1) * C - n * OPERAND:(E - 1) * C]
+            t = t.rearrange("p (s j n) -> p s j n", j=J, n=N)
+            stream.append((max(tenant[i] for i in places), t, w2_slabs[:, slab:slab + n]))
             w2_raw.append(t)
-            block += n
+            slab += n
         gate_t = keep.tile([P, 2, T], F32, name="gate_t", tag="first_last", align_bytes=256)
-        stream.append((after, gate_t[:], gate.rearrange("r p t -> p r t")))
+        for dst, src in ((pos1_t[:], pos1), (pos2_t[:], pos2), (gate_t[:], gate.rearrange("r p t -> p r t"))):
+            stream.append((-1, dst, src))
         issue(-1)
 
         x_codes = keep.tile([P, T], U32, name="x_codes", align_bytes=64)
@@ -144,19 +129,15 @@ def tile_routed_moe_kernel(tc, xT, w1, w2, gate, offs, pos1, pos2, out):
                 nc.vector.quantize_mx(out=codes[:, words].bitcast(FP8X4), scales=scales[:, words], in_=values[:, at:at + width])
                 at += width
 
-        late_hidden = [(e, g) for e in range(E) for g in range(G)][-LATE_HIDDEN:]
+        late_hidden = [(e, g) for e in (E - 2, E - 1) for g in range(G)]
         hidden_of = [[key for key in ((b - 2, 0), (b - 3, 1)) if key[0] >= 0 and key not in late_hidden] for b in range(E + 1)]
         weights_of = [[(e, g) for e, g in ((b - 1, 1), (b, 0)) if 0 <= e < E] for b in range(E + 1)]
         w1_batch = {}
-        ends = []
-        block = 0
-        for shares in W2_LOADS:
-            ends.append(block + shares[0])
-            block += sum(shares)
-        ends = [z for z in ends if z > 0] + [E * G]
+        starts = [sum(sum(shares) for shares in W2_LOADS[:i]) for i in range(len(W2_LOADS))]
+        ends = [at + shares[0] for at, shares in zip(starts[1:], W2_LOADS[1:])] + [E * G - 1, E * G]
         w2_batches = [range(a, z) for a, z in zip([0] + ends[:-1], ends)]
-        late_blocks = len(w2_batches[LATE_BATCH])
-        late = keep.tile([P, (late_blocks + len(late_hidden)) * OPERAND], BF16, name="late", align_bytes=64)
+        late_slabs = len(w2_batches[LATE_BATCH])
+        late = keep.tile([P, (late_slabs + len(late_hidden)) * OPERAND], BF16, name="late", align_bytes=64)
 
         def w1_batch_tile(b):
             if b not in w1_batch:
@@ -167,32 +148,31 @@ def tile_routed_moe_kernel(tc, xT, w1, w2, gate, offs, pos1, pos2, out):
             b = e + g
             at = len(hidden_of[b]) * OPERAND + weights_of[b].index((e, g)) * HALF
             dst = w1_batch_tile(b)[:, at:at + HALF].rearrange("p (t m u j) -> p m u t j", t=J, u=2, j=2)
-            src = w1_raw[e, g].rearrange("p (u j) (m t) -> p m u t j", t=J, j=2)
+            src = w1_raw[e][:, :, g * PASS:(g + 1) * PASS].rearrange("p (u j) (m t) -> p m u t j", t=J, j=2)
             return dst, src
 
         def hidden_view(e, g):
             if (e, g) in late_hidden:
-                at = (late_blocks + late_hidden.index((e, g))) * OPERAND
+                at = (late_slabs + late_hidden.index((e, g))) * OPERAND
                 host = late
             else:
                 at = hidden_of[e + 2 + g].index((e, g)) * OPERAND
                 host = w1_batch_tile(e + 2 + g)
             return host[:, at:at + OPERAND].rearrange("p (n j) -> p n j", j=J)
 
-        code_words = (E // 2) * G * C + G * HALF // J
+        code_words = (E // 2 - 1) * G * C + G * HALF // J
         w1_codes = [keep.tile([P, code_words], U32, name="w1_codes%d" % i, align_bytes=64) for i in range(2)]
         w1_scales = [keep.tile([P, code_words], U8, name="w1_scales%d" % i, align_bytes=64) for i in range(2)]
         kept = [0, 0]
         h_q = {}
         for b in range(E + 1):
             if b < E:
-                for g in range(G):
-                    m = min(128, max(0, W1_SHARE[b] - 128 * g))
-                    dst, src = weights_view(b, g)
-                    if m > 0:
-                        nc.vector.tensor_copy(out=dst[:, 0:m], in_=src[:, 0:m])
-                    if m < 128:
-                        nc.scalar.copy(out=dst[:, m:128], in_=src[:, m:128])
+                m = W1_VECTOR_COLS
+                dst, src = weights_view(b, 0)
+                nc.vector.tensor_copy(out=dst, in_=src)
+                dst, src = weights_view(b, 1)
+                nc.vector.tensor_copy(out=dst[:, 0:m], in_=src[:, 0:m])
+                nc.scalar.copy(out=dst[:, m:128], in_=src[:, m:128])
                 issue(b)
             t = w1_batch_tile(b)
             words = slice(kept[b % 2], kept[b % 2] + t.shape[1] // J)
@@ -213,53 +193,53 @@ def tile_routed_moe_kernel(tc, xT, w1, w2, gate, offs, pos1, pos2, out):
 
         w2_batch = {LATE_BATCH: late}
 
-        def group_w2(load, first, n, block, copy):
-            b = [i for i, blocks in enumerate(w2_batches) if block in blocks][0]
+        def group_w2(load, first, n, copy):
+            slab = starts[load] + first
+            b = [i for i, slabs in enumerate(w2_batches) if slab in slabs][0]
             if b not in w2_batch:
                 w2_batch[b] = grouped_tile([P, len(w2_batches[b]) * OPERAND], BF16)
-            at = (block - w2_batches[b].start) * OPERAND
-            copy(out=w2_batch[b][:, at:at + n * OPERAND].rearrange("p (b c i j) -> p b c j i", b=n, i=2, j=J),
-                 in_=w2_raw[load][:, first:first + n].rearrange("p b j (c i) -> p b c j i", i=2))
+            at = (slab - w2_batches[b].start) * OPERAND
+            copy(out=w2_batch[b][:, at:at + n * OPERAND].rearrange("p (s c i j) -> p s c j i", s=n, i=2, j=J),
+                 in_=w2_raw[load][:, first:first + n].rearrange("p s j (c i) -> p s c j i", i=2))
+
+        w2_words = E * G * N + len(late_hidden) * C
+        w2_codes = keep.tile([P, w2_words], U32, name="w2_codes", align_bytes=64)
+        w2_scales = keep.tile([P, w2_words], U8, name="w2_scales", align_bytes=64)
+
+        def words_at(slab):
+            return slab * N + (len(late_hidden) * C if slab >= w2_batches[LATE_BATCH].stop else 0)
 
         y_bank = {}
         load = 0
-        block = 0
-        for b, blocks in enumerate(w2_batches):
-            while load < len(W2_LOADS) and block < blocks.stop:
+        for b, slabs in enumerate(w2_batches):
+            while load < len(W2_LOADS) and starts[load] < slabs.stop:
                 first = 0
                 for n, copy in zip(W2_LOADS[load], (nc.vector.tensor_copy, nc.vector.tensor_copy, nc.scalar.copy)):
                     if n > 1:
-                        group_w2(load, first, n - n % 2, block, copy)
+                        group_w2(load, first, n - n % 2, copy)
                     if n % 2:
-                        group_w2(load, first + n - 1, 1, block + n - 1, copy)
+                        group_w2(load, first + n - 1, 1, copy)
                     first += n
-                    block += n
                 load += 1
             t = w2_batch[b]
-            words = t.shape[1] // J
+            words = slice(words_at(slabs.start), words_at(slabs.start) + t.shape[1] // J)
+            quantise(t[:], w2_codes[:, words], w2_scales[:, words])
             if b == LATE_BATCH:
-                codes = keep.tile([P, words], U32, name="late_codes", align_bytes=64)
-                scales = keep.tile([P, words], U8, name="late_scales", align_bytes=64)
                 for i, key in enumerate(late_hidden):
-                    s = slice((late_blocks + i) * C, (late_blocks + i + 1) * C)
-                    h_q[key] = (codes[:, s], scales[:, s])
-            else:
-                codes = ring.tile([P, words], U32, name="codes", tag="codes", bufs=3, align_bytes=64)
-                scales = ring.tile([P, words], U8, name="scales", tag="scales", bufs=3, align_bytes=64)
-            quantise(t[:], codes[:], scales[:])
-            for i, number in enumerate(blocks):
-                e, g = divmod(number, G)
-                bank = [q for q, (a, z) in enumerate(Y_BANKS) if a <= e < z][0]
+                    s = slice(words.start + late_slabs * N + i * C, words.start + late_slabs * N + (i + 1) * C)
+                    h_q[key] = (w2_codes[:, s], w2_scales[:, s])
+            for slab in slabs:
+                e, g = divmod(slab, G)
+                bank = [i for i, (a, z) in enumerate(Y_BANKS) if a <= e < z][0]
                 a, z = Y_BANKS[bank]
                 if bank not in y_bank:
-                    tag = "acc_y" if bank < 4 else "acc"
-                    y_bank[bank] = psum.tile([N, z - a, C], F32, name="acc_y", tag=tag, bufs=4)
+                    y_bank[bank] = psum.tile([N, z - a, C], F32, name="acc_y", tag="acc_y", bufs=len(Y_BANKS))
                 hc, hs = h_q[e, g]
-                w = slice(i * N, (i + 1) * N)
-                nc.tensor.matmul_mx(out=y_bank[bank][:, e - a, :], lhsT=codes[:, w].bitcast(FP8X4), lhsT_scale=scales[:, w],
+                w = slice(words_at(slab), words_at(slab) + N)
+                nc.tensor.matmul_mx(out=y_bank[bank][:, e - a, :], lhsT=w2_codes[:, w].bitcast(FP8X4), lhsT_scale=w2_scales[:, w],
                                     rhs=hc.bitcast(FP8X4), rhs_scale=hs, start=(g == 0), stop=(g == G - 1))
         for bank, (a, z) in enumerate(Y_BANKS):
-            copy = nc.vector.tensor_copy if bank in (1, 4) else nc.scalar.copy
+            copy = nc.vector.tensor_copy if bank % 2 else nc.scalar.copy
             copy(out=y_all[:, a * C:z * C], in_=y_bank[bank][:].rearrange("p e n -> p (e n)"))
 
         chunks = []

@@ -26,11 +26,12 @@ WIDEST = 4096
 
 X_SPLIT = 512
 GATHER = 512
-W1_VECTOR_COLS = 32
 W1_LOADS = (3, 2, 2, 1, 1, 1, 1, 1)
 PLACES = 7
 PLACE = J * H
 GROUPED_BUFS = 4
+LED_BUFS = 3
+CODE_BUFS = 3
 W2_LOADS = ((0, 0, 2), (3, 1, 2), (1, 1, 2), (1, 1, 2), (1, 1, 1), (1, 1, 1), (0, 1, 1))
 LATE_BATCH = 1
 Y_BANKS = ((0, 4), (4, 8), (8, 11), (11, 12))
@@ -129,85 +130,102 @@ def tile_routed_moe_kernel(tc, xT, w1, w2, gate, offs, pos1, pos2, out):
                 nc.vector.quantize_mx(out=codes[:, words].bitcast(FP8X4), scales=scales[:, words], in_=values[:, at:at + width])
                 at += width
 
-        late_hidden = [(e, g) for e in (E - 2, E - 1) for g in range(G)]
-        hidden_of = [[key for key in ((b - 2, 0), (b - 3, 1)) if key[0] >= 0 and key not in late_hidden] for b in range(E + 1)]
-        weights_of = [[(e, g) for e, g in ((b - 1, 1), (b, 0)) if 0 <= e < E] for b in range(E + 1)]
-        w1_batch = {}
+        whole = [sum(W1_LOADS[:i]) for i, n in enumerate(W1_LOADS) if n > 1]
+        steps = []
+        for b in range(E + 1):
+            new = [(b, G if b in whole else 1)] if b < E else []
+            old = [(b - 1, 0)] if b > 0 and b - 1 not in whole else []
+            if b >= 4 and b % 2 == 0:
+                steps.append([(None, old), (b // 2 - 2, new)] if old and new else [(b // 2 - 2, old + new)])
+            elif b in whole:
+                steps.append([(None, old), (None, new)] if old else [(None, new)])
+            else:
+                steps.append([(None, old + new)])
+        home = {}
+        for b, batches in enumerate(steps):
+            for i, (pair, shares) in enumerate(batches):
+                at = 0 if pair is None else HALF
+                for share in shares:
+                    home[share] = (b, i, at)
+                    at += max(share[1], 1) * HALF
+        led = {}
+        plain = {}
+
+        def led_tile(pair):
+            if pair not in led:
+                led[pair] = ring.tile([P, WIDEST], BF16, name="led", tag="led", bufs=LED_BUFS, align_bytes=64)
+            return led[pair]
+
+        def batch_tile(b, i):
+            pair, shares = steps[b][i]
+            if pair is not None:
+                return led_tile(pair)
+            if (b, i) not in plain:
+                plain[b, i] = grouped_tile([P, sum(max(n, 1) for e, n in shares) * HALF], BF16)
+            return plain[b, i]
+
+        def copy_w1(share, copy):
+            e, n = share
+            b, i, at = home[share]
+            first = 0 if n else PASS
+            n = max(n, 1)
+            copy(out=batch_tile(b, i)[:, at:at + n * HALF].rearrange("p (t m u j) -> p m u t j", t=J, u=2, j=2),
+                 in_=w1_raw[e][:, :, first:first + n * PASS].rearrange("p (u j) (m t) -> p m u t j", t=J, j=2))
+
+        kept = HALF // J
+        led_codes = keep.tile([P, (E // 2 + 1) * kept], U32, name="led_codes", align_bytes=64)
+        led_scales = keep.tile([P, (E // 2 + 1) * kept], U8, name="led_scales", align_bytes=64)
+        h_q = {}
+
+        def quantise_batch(values, pair):
+            words = values.shape[1] // J
+            if pair is None:
+                codes = ring.tile([P, words], U32, name="codes", tag="codes", bufs=CODE_BUFS, align_bytes=64)
+                scales = ring.tile([P, words], U8, name="scales", tag="scales", bufs=CODE_BUFS, align_bytes=64)
+                codes, scales = codes[:], scales[:]
+            else:
+                codes, scales = led_codes[:, pair * kept:pair * kept + words], led_scales[:, pair * kept:pair * kept + words]
+                for i in range(2 * G):
+                    h_q[2 * pair + i // G, i % G] = (codes[:, i * C:(i + 1) * C], scales[:, i * C:(i + 1) * C])
+            quantise(values, codes, scales)
+            return codes, scales
+
+        for b in range(E + 1):
+            if b < E:
+                copy_w1((b, G if b in whole else 1), nc.vector.tensor_copy)
+                if b not in whole:
+                    copy_w1((b, 0), nc.scalar.copy)
+                issue(b)
+            for i, (pair, shares) in enumerate(steps[b]):
+                codes, scales = quantise_batch(batch_tile(b, i)[:], pair)
+                for share in shares:
+                    e, n = share
+                    xc, xs = slot_q[e]
+                    for r in range(max(n, 1)):
+                        g = r if n else 1
+                        acc = psum.tile([P, J, C], F32, name="acc", tag="acc", bufs=2 * G)
+                        for q in range(J):
+                            at = home[share][2] // J + (q * max(n, 1) + r) * 128
+                            s = slice(at, at + 128)
+                            nc.tensor.matmul_mx(out=acc[:, q, :], lhsT=codes[:, s].bitcast(FP8X4), lhsT_scale=scales[:, s],
+                                                rhs=xc.bitcast(FP8X4), rhs_scale=xs, start=True, stop=True)
+                        at = (G * (e % 2) + g) * OPERAND
+                        nc.scalar.activation(led_tile(e // 2)[:, at:at + OPERAND].rearrange("p (n j) -> p n j", j=J),
+                                             acc[:].rearrange("p t n -> p n t"), SILU)
+
         starts = [sum(sum(shares) for shares in W2_LOADS[:i]) for i in range(len(W2_LOADS))]
         ends = [at + shares[0] for at, shares in zip(starts[1:], W2_LOADS[1:])] + [E * G - 1, E * G]
         w2_batches = [range(a, z) for a, z in zip([0] + ends[:-1], ends)]
-        late_slabs = len(w2_batches[LATE_BATCH])
-        late = keep.tile([P, (late_slabs + len(late_hidden)) * OPERAND], BF16, name="late", align_bytes=64)
-
-        def w1_batch_tile(b):
-            if b not in w1_batch:
-                w1_batch[b] = grouped_tile([P, len(hidden_of[b]) * OPERAND + len(weights_of[b]) * HALF], BF16)
-            return w1_batch[b]
-
-        def weights_view(e, g):
-            b = e + g
-            at = len(hidden_of[b]) * OPERAND + weights_of[b].index((e, g)) * HALF
-            dst = w1_batch_tile(b)[:, at:at + HALF].rearrange("p (t m u j) -> p m u t j", t=J, u=2, j=2)
-            src = w1_raw[e][:, :, g * PASS:(g + 1) * PASS].rearrange("p (u j) (m t) -> p m u t j", t=J, j=2)
-            return dst, src
-
-        def hidden_view(e, g):
-            if (e, g) in late_hidden:
-                at = (late_slabs + late_hidden.index((e, g))) * OPERAND
-                host = late
-            else:
-                at = hidden_of[e + 2 + g].index((e, g)) * OPERAND
-                host = w1_batch_tile(e + 2 + g)
-            return host[:, at:at + OPERAND].rearrange("p (n j) -> p n j", j=J)
-
-        code_words = (E // 2 - 1) * G * C + G * HALF // J
-        w1_codes = [keep.tile([P, code_words], U32, name="w1_codes%d" % i, align_bytes=64) for i in range(2)]
-        w1_scales = [keep.tile([P, code_words], U8, name="w1_scales%d" % i, align_bytes=64) for i in range(2)]
-        kept = [0, 0]
-        h_q = {}
-        for b in range(E + 1):
-            if b < E:
-                m = W1_VECTOR_COLS
-                dst, src = weights_view(b, 0)
-                nc.vector.tensor_copy(out=dst, in_=src)
-                dst, src = weights_view(b, 1)
-                nc.vector.tensor_copy(out=dst[:, 0:m], in_=src[:, 0:m])
-                nc.scalar.copy(out=dst[:, m:128], in_=src[:, m:128])
-                issue(b)
-            t = w1_batch_tile(b)
-            words = slice(kept[b % 2], kept[b % 2] + t.shape[1] // J)
-            codes, scales = w1_codes[b % 2][:, words], w1_scales[b % 2][:, words]
-            quantise(t[:], codes, scales)
-            for i, key in enumerate(hidden_of[b]):
-                h_q[key] = (codes[:, i * C:(i + 1) * C], scales[:, i * C:(i + 1) * C])
-            kept[b % 2] += len(hidden_of[b]) * C
-            for i, (e, g) in enumerate(weights_of[b]):
-                xc, xs = slot_q[e]
-                acc = psum.tile([P, J, C], F32, name="acc", tag="acc", bufs=2 * G)
-                for q in range(J):
-                    at = len(hidden_of[b]) * C + (J * i + q) * 128
-                    s = slice(at, at + 128)
-                    nc.tensor.matmul_mx(out=acc[:, q, :], lhsT=codes[:, s].bitcast(FP8X4), lhsT_scale=scales[:, s],
-                                        rhs=xc.bitcast(FP8X4), rhs_scale=xs, start=True, stop=True)
-                nc.scalar.activation(hidden_view(e, g), acc[:].rearrange("p t n -> p n t"), SILU)
-
-        w2_batch = {LATE_BATCH: late}
+        w2_batch = {LATE_BATCH: led_tile(E // 2 - 1)}
 
         def group_w2(load, first, n, copy):
             slab = starts[load] + first
             b = [i for i, slabs in enumerate(w2_batches) if slab in slabs][0]
             if b not in w2_batch:
                 w2_batch[b] = grouped_tile([P, len(w2_batches[b]) * OPERAND], BF16)
-            at = (slab - w2_batches[b].start) * OPERAND
+            at = (slab - w2_batches[b].start) * OPERAND + (HALF if b == LATE_BATCH else 0)
             copy(out=w2_batch[b][:, at:at + n * OPERAND].rearrange("p (s c i j) -> p s c j i", s=n, i=2, j=J),
                  in_=w2_raw[load][:, first:first + n].rearrange("p s j (c i) -> p s c j i", i=2))
-
-        w2_words = E * G * N + len(late_hidden) * C
-        w2_codes = keep.tile([P, w2_words], U32, name="w2_codes", align_bytes=64)
-        w2_scales = keep.tile([P, w2_words], U8, name="w2_scales", align_bytes=64)
-
-        def words_at(slab):
-            return slab * N + (len(late_hidden) * C if slab >= w2_batches[LATE_BATCH].stop else 0)
 
         y_bank = {}
         load = 0
@@ -221,13 +239,7 @@ def tile_routed_moe_kernel(tc, xT, w1, w2, gate, offs, pos1, pos2, out):
                         group_w2(load, first + n - 1, 1, copy)
                     first += n
                 load += 1
-            t = w2_batch[b]
-            words = slice(words_at(slabs.start), words_at(slabs.start) + t.shape[1] // J)
-            quantise(t[:], w2_codes[:, words], w2_scales[:, words])
-            if b == LATE_BATCH:
-                for i, key in enumerate(late_hidden):
-                    s = slice(words.start + late_slabs * N + i * C, words.start + late_slabs * N + (i + 1) * C)
-                    h_q[key] = (w2_codes[:, s], w2_scales[:, s])
+            codes, scales = quantise_batch(w2_batch[b][:], E // 2 - 1 if b == LATE_BATCH else None)
             for slab in slabs:
                 e, g = divmod(slab, G)
                 bank = [i for i, (a, z) in enumerate(Y_BANKS) if a <= e < z][0]
@@ -235,8 +247,9 @@ def tile_routed_moe_kernel(tc, xT, w1, w2, gate, offs, pos1, pos2, out):
                 if bank not in y_bank:
                     y_bank[bank] = psum.tile([N, z - a, C], F32, name="acc_y", tag="acc_y", bufs=len(Y_BANKS))
                 hc, hs = h_q[e, g]
-                w = slice(words_at(slab), words_at(slab) + N)
-                nc.tensor.matmul_mx(out=y_bank[bank][:, e - a, :], lhsT=w2_codes[:, w].bitcast(FP8X4), lhsT_scale=w2_scales[:, w],
+                at = (slab - slabs.start) * N + (kept if b == LATE_BATCH else 0)
+                w = slice(at, at + N)
+                nc.tensor.matmul_mx(out=y_bank[bank][:, e - a, :], lhsT=codes[:, w].bitcast(FP8X4), lhsT_scale=scales[:, w],
                                     rhs=hc.bitcast(FP8X4), rhs_scale=hs, start=(g == 0), stop=(g == G - 1))
         for bank, (a, z) in enumerate(Y_BANKS):
             copy = nc.vector.tensor_copy if bank % 2 else nc.scalar.copy

@@ -26,16 +26,19 @@ WIDEST = 4096
 
 X_SPLIT = 512
 GATHER = 512
-W1_LOADS = (3, 2, 2, 1, 1, 1, 1, 1)
+W1_LOADS = (1,) * E
 PLACES = 7
 PLACE = J * H
 GROUPED_BUFS = 4
 LED_BUFS = 3
 CODE_BUFS = 3
-W2_LOADS = ((0, 0, 2), (3, 1, 2), (1, 1, 2), (1, 1, 2), (1, 1, 1), (1, 1, 1), (0, 1, 1))
+W2_LOADS = ((0, 0, 2), (3, 2, 1), (1, 1, 2), (1, 1, 1), (0, 0, 1), (1, 1, 1), (0, 0, 1), (0, 0, 1), (1, 0, 0))
+SHARED = (32, 48)
+W2_BATCH_ENDS = (5, 9, 13, 17, 20, 22, 23, 24)
 LATE_BATCH = 1
 Y_BANKS = ((0, 4), (4, 8), (8, 11), (11, 12))
-OUT_CHUNKS = (512, 256)
+EARLY_SLAB = 15
+OUT_CHUNKS = (384, 384)
 
 
 def tile_routed_moe_kernel(tc, xT, w1, w2, gate, offs, pos1, pos2, out):
@@ -83,18 +86,19 @@ def tile_routed_moe_kernel(tc, xT, w1, w2, gate, offs, pos1, pos2, out):
         w2_slabs = w2.rearrange("e (g p j) n -> p (e g) j n", p=P, j=J)
         w2_raw = []
         slab = 0
-        for shares in W2_LOADS:
-            n = sum(shares)
-            if slab + n < E * G:
+        for n in [sum(shares) for shares in W2_LOADS] + [1] * len(SHARED):
+            if slab == EARLY_SLAB:
+                t = y_all[:, 0:OPERAND]
+            elif slab + n < E * G:
                 t, places = land(n * OPERAND)
             else:
-                t = y_all[:, (E - 1) * C - n * OPERAND:(E - 1) * C]
+                t = y_all[:, Y_BANKS[2][0] * C - OPERAND // 2:Y_BANKS[2][0] * C + OPERAND // 2]
             t = t.rearrange("p (s j n) -> p s j n", j=J, n=N)
             stream.append((max(tenant[i] for i in places), t, w2_slabs[:, slab:slab + n]))
             w2_raw.append(t)
             slab += n
         gate_t = keep.tile([P, 2, T], F32, name="gate_t", tag="first_last", align_bytes=256)
-        for dst, src in ((pos1_t[:], pos1), (pos2_t[:], pos2), (gate_t[:], gate.rearrange("r p t -> p r t"))):
+        for dst, src in ((pos1_t[:], pos1), (gate_t[:, 0], gate[0]), (pos2_t[:], pos2), (gate_t[:, 1], gate[1])):
             stream.append((-1, dst, src))
         issue(-1)
 
@@ -213,19 +217,19 @@ def tile_routed_moe_kernel(tc, xT, w1, w2, gate, offs, pos1, pos2, out):
                         nc.scalar.activation(led_tile(e // 2)[:, at:at + OPERAND].rearrange("p (n j) -> p n j", j=J),
                                              acc[:].rearrange("p t n -> p n t"), SILU)
 
-        starts = [sum(sum(shares) for shares in W2_LOADS[:i]) for i in range(len(W2_LOADS))]
-        ends = [at + shares[0] for at, shares in zip(starts[1:], W2_LOADS[1:])] + [E * G - 1, E * G]
+        starts = [sum(sum(shares) for shares in W2_LOADS[:i]) for i in range(len(W2_LOADS))] + [E * G - 2, E * G - 1]
+        ends = list(W2_BATCH_ENDS)
         w2_batches = [range(a, z) for a, z in zip([0] + ends[:-1], ends)]
         w2_batch = {LATE_BATCH: led_tile(E // 2 - 1)}
 
-        def group_w2(load, first, n, copy):
+        def group_w2(load, first, n, copy, pairs=slice(0, N // 2)):
             slab = starts[load] + first
             b = [i for i, slabs in enumerate(w2_batches) if slab in slabs][0]
             if b not in w2_batch:
                 w2_batch[b] = grouped_tile([P, len(w2_batches[b]) * OPERAND], BF16)
             at = (slab - w2_batches[b].start) * OPERAND + (HALF if b == LATE_BATCH else 0)
-            copy(out=w2_batch[b][:, at:at + n * OPERAND].rearrange("p (s c i j) -> p s c j i", s=n, i=2, j=J),
-                 in_=w2_raw[load][:, first:first + n].rearrange("p s j (c i) -> p s c j i", i=2))
+            copy(out=w2_batch[b][:, at:at + n * OPERAND].rearrange("p (s c i j) -> p s c j i", s=n, i=2, j=J)[:, :, pairs],
+                 in_=w2_raw[load][:, first:first + n].rearrange("p s j (c i) -> p s c j i", i=2)[:, :, pairs])
 
         y_bank = {}
         load = 0
@@ -238,6 +242,11 @@ def tile_routed_moe_kernel(tc, xT, w1, w2, gate, offs, pos1, pos2, out):
                     if n % 2:
                         group_w2(load, first + n - 1, 1, copy)
                     first += n
+                load += 1
+            if slabs.start >= E * G - len(SHARED):
+                columns = SHARED[load - len(W2_LOADS)]
+                group_w2(load, 0, 1, nc.vector.tensor_copy, slice(0, columns // 2))
+                group_w2(load, 0, 1, nc.scalar.copy, slice(columns // 2, N // 2))
                 load += 1
             codes, scales = quantise_batch(w2_batch[b][:], E // 2 - 1 if b == LATE_BATCH else None)
             for slab in slabs:
@@ -252,28 +261,16 @@ def tile_routed_moe_kernel(tc, xT, w1, w2, gate, offs, pos1, pos2, out):
                 nc.tensor.matmul_mx(out=y_bank[bank][:, e - a, :], lhsT=codes[:, w].bitcast(FP8X4), lhsT_scale=scales[:, w],
                                     rhs=hc.bitcast(FP8X4), rhs_scale=hs, start=(g == 0), stop=(g == G - 1))
         for bank, (a, z) in enumerate(Y_BANKS):
-            copy = nc.vector.tensor_copy if bank % 2 else nc.scalar.copy
+            copy = nc.vector.tensor_copy if bank == 1 else nc.scalar.copy
             copy(out=y_all[:, a * C:z * C], in_=y_bank[bank][:].rearrange("p e n -> p (e n)"))
 
-        chunks = []
-        at = 0
-        for n in OUT_CHUNKS:
-            terms = (grouped_tile([P, n], F32), grouped_tile([P, n], F32))
-            chunks.append((slice(at, at + n), slice(at // LIST_ROWS, (at + n) // LIST_ROWS), terms))
-            at += n
-
-        def fetch(chunk, r):
-            tokens, columns, terms = chunks[chunk]
-            nc.vector.tensor_tensor(terms[r][:], y_all[:].indirect((pos1_t, pos2_t)[r][:, columns]), gate_t[:, r, tokens], MULT)
-
-        def finish(chunk):
-            tokens, columns, terms = chunks[chunk]
-            nc.vector.tensor_tensor(terms[0][:], terms[0][:], terms[1][:], ADD)
-            nc.sync.dma_start(out=out[:, tokens], in_=terms[0][:])
-
-        fetch(0, 0)
-        fetch(0, 1)
-        fetch(1, 0)
-        finish(0)
-        fetch(1, 1)
-        finish(1)
+        first = grouped_tile([P, T], F32)
+        second = grouped_tile([P, T], F32)
+        nc.vector.tensor_tensor(first[:], y_all[:].indirect(pos1_t[:]), gate_t[:, 0, :], MULT)
+        chunks = [slice(sum(OUT_CHUNKS[:i]), sum(OUT_CHUNKS[:i + 1])) for i in range(len(OUT_CHUNKS))]
+        for tokens in chunks:
+            columns = slice(tokens.start // LIST_ROWS, tokens.stop // LIST_ROWS)
+            nc.vector.tensor_tensor(second[:, tokens], y_all[:].indirect(pos2_t[:, columns]), gate_t[:, 1, tokens], MULT)
+        for tokens in chunks:
+            nc.vector.tensor_tensor(first[:, tokens], first[:, tokens], second[:, tokens], ADD)
+            nc.sync.dma_start(out=out[:, tokens], in_=first[:, tokens])

@@ -26,27 +26,29 @@ WIDEST = 4096
 
 X_SPLIT = 512
 GATHER = 512
-W1_LOADS = (1,) * E
 PLACES = 7
 PLACE = J * H
+PAIRS = E // 2
+PAIR_LAG = 2
 GROUPED_BUFS = 4
 LED_BUFS = 3
 CODE_BUFS = 3
-W2_LOADS = ((0, 0, 2), (3, 2, 1), (1, 1, 2), (1, 1, 1), (0, 0, 1), (1, 1, 1), (0, 0, 1), (0, 0, 1), (1, 0, 0))
-SHARED = (32, 48)
-W2_BATCH_ENDS = (5, 9, 13, 17, 20, 22, 23, 24)
+
+W2_BATCHES = (("SS", "VV", "V"), ("VV", "S", "V"), ("V", "SS", "V"), ("V", "S", "S", "V"), ("V", "S", "S"), ("S", "V"))
+SHARED_COLUMNS = (32, 48)
 LATE_BATCH = 1
 Y_BANKS = ((0, 4), (4, 8), (8, 11), (11, 12))
 EARLY_SLAB = 15
-OUT_CHUNKS = (384, 384)
+OUT_CHUNK = T // 2
 
 
 def tile_routed_moe_kernel(tc, xT, w1, w2, gate, offs, pos1, pos2, out):
     nc = tc.nc
+    copier = {"V": nc.vector.tensor_copy, "S": nc.scalar.copy}
     with ExitStack() as ctx:
         keep = ctx.enter_context(tc.tile_pool(name="keep", bufs=1))
-        ring = ctx.enter_context(tc.tile_pool(name="ring", bufs=2))
-        psum = ctx.enter_context(tc.psum_pool(name="psum", bufs=2))
+        ring = ctx.enter_context(tc.tile_pool(name="ring", bufs=1))
+        psum = ctx.enter_context(tc.psum_pool(name="psum", bufs=1))
 
         offs_t = keep.tile([P, E * C // LIST_ROWS], U16, name="offs_t")
         pos1_t = keep.tile([P, T // LIST_ROWS], U16, name="pos1_t")
@@ -75,27 +77,26 @@ def tile_routed_moe_kernel(tc, xT, w1, w2, gate, offs, pos1, pos2, out):
         nc.sync.dma_start(out=x_raw[:], in_=xT.rearrange("(p j) n -> p j n", j=J))
         nc.sync.dma_start(out=offs_t[:], in_=offs)
         w1_raw = []
-        for n in W1_LOADS:
-            t, places = land(n * PLACE)
-            t = t.rearrange("p (e j h) -> p e j h", j=J, h=H)
-            e = len(w1_raw)
-            stream.append((max(tenant[i] for i in places), t, w1[e:e + n].rearrange("e (p j) h -> p e j h", j=J)))
-            for i in range(n):
-                tenant[places[i]] = e + i
-                w1_raw.append(t[:, i])
+        for e in range(E):
+            t, places = land(PLACE)
+            t = t.rearrange("p (j h) -> p j h", j=J)
+            stream.append((tenant[places[0]], t, w1[e].rearrange("(p j) h -> p j h", j=J)))
+            tenant[places[0]] = e
+            w1_raw.append(t)
         w2_slabs = w2.rearrange("e (g p j) n -> p (e g) j n", p=P, j=J)
-        w2_raw = []
+        w2_raw = {}
         slab = 0
-        for n in [sum(shares) for shares in W2_LOADS] + [1] * len(SHARED):
+        for n in [len(load) for batch in W2_BATCHES for load in batch] + [1] * len(SHARED_COLUMNS):
             if slab == EARLY_SLAB:
-                t = y_all[:, 0:OPERAND]
-            elif slab + n < E * G:
-                t, places = land(n * OPERAND)
+                t, freed_by = y_all[:, 0:OPERAND], -1
+            elif slab == E * G - 1:
+                border = Y_BANKS[2][0] * C
+                t, freed_by = y_all[:, border - OPERAND // 2:border + OPERAND // 2], -1
             else:
-                t = y_all[:, Y_BANKS[2][0] * C - OPERAND // 2:Y_BANKS[2][0] * C + OPERAND // 2]
-            t = t.rearrange("p (s j n) -> p s j n", j=J, n=N)
-            stream.append((max(tenant[i] for i in places), t, w2_slabs[:, slab:slab + n]))
-            w2_raw.append(t)
+                t, places = land(n * OPERAND)
+                freed_by = max(tenant[i] for i in places)
+            w2_raw[slab] = t.rearrange("p (s j n) -> p s j n", j=J, n=N)
+            stream.append((freed_by, w2_raw[slab], w2_slabs[:, slab:slab + n]))
             slab += n
         gate_t = keep.tile([P, 2, T], F32, name="gate_t", tag="first_last", align_bytes=256)
         for dst, src in ((pos1_t[:], pos1), (gate_t[:, 0], gate[0]), (pos2_t[:], pos2), (gate_t[:, 1], gate[1])):
@@ -106,12 +107,13 @@ def tile_routed_moe_kernel(tc, xT, w1, w2, gate, offs, pos1, pos2, out):
         x_scales = keep.tile([P, T], U8, name="x_scales", align_bytes=64)
         nc.gpsimd.memset(x_scales[:], 0)
         x_parts = []
-        for a, b, copy in ((0, X_SPLIT, nc.vector.tensor_copy), (X_SPLIT, T, nc.scalar.copy)):
-            t = grouped_tile([P, b - a, J], BF16)
-            copy(out=t[:].rearrange("p (c i) j -> p c j i", i=2), in_=x_raw[:, :, a:b].rearrange("p j (c i) -> p c j i", i=2))
-            x_parts.append((a, b, t))
-        for a, b, t in x_parts:
-            nc.vector.quantize_mx(out=x_codes[:, a:b].bitcast(FP8X4), scales=x_scales[:, a:b],
+        for a, z, engine in ((0, X_SPLIT, "V"), (X_SPLIT, T, "S")):
+            t = grouped_tile([P, z - a, J], BF16)
+            copier[engine](out=t[:].rearrange("p (c i) j -> p c j i", i=2),
+                           in_=x_raw[:, :, a:z].rearrange("p j (c i) -> p c j i", i=2))
+            x_parts.append((a, z, t))
+        for a, z, t in x_parts:
+            nc.vector.quantize_mx(out=x_codes[:, a:z].bitcast(FP8X4), scales=x_scales[:, a:z],
                                   in_=t[:].rearrange("p n j -> p (n j)"))
         slot_q = {}
         for at in range(0, E * C, GATHER):
@@ -123,8 +125,29 @@ def tile_routed_moe_kernel(tc, xT, w1, w2, gate, offs, pos1, pos2, out):
             for q in range(GATHER // C):
                 slot_q[at // C + q] = (codes[:, q * C:(q + 1) * C], scales[:, q * C:(q + 1) * C])
 
-        def quantise(values, codes, scales):
+        led = {}
+
+        def led_tile(pair):
+            if pair not in led:
+                led[pair] = ring.tile([P, WIDEST], BF16, name="led", tag="led", bufs=LED_BUFS, align_bytes=64)
+            return led[pair]
+
+        kept = HALF // J
+        led_codes = keep.tile([P, (PAIRS + 1) * kept], U32, name="led_codes", align_bytes=64)
+        led_scales = keep.tile([P, (PAIRS + 1) * kept], U8, name="led_scales", align_bytes=64)
+        h_q = {}
+
+        def quantise(values, pair):
             n = values.shape[1]
+            if pair is None:
+                codes = ring.tile([P, n // J], U32, name="codes", tag="codes", bufs=CODE_BUFS, align_bytes=64)
+                scales = ring.tile([P, n // J], U8, name="scales", tag="scales", bufs=CODE_BUFS, align_bytes=64)
+                codes, scales = codes[:], scales[:]
+            else:
+                words = slice(pair * kept, pair * kept + n // J)
+                codes, scales = led_codes[:, words], led_scales[:, words]
+                for i in range(2 * G):
+                    h_q[2 * pair + i // G, i % G] = (codes[:, i * C:(i + 1) * C], scales[:, i * C:(i + 1) * C])
             at = 0
             while at < n:
                 width = WIDEST
@@ -133,144 +156,99 @@ def tile_routed_moe_kernel(tc, xT, w1, w2, gate, offs, pos1, pos2, out):
                 words = slice(at // J, (at + width) // J)
                 nc.vector.quantize_mx(out=codes[:, words].bitcast(FP8X4), scales=scales[:, words], in_=values[:, at:at + width])
                 at += width
+            first = 0 if pair is None else kept
+            return codes[:, first:], scales[:, first:]
 
-        whole = [sum(W1_LOADS[:i]) for i, n in enumerate(W1_LOADS) if n > 1]
         steps = []
         for b in range(E + 1):
-            new = [(b, G if b in whole else 1)] if b < E else []
-            old = [(b - 1, 0)] if b > 0 and b - 1 not in whole else []
-            if b >= 4 and b % 2 == 0:
-                steps.append([(None, old), (b // 2 - 2, new)] if old and new else [(b // 2 - 2, old + new)])
-            elif b in whole:
-                steps.append([(None, old), (None, new)] if old else [(None, new)])
+            halves = [(e, g) for e, g in ((b - 1, 1), (b, 0)) if 0 <= e < E]
+            pair, odd = divmod(b - G - PAIR_LAG, 2)
+            if pair >= 0 and not odd:
+                steps.append([(None, [half]) for half in halves[:-1]] + [(pair, halves[-1:])])
             else:
-                steps.append([(None, old + new)])
+                steps.append([(None, halves)])
         home = {}
         for b, batches in enumerate(steps):
-            for i, (pair, shares) in enumerate(batches):
-                at = 0 if pair is None else HALF
-                for share in shares:
-                    home[share] = (b, i, at)
-                    at += max(share[1], 1) * HALF
-        led = {}
+            for i, (pair, halves) in enumerate(batches):
+                for r, half in enumerate(halves):
+                    home[half] = (b, i, (r if pair is None else r + 1) * HALF)
         plain = {}
 
-        def led_tile(pair):
-            if pair not in led:
-                led[pair] = ring.tile([P, WIDEST], BF16, name="led", tag="led", bufs=LED_BUFS, align_bytes=64)
-            return led[pair]
-
         def batch_tile(b, i):
-            pair, shares = steps[b][i]
+            pair, halves = steps[b][i]
             if pair is not None:
                 return led_tile(pair)
             if (b, i) not in plain:
-                plain[b, i] = grouped_tile([P, sum(max(n, 1) for e, n in shares) * HALF], BF16)
+                plain[b, i] = grouped_tile([P, len(halves) * HALF], BF16)
             return plain[b, i]
-
-        def copy_w1(share, copy):
-            e, n = share
-            b, i, at = home[share]
-            first = 0 if n else PASS
-            n = max(n, 1)
-            copy(out=batch_tile(b, i)[:, at:at + n * HALF].rearrange("p (t m u j) -> p m u t j", t=J, u=2, j=2),
-                 in_=w1_raw[e][:, :, first:first + n * PASS].rearrange("p (u j) (m t) -> p m u t j", t=J, j=2))
-
-        kept = HALF // J
-        led_codes = keep.tile([P, (E // 2 + 1) * kept], U32, name="led_codes", align_bytes=64)
-        led_scales = keep.tile([P, (E // 2 + 1) * kept], U8, name="led_scales", align_bytes=64)
-        h_q = {}
-
-        def quantise_batch(values, pair):
-            words = values.shape[1] // J
-            if pair is None:
-                codes = ring.tile([P, words], U32, name="codes", tag="codes", bufs=CODE_BUFS, align_bytes=64)
-                scales = ring.tile([P, words], U8, name="scales", tag="scales", bufs=CODE_BUFS, align_bytes=64)
-                codes, scales = codes[:], scales[:]
-            else:
-                codes, scales = led_codes[:, pair * kept:pair * kept + words], led_scales[:, pair * kept:pair * kept + words]
-                for i in range(2 * G):
-                    h_q[2 * pair + i // G, i % G] = (codes[:, i * C:(i + 1) * C], scales[:, i * C:(i + 1) * C])
-            quantise(values, codes, scales)
-            return codes, scales
 
         for b in range(E + 1):
             if b < E:
-                copy_w1((b, G if b in whole else 1), nc.vector.tensor_copy)
-                if b not in whole:
-                    copy_w1((b, 0), nc.scalar.copy)
+                for g, engine in enumerate("VS"):
+                    step, i, at = home[b, g]
+                    copier[engine](out=batch_tile(step, i)[:, at:at + HALF].rearrange("p (t m u j) -> p m u t j", t=J, u=2, j=2),
+                                   in_=w1_raw[b][:, :, g * PASS:(g + 1) * PASS].rearrange("p (u j) (m t) -> p m u t j", t=J, j=2))
                 issue(b)
-            for i, (pair, shares) in enumerate(steps[b]):
-                codes, scales = quantise_batch(batch_tile(b, i)[:], pair)
-                for share in shares:
-                    e, n = share
+            for i, (pair, halves) in enumerate(steps[b]):
+                codes, scales = quantise(batch_tile(b, i)[:], pair)
+                for r, (e, g) in enumerate(halves):
                     xc, xs = slot_q[e]
-                    for r in range(max(n, 1)):
-                        g = r if n else 1
-                        acc = psum.tile([P, J, C], F32, name="acc", tag="acc", bufs=2 * G)
-                        for q in range(J):
-                            at = home[share][2] // J + (q * max(n, 1) + r) * 128
-                            s = slice(at, at + 128)
-                            nc.tensor.matmul_mx(out=acc[:, q, :], lhsT=codes[:, s].bitcast(FP8X4), lhsT_scale=scales[:, s],
-                                                rhs=xc.bitcast(FP8X4), rhs_scale=xs, start=True, stop=True)
-                        at = (G * (e % 2) + g) * OPERAND
-                        nc.scalar.activation(led_tile(e // 2)[:, at:at + OPERAND].rearrange("p (n j) -> p n j", j=J),
-                                             acc[:].rearrange("p t n -> p n t"), SILU)
-
-        starts = [sum(sum(shares) for shares in W2_LOADS[:i]) for i in range(len(W2_LOADS))] + [E * G - 2, E * G - 1]
-        ends = list(W2_BATCH_ENDS)
-        w2_batches = [range(a, z) for a, z in zip([0] + ends[:-1], ends)]
-        w2_batch = {LATE_BATCH: led_tile(E // 2 - 1)}
-
-        def group_w2(load, first, n, copy, pairs=slice(0, N // 2)):
-            slab = starts[load] + first
-            b = [i for i, slabs in enumerate(w2_batches) if slab in slabs][0]
-            if b not in w2_batch:
-                w2_batch[b] = grouped_tile([P, len(w2_batches[b]) * OPERAND], BF16)
-            at = (slab - w2_batches[b].start) * OPERAND + (HALF if b == LATE_BATCH else 0)
-            copy(out=w2_batch[b][:, at:at + n * OPERAND].rearrange("p (s c i j) -> p s c j i", s=n, i=2, j=J)[:, :, pairs],
-                 in_=w2_raw[load][:, first:first + n].rearrange("p s j (c i) -> p s c j i", i=2)[:, :, pairs])
+                    acc = psum.tile([P, J, C], F32, name="acc", tag="acc", bufs=2 * G)
+                    for q in range(J):
+                        s = slice((J * r + q) * 128, (J * r + q + 1) * 128)
+                        nc.tensor.matmul_mx(out=acc[:, q, :], lhsT=codes[:, s].bitcast(FP8X4), lhsT_scale=scales[:, s],
+                                            rhs=xc.bitcast(FP8X4), rhs_scale=xs, start=True, stop=True)
+                    at = (G * (e % 2) + g) * OPERAND
+                    nc.scalar.activation(led_tile(e // 2)[:, at:at + OPERAND].rearrange("p (n j) -> p n j", j=J),
+                                         acc[:].rearrange("p t n -> p n t"), SILU)
 
         y_bank = {}
-        load = 0
-        for b, slabs in enumerate(w2_batches):
-            while load < len(W2_LOADS) and starts[load] < slabs.stop:
-                first = 0
-                for n, copy in zip(W2_LOADS[load], (nc.vector.tensor_copy, nc.vector.tensor_copy, nc.scalar.copy)):
-                    if n > 1:
-                        group_w2(load, first, n - n % 2, copy)
-                    if n % 2:
-                        group_w2(load, first + n - 1, 1, copy)
-                    first += n
-                load += 1
-            if slabs.start >= E * G - len(SHARED):
-                columns = SHARED[load - len(W2_LOADS)]
-                group_w2(load, 0, 1, nc.vector.tensor_copy, slice(0, columns // 2))
-                group_w2(load, 0, 1, nc.scalar.copy, slice(columns // 2, N // 2))
-                load += 1
-            codes, scales = quantise_batch(w2_batch[b][:], E // 2 - 1 if b == LATE_BATCH else None)
-            for slab in slabs:
+
+        def group_w2(engine, dst, first, columns):
+            twos = slice(columns.start // 2, columns.stop // 2)
+            copier[engine](out=dst.rearrange("p (s c i j) -> p s c j i", c=N // 2, i=2, j=J)[:, :, twos],
+                           in_=w2_raw[first].rearrange("p s j (c i) -> p s c j i", i=2)[:, :, twos])
+
+        def multiply(slabs, codes, scales):
+            for r, slab in enumerate(slabs):
                 e, g = divmod(slab, G)
                 bank = [i for i, (a, z) in enumerate(Y_BANKS) if a <= e < z][0]
                 a, z = Y_BANKS[bank]
                 if bank not in y_bank:
                     y_bank[bank] = psum.tile([N, z - a, C], F32, name="acc_y", tag="acc_y", bufs=len(Y_BANKS))
                 hc, hs = h_q[e, g]
-                at = (slab - slabs.start) * N + (kept if b == LATE_BATCH else 0)
-                w = slice(at, at + N)
-                nc.tensor.matmul_mx(out=y_bank[bank][:, e - a, :], lhsT=codes[:, w].bitcast(FP8X4), lhsT_scale=scales[:, w],
+                s = slice(r * N, (r + 1) * N)
+                nc.tensor.matmul_mx(out=y_bank[bank][:, e - a, :], lhsT=codes[:, s].bitcast(FP8X4), lhsT_scale=scales[:, s],
                                     rhs=hc.bitcast(FP8X4), rhs_scale=hs, start=(g == 0), stop=(g == G - 1))
-        for bank, (a, z) in enumerate(Y_BANKS):
-            copy = nc.vector.tensor_copy if bank == 1 else nc.scalar.copy
-            copy(out=y_all[:, a * C:z * C], in_=y_bank[bank][:].rearrange("p e n -> p (e n)"))
 
-        first = grouped_tile([P, T], F32)
-        second = grouped_tile([P, T], F32)
-        nc.vector.tensor_tensor(first[:], y_all[:].indirect(pos1_t[:]), gate_t[:, 0, :], MULT)
-        chunks = [slice(sum(OUT_CHUNKS[:i]), sum(OUT_CHUNKS[:i + 1])) for i in range(len(OUT_CHUNKS))]
+        start = 0
+        for b, loads in enumerate(W2_BATCHES):
+            n = sum(len(load) for load in loads)
+            pair = PAIRS - 1 if b == LATE_BATCH else None
+            t = grouped_tile([P, n * OPERAND], BF16) if pair is None else led_tile(pair)
+            at = 0 if pair is None else HALF
+            slab = start
+            for load in loads:
+                group_w2(load[0], t[:, at:at + len(load) * OPERAND], slab, slice(0, N))
+                at += len(load) * OPERAND
+                slab += len(load)
+            multiply(range(start, slab), *quantise(t[:], pair))
+            start = slab
+        for slab, split in enumerate(SHARED_COLUMNS, start):
+            t = grouped_tile([P, OPERAND], BF16)
+            group_w2("V", t[:], slab, slice(0, split))
+            group_w2("S", t[:], slab, slice(split, N))
+            multiply([slab], *quantise(t[:], None))
+        for (a, z), bank, engine in zip(Y_BANKS, range(len(Y_BANKS)), "SVSS"):
+            copier[engine](out=y_all[:, a * C:z * C], in_=y_bank[bank][:].rearrange("p e n -> p (e n)"))
+
+        term1 = grouped_tile([P, T], F32)
+        term2 = grouped_tile([P, T], F32)
+        nc.vector.tensor_tensor(term1[:], y_all[:].indirect(pos1_t[:]), gate_t[:, 0, :], MULT)
+        chunks = [slice(at, at + OUT_CHUNK) for at in range(0, T, OUT_CHUNK)]
         for tokens in chunks:
-            columns = slice(tokens.start // LIST_ROWS, tokens.stop // LIST_ROWS)
-            nc.vector.tensor_tensor(second[:, tokens], y_all[:].indirect(pos2_t[:, columns]), gate_t[:, 1, tokens], MULT)
+            part = pos2_t[:, tokens.start // LIST_ROWS:tokens.stop // LIST_ROWS]
+            nc.vector.tensor_tensor(term2[:, tokens], y_all[:].indirect(part), gate_t[:, 1, tokens], MULT)
         for tokens in chunks:
-            nc.vector.tensor_tensor(first[:, tokens], first[:, tokens], second[:, tokens], ADD)
-            nc.sync.dma_start(out=out[:, tokens], in_=first[:, tokens])
+            nc.vector.tensor_tensor(term1[:, tokens], term1[:, tokens], term2[:, tokens], ADD)
+            nc.sync.dma_start(out=out[:, tokens], in_=term1[:, tokens])

@@ -12,6 +12,7 @@ U16 = mybir.dt.uint16
 U8 = mybir.dt.uint8
 FP8X4 = mybir.dt.float8_e4m3fn_x4
 SILU = mybir.ActivationFunctionType.Silu
+COPY = mybir.ActivationFunctionType.Copy
 MULT = mybir.AluOpType.mult
 ADD = mybir.AluOpType.add
 
@@ -99,7 +100,7 @@ def tile_routed_moe_kernel(tc, xT, w1, w2, gate, offs, pos1, pos2, out):
             stream.append((freed_by, w2_raw[slab], w2_slabs[:, slab:slab + n]))
             slab += n
         gate_t = keep.tile([P, 2, T], F32, name="gate_t", tag="first_last", align_bytes=256)
-        for dst, src in ((pos1_t[:], pos1), (gate_t[:, 0], gate[0]), (pos2_t[:], pos2), (gate_t[:, 1], gate[1])):
+        for dst, src in ((pos1_t[:], pos1), (pos2_t[:], pos2), (gate_t[:, 0], gate[0]), (gate_t[:, 1], gate[1])):
             stream.append((-1, dst, src))
         issue(-1)
 
@@ -244,11 +245,13 @@ def tile_routed_moe_kernel(tc, xT, w1, w2, gate, offs, pos1, pos2, out):
 
         term1 = grouped_tile([P, T], F32)
         term2 = grouped_tile([P, T], F32)
-        nc.vector.tensor_tensor(term1[:], y_all[:].indirect(pos1_t[:]), gate_t[:, 0, :], MULT)
         chunks = [slice(at, at + OUT_CHUNK) for at in range(0, T, OUT_CHUNK)]
+        nc.vector.tensor_tensor(term1[:], y_all[:].indirect(pos1_t[:]), gate_t[:, 0, :], MULT)
         for tokens in chunks:
             part = pos2_t[:, tokens.start // LIST_ROWS:tokens.stop // LIST_ROWS]
-            nc.vector.tensor_tensor(term2[:, tokens], y_all[:].indirect(part), gate_t[:, 1, tokens], MULT)
+            nc.scalar.activation(term2[:, tokens], y_all[:].indirect(part), COPY)
+        for tokens in chunks:
+            nc.vector.tensor_tensor(term2[:, tokens], term2[:, tokens], gate_t[:, 1, tokens], MULT)
         for tokens in chunks:
             nc.vector.tensor_tensor(term1[:, tokens], term1[:, tokens], term2[:, tokens], ADD)
             nc.sync.dma_start(out=out[:, tokens], in_=term1[:, tokens])

@@ -35,12 +35,12 @@ GROUPED_BUFS = 4
 LED_BUFS = 3
 CODE_BUFS = 3
 
-W2_BATCHES = (("SS", "VV", "V"), ("VV", "S", "V"), ("V", "SS", "V"), ("V", "S", "S", "V"), ("V", "S", "S"), ("S", "V"))
+W2_BATCHES = (("SS", "VV", "V"), ("VV", "S", "V"), ("V", "SS", "V"), ("V", "S", "S", "V"), ("V", "S", "V"), ("S", "V"))
 SHARED_COLUMNS = (32, 48)
 LATE_BATCH = 1
 Y_BANKS = ((0, 4), (4, 8), (8, 11), (11, 12))
 EARLY_SLAB = 15
-OUT_CHUNK = T // 2
+CHUNKS = (384, 192, 192)
 
 
 def tile_routed_moe_kernel(tc, xT, w1, w2, gate, offs, pos1, pos2, out):
@@ -245,13 +245,23 @@ def tile_routed_moe_kernel(tc, xT, w1, w2, gate, offs, pos1, pos2, out):
 
         term1 = grouped_tile([P, T], F32)
         term2 = grouped_tile([P, T], F32)
-        chunks = [slice(at, at + OUT_CHUNK) for at in range(0, T, OUT_CHUNK)]
+        chunks = [slice(sum(CHUNKS[:i]), sum(CHUNKS[:i + 1])) for i in range(len(CHUNKS))]
+
+        def weigh(tokens):
+            nc.vector.tensor_tensor(term2[:, tokens], term2[:, tokens], gate_t[:, 1, tokens], MULT)
+
+        def add(tokens):
+            nc.vector.tensor_tensor(term1[:, tokens], term1[:, tokens], term2[:, tokens], ADD)
+
         nc.vector.tensor_tensor(term1[:], y_all[:].indirect(pos1_t[:]), gate_t[:, 0, :], MULT)
         for tokens in chunks:
             part = pos2_t[:, tokens.start // LIST_ROWS:tokens.stop // LIST_ROWS]
             nc.scalar.activation(term2[:, tokens], y_all[:].indirect(part), COPY)
-        for tokens in chunks:
-            nc.vector.tensor_tensor(term2[:, tokens], term2[:, tokens], gate_t[:, 1, tokens], MULT)
-        for tokens in chunks:
-            nc.vector.tensor_tensor(term1[:, tokens], term1[:, tokens], term2[:, tokens], ADD)
-            nc.sync.dma_start(out=out[:, tokens], in_=term1[:, tokens])
+        weigh(chunks[0])
+        weigh(chunks[1])
+        add(chunks[0])
+        nc.sync.dma_start(out=out[:, chunks[0]], in_=term1[:, chunks[0]])
+        weigh(chunks[2])
+        add(chunks[1])
+        add(chunks[2])
+        nc.sync.dma_start(out=out[:, CHUNKS[0]:], in_=term1[:, CHUNKS[0]:])

@@ -29,14 +29,15 @@ X_SPLIT = 512
 GATHER = 512
 PLACES = 7
 PLACE = J * H
+W1_VECTOR = 32
 PAIRS = E // 2
-PAIR_LAG = 2
+PAIR_LAG = 1
 GROUPED_BUFS = 4
 LED_BUFS = 3
 CODE_BUFS = 3
 
 W2_BATCHES = (("SS", "VV", "V"), ("VV", "S", "V"), ("V", "SS", "V"), ("V", "S", "S", "V"), ("V", "S", "V"), ("S", "V"))
-SHARED_COLUMNS = (32, 48)
+SHARED_COLUMNS = (32, 80)
 LATE_BATCH = 1
 Y_BANKS = ((0, 4), (4, 8), (8, 11), (11, 12))
 EARLY_SLAB = 15
@@ -185,10 +186,11 @@ def tile_routed_moe_kernel(tc, xT, w1, w2, gate, offs, pos1, pos2, out):
 
         for b in range(E + 1):
             if b < E:
-                for g, engine in enumerate("VS"):
+                for g, engine, columns in ((0, "V", slice(0, 128)), (1, "V", slice(0, W1_VECTOR)), (1, "S", slice(W1_VECTOR, 128))):
                     step, i, at = home[b, g]
-                    copier[engine](out=batch_tile(step, i)[:, at:at + HALF].rearrange("p (t m u j) -> p m u t j", t=J, u=2, j=2),
-                                   in_=w1_raw[b][:, :, g * PASS:(g + 1) * PASS].rearrange("p (u j) (m t) -> p m u t j", t=J, j=2))
+                    dst = batch_tile(step, i)[:, at:at + HALF].rearrange("p (t m u j) -> p m u t j", t=J, u=2, j=2)
+                    src = w1_raw[b][:, :, g * PASS:(g + 1) * PASS].rearrange("p (u j) (m t) -> p m u t j", t=J, j=2)
+                    copier[engine](out=dst[:, columns], in_=src[:, columns])
                 issue(b)
             for i, (pair, halves) in enumerate(steps[b]):
                 codes, scales = quantise(batch_tile(b, i)[:], pair)

@@ -29,6 +29,7 @@ X_SPLIT = 512
 GATHER = 512
 PLACES = 7
 PLACE = J * H
+W1_LOADS = (2,) + (1,) * (E - 2)
 W1_VECTOR = 32
 PAIRS = E // 2
 PAIR_LAG = 1
@@ -41,7 +42,8 @@ SHARED_COLUMNS = (32, 80)
 LATE_BATCH = 1
 Y_BANKS = ((0, 4), (4, 8), (8, 11), (11, 12))
 EARLY_SLAB = 15
-CHUNKS = (384, 192, 192)
+CHUNKS = (288, 288, 192)
+STORES = (288, 240, 240)
 
 
 def tile_routed_moe_kernel(tc, xT, w1, w2, gate, offs, pos1, pos2, out):
@@ -79,12 +81,14 @@ def tile_routed_moe_kernel(tc, xT, w1, w2, gate, offs, pos1, pos2, out):
         nc.sync.dma_start(out=x_raw[:], in_=xT.rearrange("(p j) n -> p j n", j=J))
         nc.sync.dma_start(out=offs_t[:], in_=offs)
         w1_raw = []
-        for e in range(E):
-            t, places = land(PLACE)
-            t = t.rearrange("p (j h) -> p j h", j=J)
-            stream.append((tenant[places[0]], t, w1[e].rearrange("(p j) h -> p j h", j=J)))
-            tenant[places[0]] = e
-            w1_raw.append(t)
+        for n in W1_LOADS:
+            e = len(w1_raw)
+            t, places = land(n * PLACE)
+            t = t.rearrange("p (e j h) -> p e j h", j=J, h=H)
+            stream.append((max(tenant[i] for i in places), t, w1[e:e + n].rearrange("e (p j) h -> p e j h", j=J)))
+            for i, place in enumerate(places):
+                tenant[place] = e + i
+                w1_raw.append(t[:, i])
         w2_slabs = w2.rearrange("e (g p j) n -> p (e g) j n", p=P, j=J)
         w2_raw = {}
         slab = 0
@@ -248,12 +252,14 @@ def tile_routed_moe_kernel(tc, xT, w1, w2, gate, offs, pos1, pos2, out):
         term1 = grouped_tile([P, T], F32)
         term2 = grouped_tile([P, T], F32)
         chunks = [slice(sum(CHUNKS[:i]), sum(CHUNKS[:i + 1])) for i in range(len(CHUNKS))]
+        stores = [slice(sum(STORES[:i]), sum(STORES[:i + 1])) for i in range(len(STORES))]
 
         def weigh(tokens):
             nc.vector.tensor_tensor(term2[:, tokens], term2[:, tokens], gate_t[:, 1, tokens], MULT)
 
         def add(tokens):
             nc.vector.tensor_tensor(term1[:, tokens], term1[:, tokens], term2[:, tokens], ADD)
+            nc.sync.dma_start(out=out[:, tokens], in_=term1[:, tokens])
 
         nc.vector.tensor_tensor(term1[:], y_all[:].indirect(pos1_t[:]), gate_t[:, 0, :], MULT)
         for tokens in chunks:
@@ -261,9 +267,7 @@ def tile_routed_moe_kernel(tc, xT, w1, w2, gate, offs, pos1, pos2, out):
             nc.scalar.activation(term2[:, tokens], y_all[:].indirect(part), COPY)
         weigh(chunks[0])
         weigh(chunks[1])
-        add(chunks[0])
-        nc.sync.dma_start(out=out[:, chunks[0]], in_=term1[:, chunks[0]])
+        add(stores[0])
         weigh(chunks[2])
-        add(chunks[1])
-        add(chunks[2])
-        nc.sync.dma_start(out=out[:, CHUNKS[0]:], in_=term1[:, CHUNKS[0]:])
+        add(stores[1])
+        add(stores[2])

@@ -42,8 +42,8 @@ SHARED_COLUMNS = (32, 80)
 LATE_BATCH = 1
 Y_BANKS = ((0, 4), (4, 8), (8, 11), (11, 12))
 EARLY_SLAB = 15
-CHUNKS = (288, 288, 192)
-STORES = (288, 240, 240)
+CHUNKS = (384, 288, 96)
+STORES = (384, 256, 128)
 
 
 def tile_routed_moe_kernel(tc, xT, w1, w2, gate, offs, pos1, pos2, out):
@@ -246,28 +246,31 @@ def tile_routed_moe_kernel(tc, xT, w1, w2, gate, offs, pos1, pos2, out):
             group_w2("V", t[:], slab, slice(0, split))
             group_w2("S", t[:], slab, slice(split, N))
             multiply([slab], *quantise(t[:], None))
-        for (a, z), bank, engine in zip(Y_BANKS, range(len(Y_BANKS)), "SVSS"):
+        for (a, z), bank, engine in zip(Y_BANKS, range(len(Y_BANKS)), "SSVS"):
             copier[engine](out=y_all[:, a * C:z * C], in_=y_bank[bank][:].rearrange("p e n -> p (e n)"))
 
-        term1 = grouped_tile([P, T], F32)
-        term2 = grouped_tile([P, T], F32)
+        terms = grouped_tile([P, 2, T], F32)
         chunks = [slice(sum(CHUNKS[:i]), sum(CHUNKS[:i + 1])) for i in range(len(CHUNKS))]
         stores = [slice(sum(STORES[:i]), sum(STORES[:i + 1])) for i in range(len(STORES))]
+        fused = slice(0, chunks[-1].start)
 
-        def weigh(tokens):
-            nc.vector.tensor_tensor(term2[:, tokens], term2[:, tokens], gate_t[:, 1, tokens], MULT)
+        def fetched(pos_t, tokens):
+            return y_all[:].indirect(pos_t[:, tokens.start // LIST_ROWS:tokens.stop // LIST_ROWS])
+
+        def weigh(which, tokens):
+            nc.vector.tensor_tensor(terms[:, which, tokens], terms[:, which, tokens], gate_t[:, which, tokens], MULT)
 
         def add(tokens):
-            nc.vector.tensor_tensor(term1[:, tokens], term1[:, tokens], term2[:, tokens], ADD)
-            nc.sync.dma_start(out=out[:, tokens], in_=term1[:, tokens])
+            nc.vector.tensor_tensor(terms[:, 0, tokens], terms[:, 0, tokens], terms[:, 1, tokens], ADD)
+            nc.sync.dma_start(out=out[:, tokens], in_=terms[:, 0, tokens])
 
-        nc.vector.tensor_tensor(term1[:], y_all[:].indirect(pos1_t[:]), gate_t[:, 0, :], MULT)
+        nc.vector.tensor_tensor(terms[:, 0, fused], fetched(pos1_t, fused), gate_t[:, 0, fused], MULT)
         for tokens in chunks:
-            part = pos2_t[:, tokens.start // LIST_ROWS:tokens.stop // LIST_ROWS]
-            nc.scalar.activation(term2[:, tokens], y_all[:].indirect(part), COPY)
-        weigh(chunks[0])
-        weigh(chunks[1])
+            nc.scalar.activation(terms[:, 1, tokens], fetched(pos2_t, tokens), COPY)
+        nc.scalar.activation(terms[:, 0, chunks[-1]], fetched(pos1_t, chunks[-1]), COPY)
+        weigh(1, chunks[0])
+        weigh(1, chunks[1])
         add(stores[0])
-        weigh(chunks[2])
+        weigh(slice(0, 2), chunks[2])
         add(stores[1])
         add(stores[2])

@@ -23,7 +23,8 @@ G = H // PASS
 LIST_ROWS = 16
 OPERAND = 128 * J
 HALF = J * OPERAND
-WIDEST = 4096
+HIDDEN = G * OPERAND
+WIDTHS = (4096, 2048, 1536, 1024, 512)
 
 X_SPLIT = 512
 GATHER = 512
@@ -31,17 +32,18 @@ PLACES = 7
 PLACE = J * H
 W1_LOADS = (2,) + (1,) * (E - 2)
 W1_VECTOR = 32
-PAIRS = E // 2
-PAIR_LAG = 1
+LEADS = {3: (0, 1), 5: (2, 3), 7: (4, 5), 9: (6, 7), 10: (8, 9), 11: (10,)}
+DRAIN = 9
 GROUPED_BUFS = 4
 LED_BUFS = 3
 CODE_BUFS = 3
 
-W2_BATCHES = (("SS", "VV", "V"), ("VV", "S", "V"), ("V", "SS", "V"), ("V", "S", "S", "V"), ("V", "S", "V"), ("S", "V"))
-SHARED_COLUMNS = (32, 80)
-LATE_BATCH = 1
+W2_LOADS = ((0, 0, 128), (128, 128, 0, 0), (128, 128, 0, 0), (128, 128, 0), (128, 128, 0),
+            (0,), (128,), (0,), (128,), (0,), (32,), (80,))
+W2_BATCHES = (4, 4, 1, 3, 3, 4, 2, 1, 1, 1)
+LATE_BATCH = 2
 Y_BANKS = ((0, 4), (4, 8), (8, 11), (11, 12))
-EARLY_SLAB = 15
+EARLY_LOAD = 3
 CHUNKS = (384, 288, 96)
 STORES = (384, 256, 128)
 
@@ -77,6 +79,10 @@ def tile_routed_moe_kernel(tc, xT, w1, w2, gate, offs, pos1, pos2, out):
         def grouped_tile(shape, dtype):
             return ring.tile(shape, dtype, name="grouped", tag="grouped", bufs=GROUPED_BUFS, align_bytes=64)
 
+        chunks = [slice(sum(CHUNKS[:i]), sum(CHUNKS[:i + 1])) for i in range(len(CHUNKS))]
+        stores = [slice(sum(STORES[:i]), sum(STORES[:i + 1])) for i in range(len(STORES))]
+        fused = slice(0, chunks[-1].start)
+
         x_raw = keep.tile([P, J, T], F32, name="x_raw", tag="first_last", align_bytes=256)
         nc.sync.dma_start(out=x_raw[:], in_=xT.rearrange("(p j) n -> p j n", j=J))
         nc.sync.dma_start(out=offs_t[:], in_=offs)
@@ -90,23 +96,25 @@ def tile_routed_moe_kernel(tc, xT, w1, w2, gate, offs, pos1, pos2, out):
                 tenant[place] = e + i
                 w1_raw.append(t[:, i])
         w2_slabs = w2.rearrange("e (g p j) n -> p (e g) j n", p=P, j=J)
-        w2_raw = {}
+        w2_raw = []
         slab = 0
-        for n in [len(load) for batch in W2_BATCHES for load in batch] + [1] * len(SHARED_COLUMNS):
-            if slab == EARLY_SLAB:
-                t, freed_by = y_all[:, 0:OPERAND], -1
-            elif slab == E * G - 1:
+        for l, load in enumerate(W2_LOADS):
+            if l == EARLY_LOAD:
+                t, freed_by = y_all[:, 0:len(load) * OPERAND], -1
+            elif l == len(W2_LOADS) - 1:
                 border = Y_BANKS[2][0] * C
-                t, freed_by = y_all[:, border - OPERAND // 2:border + OPERAND // 2], -1
+                t, freed_by = y_all[:, border - OPERAND // 2:border + OPERAND // 2], E
             else:
-                t, places = land(n * OPERAND)
+                t, places = land(len(load) * OPERAND)
                 freed_by = max(tenant[i] for i in places)
-            w2_raw[slab] = t.rearrange("p (s j n) -> p s j n", j=J, n=N)
-            stream.append((freed_by, w2_raw[slab], w2_slabs[:, slab:slab + n]))
-            slab += n
+            w2_raw.append(t.rearrange("p (s j n) -> p s j n", j=J, n=N))
+            stream.append((freed_by, w2_raw[-1], w2_slabs[:, slab:slab + len(load)]))
+            slab += len(load)
         gate_t = keep.tile([P, 2, T], F32, name="gate_t", tag="first_last", align_bytes=256)
-        for dst, src in ((pos1_t[:], pos1), (pos2_t[:], pos2), (gate_t[:, 0], gate[0]), (gate_t[:, 1], gate[1])):
-            stream.append((-1, dst, src))
+        stream.append((-1, pos1_t[:], pos1))
+        stream.append((-1, pos2_t[:], pos2))
+        for which, tokens in ((0, slice(0, T)), (1, slice(0, T))):
+            stream.append((-1, gate_t[:, which, tokens], gate[which][:, tokens]))
         issue(-1)
 
         x_codes = keep.tile([P, T], U32, name="x_codes", align_bytes=64)
@@ -131,73 +139,75 @@ def tile_routed_moe_kernel(tc, xT, w1, w2, gate, offs, pos1, pos2, out):
             for q in range(GATHER // C):
                 slot_q[at // C + q] = (codes[:, q * C:(q + 1) * C], scales[:, q * C:(q + 1) * C])
 
+        late = E
+        leads = dict(LEADS)
+        leads[late] = (E - 1,)
+        led_by = {e: b for b, experts in leads.items() for e in experts}
         led = {}
 
-        def led_tile(pair):
-            if pair not in led:
-                led[pair] = ring.tile([P, WIDEST], BF16, name="led", tag="led", bufs=LED_BUFS, align_bytes=64)
-            return led[pair]
+        def led_tile(b):
+            if b not in led:
+                led[b] = ring.tile([P, WIDTHS[0]], BF16, name="led", tag="led", bufs=LED_BUFS, align_bytes=64)
+            return led[b]
 
-        kept = HALF // J
-        led_codes = keep.tile([P, (PAIRS + 1) * kept], U32, name="led_codes", align_bytes=64)
-        led_scales = keep.tile([P, (PAIRS + 1) * kept], U8, name="led_scales", align_bytes=64)
+        kept = HIDDEN // J
+        led_words = (E - 1) * kept + HALF // J
+        led_codes = keep.tile([P, led_words], U32, name="led_codes", align_bytes=64)
+        led_scales = keep.tile([P, led_words], U8, name="led_scales", align_bytes=64)
         h_q = {}
 
-        def quantise(values, pair):
+        def quantise(values, experts):
             n = values.shape[1]
-            if pair is None:
+            if experts:
+                words = slice(experts[0] * kept, experts[0] * kept + n // J)
+                codes, scales = led_codes[:, words], led_scales[:, words]
+                for i in range(len(experts) * G):
+                    h_q[experts[0] + i // G, i % G] = (codes[:, i * C:(i + 1) * C], scales[:, i * C:(i + 1) * C])
+            else:
                 codes = ring.tile([P, n // J], U32, name="codes", tag="codes", bufs=CODE_BUFS, align_bytes=64)
                 scales = ring.tile([P, n // J], U8, name="scales", tag="scales", bufs=CODE_BUFS, align_bytes=64)
                 codes, scales = codes[:], scales[:]
-            else:
-                words = slice(pair * kept, pair * kept + n // J)
-                codes, scales = led_codes[:, words], led_scales[:, words]
-                for i in range(2 * G):
-                    h_q[2 * pair + i // G, i % G] = (codes[:, i * C:(i + 1) * C], scales[:, i * C:(i + 1) * C])
             at = 0
             while at < n:
-                width = WIDEST
-                while width > n - at:
-                    width //= 2
+                width = max(w for w in WIDTHS if w <= n - at)
                 words = slice(at // J, (at + width) // J)
                 nc.vector.quantize_mx(out=codes[:, words].bitcast(FP8X4), scales=scales[:, words], in_=values[:, at:at + width])
                 at += width
-            first = 0 if pair is None else kept
+            first = len(experts) * kept
             return codes[:, first:], scales[:, first:]
 
         steps = []
-        for b in range(E + 1):
-            halves = [(e, g) for e, g in ((b - 1, 1), (b, 0)) if 0 <= e < E]
-            pair, odd = divmod(b - G - PAIR_LAG, 2)
-            if pair >= 0 and not odd:
-                steps.append([(None, [half]) for half in halves[:-1]] + [(pair, halves[-1:])])
+        for b in range(E):
+            earlier = [(b - 1, 1)] if 0 < b <= DRAIN else []
+            if b in leads:
+                batches = [((), [half]) for half in earlier] + [(leads[b], [(b, 0)])]
             else:
-                steps.append([(None, halves)])
+                batches = [((), earlier + [(b, 0)])]
+            steps.append(batches + ([((), [(b, 1)])] if b >= DRAIN else []))
         home = {}
         for b, batches in enumerate(steps):
-            for i, (pair, halves) in enumerate(batches):
+            for i, (experts, halves) in enumerate(batches):
                 for r, half in enumerate(halves):
-                    home[half] = (b, i, (r if pair is None else r + 1) * HALF)
+                    home[half] = (b, i, len(experts) * HIDDEN + r * HALF)
         plain = {}
 
         def batch_tile(b, i):
-            pair, halves = steps[b][i]
-            if pair is not None:
-                return led_tile(pair)
+            experts, halves = steps[b][i]
+            if experts:
+                return led_tile(b)[:, 0:len(experts) * HIDDEN + HALF]
             if (b, i) not in plain:
                 plain[b, i] = grouped_tile([P, len(halves) * HALF], BF16)
-            return plain[b, i]
+            return plain[b, i][:]
 
-        for b in range(E + 1):
-            if b < E:
-                for g, engine, columns in ((0, "V", slice(0, 128)), (1, "V", slice(0, W1_VECTOR)), (1, "S", slice(W1_VECTOR, 128))):
-                    step, i, at = home[b, g]
-                    dst = batch_tile(step, i)[:, at:at + HALF].rearrange("p (t m u j) -> p m u t j", t=J, u=2, j=2)
-                    src = w1_raw[b][:, :, g * PASS:(g + 1) * PASS].rearrange("p (u j) (m t) -> p m u t j", t=J, j=2)
-                    copier[engine](out=dst[:, columns], in_=src[:, columns])
-                issue(b)
-            for i, (pair, halves) in enumerate(steps[b]):
-                codes, scales = quantise(batch_tile(b, i)[:], pair)
+        for b in range(E):
+            for g, engine, columns in ((0, "V", slice(0, 128)), (1, "V", slice(0, W1_VECTOR)), (1, "S", slice(W1_VECTOR, 128))):
+                step, i, at = home[b, g]
+                dst = batch_tile(step, i)[:, at:at + HALF].rearrange("p (t m u j) -> p m u t j", t=J, u=2, j=2)
+                src = w1_raw[b][:, :, g * PASS:(g + 1) * PASS].rearrange("p (u j) (m t) -> p m u t j", t=J, j=2)
+                copier[engine](out=dst[:, columns], in_=src[:, columns])
+            issue(b)
+            for i, (experts, halves) in enumerate(steps[b]):
+                codes, scales = quantise(batch_tile(b, i), experts)
                 for r, (e, g) in enumerate(halves):
                     xc, xs = slot_q[e]
                     acc = psum.tile([P, J, C], F32, name="acc", tag="acc", bufs=2 * G)
@@ -205,20 +215,47 @@ def tile_routed_moe_kernel(tc, xT, w1, w2, gate, offs, pos1, pos2, out):
                         s = slice((J * r + q) * 128, (J * r + q + 1) * 128)
                         nc.tensor.matmul_mx(out=acc[:, q, :], lhsT=codes[:, s].bitcast(FP8X4), lhsT_scale=scales[:, s],
                                             rhs=xc.bitcast(FP8X4), rhs_scale=xs, start=True, stop=True)
-                    at = (G * (e % 2) + g) * OPERAND
-                    nc.scalar.activation(led_tile(e // 2)[:, at:at + OPERAND].rearrange("p (n j) -> p n j", j=J),
+                    at = (e - leads[led_by[e]][0]) * HIDDEN + g * OPERAND
+                    nc.scalar.activation(led_tile(led_by[e])[:, at:at + OPERAND].rearrange("p (n j) -> p n j", j=J),
                                          acc[:].rearrange("p t n -> p n t"), SILU)
 
         y_bank = {}
+        batch_of = [b for b, n in enumerate(W2_BATCHES) for r in range(n)]
+        load_of = [l for l, load in enumerate(W2_LOADS) for r in load]
+        share = [v for load in W2_LOADS for v in load]
+        staged = {}
 
-        def group_w2(engine, dst, first, columns):
-            twos = slice(columns.start // 2, columns.stop // 2)
-            copier[engine](out=dst.rearrange("p (s c i j) -> p s c j i", c=N // 2, i=2, j=J)[:, :, twos],
-                           in_=w2_raw[first].rearrange("p s j (c i) -> p s c j i", i=2)[:, :, twos])
+        def stage(b):
+            if b not in staged:
+                n = W2_BATCHES[b] * OPERAND
+                staged[b] = led_tile(late)[:, 0:HIDDEN + n] if b == LATE_BATCH else grouped_tile([P, n], BF16)[:]
+            return staged[b]
 
-        def multiply(slabs, codes, scales):
-            for r, slab in enumerate(slabs):
-                e, g = divmod(slab, G)
+        def empty(bank, engine):
+            a, z = Y_BANKS[bank]
+            copier[engine](out=y_all[:, a * C:z * C], in_=y_bank[bank][:].rearrange("p e n -> p (e n)"))
+
+        def copy_load(l):
+            first = load_of.index(l)
+            for engine in "VS":
+                slab = first
+                while slab < first + len(W2_LOADS[l]):
+                    n = 1
+                    while n < 2 and slab + n < first + len(W2_LOADS[l]) and (share[slab + n], batch_of[slab + n]) == (share[slab], batch_of[slab]):
+                        n += 1
+                    twos = slice(0, share[slab] // 2) if engine == "V" else slice(share[slab] // 2, N // 2)
+                    if twos.start < twos.stop:
+                        b = batch_of[slab]
+                        at = (slab - batch_of.index(b)) * OPERAND + (HIDDEN if b == LATE_BATCH else 0)
+                        dst = stage(b)[:, at:at + n * OPERAND].rearrange("p (s c i j) -> p s c j i", c=N // 2, i=2, j=J)
+                        src = w2_raw[l][:, slab - first:slab - first + n].rearrange("p s j (c i) -> p s c j i", i=2)
+                        copier[engine](out=dst[:, :, twos], in_=src[:, :, twos])
+                    slab += n
+
+        def multiply(b):
+            codes, scales = quantise(stage(b), leads[late] if b == LATE_BATCH else ())
+            for r in range(W2_BATCHES[b]):
+                e, g = divmod(batch_of.index(b) + r, G)
                 bank = [i for i, (a, z) in enumerate(Y_BANKS) if a <= e < z][0]
                 a, z = Y_BANKS[bank]
                 if bank not in y_bank:
@@ -228,31 +265,25 @@ def tile_routed_moe_kernel(tc, xT, w1, w2, gate, offs, pos1, pos2, out):
                 nc.tensor.matmul_mx(out=y_bank[bank][:, e - a, :], lhsT=codes[:, s].bitcast(FP8X4), lhsT_scale=scales[:, s],
                                     rhs=hc.bitcast(FP8X4), rhs_scale=hs, start=(g == 0), stop=(g == G - 1))
 
-        start = 0
-        for b, loads in enumerate(W2_BATCHES):
-            n = sum(len(load) for load in loads)
-            pair = PAIRS - 1 if b == LATE_BATCH else None
-            t = grouped_tile([P, n * OPERAND], BF16) if pair is None else led_tile(pair)
-            at = 0 if pair is None else HALF
-            slab = start
-            for load in loads:
-                group_w2(load[0], t[:, at:at + len(load) * OPERAND], slab, slice(0, N))
-                at += len(load) * OPERAND
-                slab += len(load)
-            multiply(range(start, slab), *quantise(t[:], pair))
-            start = slab
-        for slab, split in enumerate(SHARED_COLUMNS, start):
-            t = grouped_tile([P, OPERAND], BF16)
-            group_w2("V", t[:], slab, slice(0, split))
-            group_w2("S", t[:], slab, slice(split, N))
-            multiply([slab], *quantise(t[:], None))
-        for (a, z), bank, engine in zip(Y_BANKS, range(len(Y_BANKS)), "SSVS"):
-            copier[engine](out=y_all[:, a * C:z * C], in_=y_bank[bank][:].rearrange("p e n -> p (e n)"))
+        due = []
+        for b in range(len(W2_BATCHES)):
+            slabs = [s for s in range(E * G) if batch_of[s] == b]
+            due.append(max(load_of[s] + (share[s] < N) for s in slabs))
+        done = 0
+        for l in range(len(W2_LOADS) + 1):
+            if l < len(W2_LOADS):
+                copy_load(l)
+            if l == EARLY_LOAD:
+                empty(0, "S")
+            if l == len(W2_LOADS) - 2:
+                issue(E)
+            while done < len(due) and due[done] <= l:
+                multiply(done)
+                done += 1
+        for bank, engine in ((1, "S"), (2, "V"), (3, "S")):
+            empty(bank, engine)
 
         terms = grouped_tile([P, 2, T], F32)
-        chunks = [slice(sum(CHUNKS[:i]), sum(CHUNKS[:i + 1])) for i in range(len(CHUNKS))]
-        stores = [slice(sum(STORES[:i]), sum(STORES[:i + 1])) for i in range(len(STORES))]
-        fused = slice(0, chunks[-1].start)
 
         def fetched(pos_t, tokens):
             return y_all[:].indirect(pos_t[:, tokens.start // LIST_ROWS:tokens.stop // LIST_ROWS])

@@ -32,15 +32,16 @@ PLACES = 7
 PLACE = J * H
 W1_LOADS = (2,) + (1,) * (E - 2)
 W1_VECTOR = 32
+SHARED_FROM = 8
 LEADS = {3: (0, 1), 5: (2, 3), 7: (4, 5), 9: (6, 7), 10: (8, 9), 11: (10,)}
 DRAIN = 9
 GROUPED_BUFS = 4
 LED_BUFS = 3
 CODE_BUFS = 3
 
-W2_LOADS = ((0, 0, 128), (128, 128, 0, 0), (128, 128, 0, 0), (128, 128, 0), (128, 128, 0),
-            (0,), (128,), (0,), (128,), (0,), (32,), (80,))
-W2_BATCHES = (4, 4, 1, 3, 3, 4, 2, 1, 1, 1)
+W2_LOADS = ((0, 0, 128), (128, 128, 0, 0), (128, 128, 0, 0), (128, 128, 0), (128, 128), (0, 128),
+            (0,), (128,), (0,), (128,), (32,), (80,))
+W2_BATCHES = ((8,), (8,), (2,), (6,), (6,), (1, 4, 4, 4, 1, 2, 2))
 LATE_BATCH = 2
 Y_BANKS = ((0, 4), (4, 8), (8, 11), (11, 12))
 EARLY_LOAD = 3
@@ -156,6 +157,11 @@ def tile_routed_moe_kernel(tc, xT, w1, w2, gate, offs, pos1, pos2, out):
         led_scales = keep.tile([P, led_words], U8, name="led_scales", align_bytes=64)
         h_q = {}
 
+        def code_tiles(words):
+            codes = ring.tile([P, words], U32, name="codes", tag="codes", bufs=CODE_BUFS, align_bytes=64)
+            scales = ring.tile([P, words], U8, name="scales", tag="scales", bufs=CODE_BUFS, align_bytes=64)
+            return codes[:], scales[:]
+
         def quantise(values, experts):
             n = values.shape[1]
             if experts:
@@ -164,9 +170,7 @@ def tile_routed_moe_kernel(tc, xT, w1, w2, gate, offs, pos1, pos2, out):
                 for i in range(len(experts) * G):
                     h_q[experts[0] + i // G, i % G] = (codes[:, i * C:(i + 1) * C], scales[:, i * C:(i + 1) * C])
             else:
-                codes = ring.tile([P, n // J], U32, name="codes", tag="codes", bufs=CODE_BUFS, align_bytes=64)
-                scales = ring.tile([P, n // J], U8, name="scales", tag="scales", bufs=CODE_BUFS, align_bytes=64)
-                codes, scales = codes[:], scales[:]
+                codes, scales = code_tiles(n // J)
             at = 0
             while at < n:
                 width = max(w for w in WIDTHS if w <= n - at)
@@ -200,7 +204,10 @@ def tile_routed_moe_kernel(tc, xT, w1, w2, gate, offs, pos1, pos2, out):
             return plain[b, i][:]
 
         for b in range(E):
-            for g, engine, columns in ((0, "V", slice(0, 128)), (1, "V", slice(0, W1_VECTOR)), (1, "S", slice(W1_VECTOR, 128))):
+            shared = W1_VECTOR if b >= SHARED_FROM else 0
+            for g, engine, columns in ((0, "V", slice(0, 128)), (1, "V", slice(0, shared)), (1, "S", slice(shared, 128))):
+                if columns.start == columns.stop:
+                    continue
                 step, i, at = home[b, g]
                 dst = batch_tile(step, i)[:, at:at + HALF].rearrange("p (t m u j) -> p m u t j", t=J, u=2, j=2)
                 src = w1_raw[b][:, :, g * PASS:(g + 1) * PASS].rearrange("p (u j) (m t) -> p m u t j", t=J, j=2)
@@ -220,14 +227,22 @@ def tile_routed_moe_kernel(tc, xT, w1, w2, gate, offs, pos1, pos2, out):
                                          acc[:].rearrange("p t n -> p n t"), SILU)
 
         y_bank = {}
-        batch_of = [b for b, n in enumerate(W2_BATCHES) for r in range(n)]
-        load_of = [l for l, load in enumerate(W2_LOADS) for r in load]
+        load_of = [l for l, load in enumerate(W2_LOADS) for v in load]
         share = [v for load in W2_LOADS for v in load]
+        pieces = []
+        for b, widths in enumerate(W2_BATCHES):
+            for n in widths:
+                at = pieces[-1][2] if pieces else 0
+                pieces.append((b, at, at + n))
+        first_of = {b: min(a for i, a, z in pieces if i == b) // 2 for b in range(len(W2_BATCHES))}
+        batch_of = [b for b, a, z in pieces for half in range(a, z) if half % 2 == 0]
+        cut = [z // 2 for b, a, z in pieces if z % 2 and a < z - 1]
         staged = {}
+        coded = {}
 
         def stage(b):
             if b not in staged:
-                n = W2_BATCHES[b] * OPERAND
+                n = sum(W2_BATCHES[b]) * OPERAND // 2
                 staged[b] = led_tile(late)[:, 0:HIDDEN + n] if b == LATE_BATCH else grouped_tile([P, n], BF16)[:]
             return staged[b]
 
@@ -241,34 +256,43 @@ def tile_routed_moe_kernel(tc, xT, w1, w2, gate, offs, pos1, pos2, out):
                 slab = first
                 while slab < first + len(W2_LOADS[l]):
                     n = 1
-                    while n < 2 and slab + n < first + len(W2_LOADS[l]) and (share[slab + n], batch_of[slab + n]) == (share[slab], batch_of[slab]):
-                        n += 1
-                    twos = slice(0, share[slab] // 2) if engine == "V" else slice(share[slab] // 2, N // 2)
-                    if twos.start < twos.stop:
-                        b = batch_of[slab]
-                        at = (slab - batch_of.index(b)) * OPERAND + (HIDDEN if b == LATE_BATCH else 0)
-                        dst = stage(b)[:, at:at + n * OPERAND].rearrange("p (s c i j) -> p s c j i", c=N // 2, i=2, j=J)
-                        src = w2_raw[l][:, slab - first:slab - first + n].rearrange("p s j (c i) -> p s c j i", i=2)
-                        copier[engine](out=dst[:, :, twos], in_=src[:, :, twos])
+                    nxt = slab + 1
+                    if nxt < first + len(W2_LOADS[l]) and (share[nxt], batch_of[nxt]) == (share[slab], batch_of[slab]):
+                        n = 2
+                    columns = (0, share[slab]) if engine == "V" else (share[slab], N)
+                    if slab in cut and engine == "V":
+                        columns = (0, N // 2, N)
+                    for a, z in zip(columns, columns[1:]):
+                        if a < z:
+                            b = batch_of[slab]
+                            at = (slab - first_of[b]) * OPERAND + (HIDDEN if b == LATE_BATCH else 0)
+                            dst = stage(b)[:, at:at + n * OPERAND].rearrange("p (s c i j) -> p s c j i", c=N // 2, i=2, j=J)
+                            src = w2_raw[l][:, slab - first:slab - first + n].rearrange("p s j (c i) -> p s c j i", i=2)
+                            copier[engine](out=dst[:, :, a // 2:z // 2], in_=src[:, :, a // 2:z // 2])
                     slab += n
 
-        def multiply(b):
-            codes, scales = quantise(stage(b), leads[late] if b == LATE_BATCH else ())
-            for r in range(W2_BATCHES[b]):
-                e, g = divmod(batch_of.index(b) + r, G)
-                bank = [i for i, (a, z) in enumerate(Y_BANKS) if a <= e < z][0]
-                a, z = Y_BANKS[bank]
+        def multiply(b, a, z):
+            if b == LATE_BATCH:
+                coded[b] = quantise(stage(b), leads[late])
+            else:
+                if b not in coded:
+                    coded[b] = code_tiles(stage(b).shape[1] // J)
+                values = slice((a - 2 * first_of[b]) * OPERAND // 2, (z - 2 * first_of[b]) * OPERAND // 2)
+                words = slice(values.start // J, values.stop // J)
+                nc.vector.quantize_mx(out=coded[b][0][:, words].bitcast(FP8X4), scales=coded[b][1][:, words], in_=stage(b)[:, values])
+            codes, scales = coded[b]
+            for slab in range(a // 2, z // 2):
+                e, g = divmod(slab, G)
+                bank = [i for i, (lo, hi) in enumerate(Y_BANKS) if lo <= e < hi][0]
+                lo, hi = Y_BANKS[bank]
                 if bank not in y_bank:
-                    y_bank[bank] = psum.tile([N, z - a, C], F32, name="acc_y", tag="acc_y", bufs=len(Y_BANKS))
+                    y_bank[bank] = psum.tile([N, hi - lo, C], F32, name="acc_y", tag="acc_y", bufs=len(Y_BANKS))
                 hc, hs = h_q[e, g]
-                s = slice(r * N, (r + 1) * N)
-                nc.tensor.matmul_mx(out=y_bank[bank][:, e - a, :], lhsT=codes[:, s].bitcast(FP8X4), lhsT_scale=scales[:, s],
+                s = slice((slab - first_of[b]) * N, (slab - first_of[b] + 1) * N)
+                nc.tensor.matmul_mx(out=y_bank[bank][:, e - lo, :], lhsT=codes[:, s].bitcast(FP8X4), lhsT_scale=scales[:, s],
                                     rhs=hc.bitcast(FP8X4), rhs_scale=hs, start=(g == 0), stop=(g == G - 1))
 
-        due = []
-        for b in range(len(W2_BATCHES)):
-            slabs = [s for s in range(E * G) if batch_of[s] == b]
-            due.append(max(load_of[s] + (share[s] < N) for s in slabs))
+        due = [max(load_of[s] + (share[s] < N) for s in range(a // 2, (z + 1) // 2)) for b, a, z in pieces]
         done = 0
         for l in range(len(W2_LOADS) + 1):
             if l < len(W2_LOADS):
@@ -278,7 +302,7 @@ def tile_routed_moe_kernel(tc, xT, w1, w2, gate, offs, pos1, pos2, out):
             if l == len(W2_LOADS) - 2:
                 issue(E)
             while done < len(due) and due[done] <= l:
-                multiply(done)
+                multiply(*pieces[done])
                 done += 1
         for bank, engine in ((1, "S"), (2, "V"), (3, "S")):
             empty(bank, engine)

@@ -30,7 +30,7 @@ X_SPLIT = 512
 GATHER = 512
 PLACES = 7
 PLACE = J * H
-W1_LOADS = (2,) + (1,) * (E - 2)
+W1_LOADS = (2, 2) + (1,) * (E - 4)
 W1_VECTOR = 32
 SHARED_FROM = 8
 LEADS = {3: (0, 1), 5: (2, 3), 7: (4, 5), 9: (6, 7), 10: (8, 9), 11: (10,)}
@@ -45,8 +45,9 @@ W2_BATCHES = ((8,), (8,), (2,), (6,), (6,), (1, 4, 4, 4, 1, 2, 2))
 LATE_BATCH = 2
 Y_BANKS = ((0, 4), (4, 8), (8, 11), (11, 12))
 EARLY_LOAD = 3
-CHUNKS = (384, 288, 96)
-STORES = (384, 256, 128)
+CHUNKS = (192, 448, 128)
+CHUNK_BANKS = (0, 1, 0)
+STORES = (192, 192, 192, 192)
 
 
 def tile_routed_moe_kernel(tc, xT, w1, w2, gate, offs, pos1, pos2, out):
@@ -82,11 +83,22 @@ def tile_routed_moe_kernel(tc, xT, w1, w2, gate, offs, pos1, pos2, out):
 
         chunks = [slice(sum(CHUNKS[:i]), sum(CHUNKS[:i + 1])) for i in range(len(CHUNKS))]
         stores = [slice(sum(STORES[:i]), sum(STORES[:i + 1])) for i in range(len(STORES))]
-        fused = slice(0, chunks[-1].start)
 
         x_raw = keep.tile([P, J, T], F32, name="x_raw", tag="first_last", align_bytes=256)
         nc.sync.dma_start(out=x_raw[:], in_=xT.rearrange("(p j) n -> p j n", j=J))
         nc.sync.dma_start(out=offs_t[:], in_=offs)
+        row = keep.tile([P, T], F32, name="row")
+        ones = keep.tile([P, P], F32, name="ones")
+        nc.gpsimd.memset(row[:], 0.0)
+        nc.gpsimd.memset(ones[:], 1.0)
+        nc.sync.dma_start(out=row[0:1, :], in_=gate[1][0:1, :])
+        banks = [psum.tile([P, 512], F32, name="second", tag="second", bufs=2) for b in range(2)]
+        filled = [0, 0]
+        second = []
+        for tokens, b in zip(chunks, CHUNK_BANKS):
+            second.append(banks[b][:, filled[b]:filled[b] + tokens.stop - tokens.start])
+            filled[b] += tokens.stop - tokens.start
+            nc.tensor.matmul(second[-1], ones[:], row[:, tokens], start=True, stop=True)
         w1_raw = []
         for n in W1_LOADS:
             e = len(w1_raw)
@@ -111,11 +123,10 @@ def tile_routed_moe_kernel(tc, xT, w1, w2, gate, offs, pos1, pos2, out):
             w2_raw.append(t.rearrange("p (s j n) -> p s j n", j=J, n=N))
             stream.append((freed_by, w2_raw[-1], w2_slabs[:, slab:slab + len(load)]))
             slab += len(load)
-        gate_t = keep.tile([P, 2, T], F32, name="gate_t", tag="first_last", align_bytes=256)
+        gate_t = keep.tile([P, T], F32, name="gate_t", tag="first_last", align_bytes=256)
         stream.append((-1, pos1_t[:], pos1))
+        stream.append((-1, gate_t[:], gate[0]))
         stream.append((-1, pos2_t[:], pos2))
-        for which, tokens in ((0, slice(0, T)), (1, slice(0, T))):
-            stream.append((-1, gate_t[:, which, tokens], gate[which][:, tokens]))
         issue(-1)
 
         x_codes = keep.tile([P, T], U32, name="x_codes", align_bytes=64)
@@ -286,7 +297,10 @@ def tile_routed_moe_kernel(tc, xT, w1, w2, gate, offs, pos1, pos2, out):
                 bank = [i for i, (lo, hi) in enumerate(Y_BANKS) if lo <= e < hi][0]
                 lo, hi = Y_BANKS[bank]
                 if bank not in y_bank:
-                    y_bank[bank] = psum.tile([N, hi - lo, C], F32, name="acc_y", tag="acc_y", bufs=len(Y_BANKS))
+                    if bank < 2:
+                        y_bank[bank] = psum.tile([N, hi - lo, C], F32, name="acc_y", tag="acc_y", bufs=2)
+                    else:
+                        y_bank[bank] = psum.tile([N, hi - lo, C], F32, name="acc_late", tag="acc", bufs=2 * G)
                 hc, hs = h_q[e, g]
                 s = slice((slab - first_of[b]) * N, (slab - first_of[b] + 1) * N)
                 nc.tensor.matmul_mx(out=y_bank[bank][:, e - lo, :], lhsT=codes[:, s].bitcast(FP8X4), lhsT_scale=scales[:, s],
@@ -312,20 +326,15 @@ def tile_routed_moe_kernel(tc, xT, w1, w2, gate, offs, pos1, pos2, out):
         def fetched(pos_t, tokens):
             return y_all[:].indirect(pos_t[:, tokens.start // LIST_ROWS:tokens.stop // LIST_ROWS])
 
-        def weigh(which, tokens):
-            nc.vector.tensor_tensor(terms[:, which, tokens], terms[:, which, tokens], gate_t[:, which, tokens], MULT)
-
-        def add(tokens):
-            nc.vector.tensor_tensor(terms[:, 0, tokens], terms[:, 0, tokens], terms[:, 1, tokens], ADD)
+        def add(engine, tokens):
+            engine.tensor_tensor(terms[:, 0, tokens], terms[:, 0, tokens], terms[:, 1, tokens], ADD)
             nc.sync.dma_start(out=out[:, tokens], in_=terms[:, 0, tokens])
 
-        nc.vector.tensor_tensor(terms[:, 0, fused], fetched(pos1_t, fused), gate_t[:, 0, fused], MULT)
+        nc.vector.tensor_tensor(terms[:, 0, :], fetched(pos1_t, slice(0, T)), gate_t[:], MULT)
         for tokens in chunks:
             nc.scalar.activation(terms[:, 1, tokens], fetched(pos2_t, tokens), COPY)
-        nc.scalar.activation(terms[:, 0, chunks[-1]], fetched(pos1_t, chunks[-1]), COPY)
-        weigh(1, chunks[0])
-        weigh(1, chunks[1])
-        add(stores[0])
-        weigh(slice(0, 2), chunks[2])
-        add(stores[1])
-        add(stores[2])
+        for tokens, weight in zip(chunks, second):
+            nc.vector.tensor_tensor(terms[:, 1, tokens], terms[:, 1, tokens], weight, MULT)
+        add(nc.gpsimd, stores[0])
+        for tokens in stores[1:]:
+            add(nc.vector, tokens)

@@ -45,6 +45,7 @@ W2_BATCHES = ((8,), (8,), (2,), (6,), (6,), (1, 4, 4, 4, 1, 2, 2))
 LATE_BATCH = 2
 Y_BANKS = ((0, 4), (4, 8), (8, 11), (11, 12))
 EARLY_LOAD = 3
+ROW_BEFORE = 5
 CHUNKS = (192, 448, 128)
 CHUNK_BANKS = (0, 1, 0)
 STORES = (192, 192, 192, 192)
@@ -91,14 +92,6 @@ def tile_routed_moe_kernel(tc, xT, w1, w2, gate, offs, pos1, pos2, out):
         ones = keep.tile([P, P], F32, name="ones")
         nc.gpsimd.memset(row[:], 0.0)
         nc.gpsimd.memset(ones[:], 1.0)
-        nc.sync.dma_start(out=row[0:1, :], in_=gate[1][0:1, :])
-        banks = [psum.tile([P, 512], F32, name="second", tag="second", bufs=2) for b in range(2)]
-        filled = [0, 0]
-        second = []
-        for tokens, b in zip(chunks, CHUNK_BANKS):
-            second.append(banks[b][:, filled[b]:filled[b] + tokens.stop - tokens.start])
-            filled[b] += tokens.stop - tokens.start
-            nc.tensor.matmul(second[-1], ones[:], row[:, tokens], start=True, stop=True)
         w1_raw = []
         for n in W1_LOADS:
             e = len(w1_raw)
@@ -120,6 +113,8 @@ def tile_routed_moe_kernel(tc, xT, w1, w2, gate, offs, pos1, pos2, out):
             else:
                 t, places = land(len(load) * OPERAND)
                 freed_by = max(tenant[i] for i in places)
+            if l == ROW_BEFORE:
+                stream.append((-1, row[0:1, :], gate[1][0:1, :]))
             w2_raw.append(t.rearrange("p (s j n) -> p s j n", j=J, n=N))
             stream.append((freed_by, w2_raw[-1], w2_slabs[:, slab:slab + len(load)]))
             slab += len(load)
@@ -306,6 +301,16 @@ def tile_routed_moe_kernel(tc, xT, w1, w2, gate, offs, pos1, pos2, out):
                 nc.tensor.matmul_mx(out=y_bank[bank][:, e - lo, :], lhsT=codes[:, s].bitcast(FP8X4), lhsT_scale=scales[:, s],
                                     rhs=hc.bitcast(FP8X4), rhs_scale=hs, start=(g == 0), stop=(g == G - 1))
 
+        second = []
+
+        def spread():
+            banks = [psum.tile([P, 512], F32, name="second", tag="second", bufs=2) for b in range(2)]
+            filled = [0, 0]
+            for tokens, b in zip(chunks, CHUNK_BANKS):
+                second.append(banks[b][:, filled[b]:filled[b] + tokens.stop - tokens.start])
+                filled[b] += tokens.stop - tokens.start
+                nc.tensor.matmul(second[-1], ones[:], row[:, tokens], start=True, stop=True)
+
         due = [max(load_of[s] + (share[s] < N) for s in range(a // 2, (z + 1) // 2)) for b, a, z in pieces]
         done = 0
         for l in range(len(W2_LOADS) + 1):
@@ -313,6 +318,8 @@ def tile_routed_moe_kernel(tc, xT, w1, w2, gate, offs, pos1, pos2, out):
                 copy_load(l)
             if l == EARLY_LOAD:
                 empty(0, "S")
+            if l == ROW_BEFORE:
+                spread()
             if l == len(W2_LOADS) - 2:
                 issue(E)
             while done < len(due) and due[done] <= l:

@@ -30,7 +30,7 @@ X_SPLIT = 512
 GATHER = 512
 PLACES = 7
 PLACE = J * H
-W1_LOADS = (2, 2) + (1,) * (E - 4)
+W1_LOADS = (2,) + (1,) * (E - 2)
 W1_VECTOR = 32
 SHARED_FROM = 8
 LEADS = {3: (0, 1), 5: (2, 3), 7: (4, 5), 9: (6, 7), 10: (8, 9), 11: (10,)}
@@ -39,8 +39,8 @@ GROUPED_BUFS = 4
 LED_BUFS = 3
 CODE_BUFS = 3
 
-W2_LOADS = ((0, 0, 128), (128, 128, 0, 0), (128, 128, 0, 0), (128, 128, 0), (128, 128), (0, 128),
-            (0,), (128,), (0,), (128,), (32,), (80,))
+W2_LOADS = ((0, 0, 128), (128, 128, 0, 0), (128, 128, 0, 0), (128, 128, 0), (128, 128), (0, 128, 0),
+            (128,), (0,), (128,), (32,), (80,))
 W2_BATCHES = ((8,), (8,), (2,), (6,), (6,), (1, 4, 4, 4, 1, 2, 2))
 LATE_BATCH = 2
 Y_BANKS = ((0, 4), (4, 8), (8, 11), (11, 12))

from contextlib import ExitStack

import concourse.mybir as mybir

K, T, E, C, H, N = 512, 768, 12, 128, 1024, 128
FLOPS = 2 * E * C * H * (K + N)

F32 = mybir.dt.float32
BF16 = mybir.dt.bfloat16
U32 = mybir.dt.uint32
U16 = mybir.dt.uint16
U8 = mybir.dt.uint8
FP8X4 = mybir.dt.float8_e4m3fn_x4
SILU = mybir.ActivationFunctionType.Silu
COPY = mybir.ActivationFunctionType.Copy
MULT = mybir.AluOpType.mult
ADD = mybir.AluOpType.add

P = 128
J = 4
PASS = P * J
G = H // PASS
LIST_ROWS = 16
OPERAND = 128 * J
HALF = J * OPERAND
HIDDEN = G * OPERAND
WIDTHS = (4096, 2048, 1536, 1024, 512)

X_SPLIT = 512
GATHER = 512
PLACES = 7
PLACE = J * H
W1_LOADS = (2,) + (1,) * (E - 2)
W1_VECTOR = 32
SHARED_FROM = 8
LEADS = {3: (0, 1), 5: (2, 3), 7: (4, 5), 9: (6, 7), 10: (8, 9), 11: (10,)}
DRAIN = 9
GROUPED_BUFS = 4
LED_BUFS = 3
CODE_BUFS = 3

W2_LOADS = ((0, 0, 128), (128, 128, 0, 0), (128, 128, 0, 0), (128, 128, 0), (128, 128), (0, 128, 0),
            (128,), (0,), (128,), (32,), (80,))
W2_BATCHES = ((8,), (8,), (2,), (6,), (6,), (1, 4, 4, 4, 1, 2, 2))
LATE_BATCH = 2
Y_BANKS = ((0, 4), (4, 8), (8, 11), (11, 12))
EARLY_LOAD = 3
ROW_BEFORE = 5
CHUNKS = (192, 448, 128)
CHUNK_BANKS = (0, 1, 0)
STORES = (192, 192, 192, 192)


def tile_routed_moe_kernel(tc, xT, w1, w2, gate, offs, pos1, pos2, out):
    nc = tc.nc
    copier = {"V": nc.vector.tensor_copy, "S": nc.scalar.copy}
    with ExitStack() as ctx:
        keep = ctx.enter_context(tc.tile_pool(name="keep", bufs=1))
        ring = ctx.enter_context(tc.tile_pool(name="ring", bufs=1))
        psum = ctx.enter_context(tc.psum_pool(name="psum", bufs=1))

        offs_t = keep.tile([P, E * C // LIST_ROWS], U16, name="offs_t")
        pos1_t = keep.tile([P, T // LIST_ROWS], U16, name="pos1_t")
        pos2_t = keep.tile([P, T // LIST_ROWS], U16, name="pos2_t")
        y_all = keep.tile([P, E * C], F32, name="y_all", align_bytes=256)
        landing = keep.tile([P, PLACES * PLACE], F32, name="landing", align_bytes=256)
        tenant = [-1] * PLACES
        cursor = [0]
        stream = []

        def land(n):
            if cursor[0] + n > PLACES * PLACE:
                cursor[0] = 0
            cursor[0] += n
            return landing[:, cursor[0] - n:cursor[0]], range((cursor[0] - n) // PLACE, (cursor[0] - 1) // PLACE + 1)

        def issue(copied):
            while stream and stream[0][0] <= copied:
                dst, src = stream.pop(0)[1:]
                nc.sync.dma_start(out=dst, in_=src)

        def grouped_tile(shape, dtype):
            return ring.tile(shape, dtype, name="grouped", tag="grouped", bufs=GROUPED_BUFS, align_bytes=64)

        chunks = [slice(sum(CHUNKS[:i]), sum(CHUNKS[:i + 1])) for i in range(len(CHUNKS))]
        stores = [slice(sum(STORES[:i]), sum(STORES[:i + 1])) for i in range(len(STORES))]

        x_raw = keep.tile([P, J, T], F32, name="x_raw", tag="first_last", align_bytes=256)
        nc.sync.dma_start(out=x_raw[:], in_=xT.rearrange("(p j) n -> p j n", j=J))
        nc.sync.dma_start(out=offs_t[:], in_=offs)
        row = keep.tile([P, T], F32, name="row")
        ones = keep.tile([P, P], F32, name="ones")
        nc.gpsimd.memset(row[:], 0.0)
        nc.gpsimd.memset(ones[:], 1.0)
        w1_raw = []
        for n in W1_LOADS:
            e = len(w1_raw)
            t, places = land(n * PLACE)
            t = t.rearrange("p (e j h) -> p e j h", j=J, h=H)
            stream.append((max(tenant[i] for i in places), t, w1[e:e + n].rearrange("e (p j) h -> p e j h", j=J)))
            for i, place in enumerate(places):
                tenant[place] = e + i
                w1_raw.append(t[:, i])
        w2_slabs = w2.rearrange("e (g p j) n -> p (e g) j n", p=P, j=J)
        w2_raw = []
        slab = 0
        for l, load in enumerate(W2_LOADS):
            if l == EARLY_LOAD:
                t, freed_by = y_all[:, 0:len(load) * OPERAND], -1
            elif l == len(W2_LOADS) - 1:
                border = Y_BANKS[2][0] * C
                t, freed_by = y_all[:, border - OPERAND // 2:border + OPERAND // 2], E
            else:
                t, places = land(len(load) * OPERAND)
                freed_by = max(tenant[i] for i in places)
            if l == ROW_BEFORE:
                stream.append((-1, row[0:1, :], gate[1][0:1, :]))
            w2_raw.append(t.rearrange("p (s j n) -> p s j n", j=J, n=N))
            stream.append((freed_by, w2_raw[-1], w2_slabs[:, slab:slab + len(load)]))
            slab += len(load)
        gate_t = keep.tile([P, T], F32, name="gate_t", tag="first_last", align_bytes=256)
        stream.append((-1, pos1_t[:], pos1))
        stream.append((-1, gate_t[:], gate[0]))
        stream.append((-1, pos2_t[:], pos2))
        issue(-1)

        x_codes = keep.tile([P, T], U32, name="x_codes", align_bytes=64)
        x_scales = keep.tile([P, T], U8, name="x_scales", align_bytes=64)
        nc.gpsimd.memset(x_scales[:], 0)
        x_parts = []
        for a, z, engine in ((0, X_SPLIT, "V"), (X_SPLIT, T, "S")):
            t = grouped_tile([P, z - a, J], BF16)
            copier[engine](out=t[:].rearrange("p (c i) j -> p c j i", i=2),
                           in_=x_raw[:, :, a:z].rearrange("p j (c i) -> p c j i", i=2))
            x_parts.append((a, z, t))
        for a, z, t in x_parts:
            nc.vector.quantize_mx(out=x_codes[:, a:z].bitcast(FP8X4), scales=x_scales[:, a:z],
                                  in_=t[:].rearrange("p n j -> p (n j)"))
        slot_q = {}
        for at in range(0, E * C, GATHER):
            codes = keep.tile([P, GATHER], U32, name="slot_codes%d" % at, align_bytes=64)
            scales = keep.tile([P, GATHER], U8, name="slot_scales%d" % at, align_bytes=64)
            part = offs_t[:, at // LIST_ROWS:(at + GATHER) // LIST_ROWS]
            nc.vector.tensor_copy(out=codes[:], in_=x_codes[:].indirect(part))
            nc.vector.tensor_copy(out=scales[:], in_=x_scales[:].indirect(part))
            for q in range(GATHER // C):
                slot_q[at // C + q] = (codes[:, q * C:(q + 1) * C], scales[:, q * C:(q + 1) * C])

        late = E
        leads = dict(LEADS)
        leads[late] = (E - 1,)
        led_by = {e: b for b, experts in leads.items() for e in experts}
        led = {}

        def led_tile(b):
            if b not in led:
                led[b] = ring.tile([P, WIDTHS[0]], BF16, name="led", tag="led", bufs=LED_BUFS, align_bytes=64)
            return led[b]

        kept = HIDDEN // J
        led_words = (E - 1) * kept + HALF // J
        led_codes = keep.tile([P, led_words], U32, name="led_codes", align_bytes=64)
        led_scales = keep.tile([P, led_words], U8, name="led_scales", align_bytes=64)
        h_q = {}

        def code_tiles(words):
            codes = ring.tile([P, words], U32, name="codes", tag="codes", bufs=CODE_BUFS, align_bytes=64)
            scales = ring.tile([P, words], U8, name="scales", tag="scales", bufs=CODE_BUFS, align_bytes=64)
            return codes[:], scales[:]

        def quantise(values, experts):
            n = values.shape[1]
            if experts:
                words = slice(experts[0] * kept, experts[0] * kept + n // J)
                codes, scales = led_codes[:, words], led_scales[:, words]
                for i in range(len(experts) * G):
                    h_q[experts[0] + i // G, i % G] = (codes[:, i * C:(i + 1) * C], scales[:, i * C:(i + 1) * C])
            else:
                codes, scales = code_tiles(n // J)
            at = 0
            while at < n:
                width = max(w for w in WIDTHS if w <= n - at)
                words = slice(at // J, (at + width) // J)
                nc.vector.quantize_mx(out=codes[:, words].bitcast(FP8X4), scales=scales[:, words], in_=values[:, at:at + width])
                at += width
            first = len(experts) * kept
            return codes[:, first:], scales[:, first:]

        steps = []
        for b in range(E):
            earlier = [(b - 1, 1)] if 0 < b <= DRAIN else []
            if b in leads:
                batches = [((), [half]) for half in earlier] + [(leads[b], [(b, 0)])]
            else:
                batches = [((), earlier + [(b, 0)])]
            steps.append(batches + ([((), [(b, 1)])] if b >= DRAIN else []))
        home = {}
        for b, batches in enumerate(steps):
            for i, (experts, halves) in enumerate(batches):
                for r, half in enumerate(halves):
                    home[half] = (b, i, len(experts) * HIDDEN + r * HALF)
        plain = {}

        def batch_tile(b, i):
            experts, halves = steps[b][i]
            if experts:
                return led_tile(b)[:, 0:len(experts) * HIDDEN + HALF]
            if (b, i) not in plain:
                plain[b, i] = grouped_tile([P, len(halves) * HALF], BF16)
            return plain[b, i][:]

        for b in range(E):
            shared = W1_VECTOR if b >= SHARED_FROM else 0
            for g, engine, columns in ((0, "V", slice(0, 128)), (1, "V", slice(0, shared)), (1, "S", slice(shared, 128))):
                if columns.start == columns.stop:
                    continue
                step, i, at = home[b, g]
                dst = batch_tile(step, i)[:, at:at + HALF].rearrange("p (t m u j) -> p m u t j", t=J, u=2, j=2)
                src = w1_raw[b][:, :, g * PASS:(g + 1) * PASS].rearrange("p (u j) (m t) -> p m u t j", t=J, j=2)
                copier[engine](out=dst[:, columns], in_=src[:, columns])
            issue(b)
            for i, (experts, halves) in enumerate(steps[b]):
                codes, scales = quantise(batch_tile(b, i), experts)
                for r, (e, g) in enumerate(halves):
                    xc, xs = slot_q[e]
                    acc = psum.tile([P, J, C], F32, name="acc", tag="acc", bufs=2 * G)
                    for q in range(J):
                        s = slice((J * r + q) * 128, (J * r + q + 1) * 128)
                        nc.tensor.matmul_mx(out=acc[:, q, :], lhsT=codes[:, s].bitcast(FP8X4), lhsT_scale=scales[:, s],
                                            rhs=xc.bitcast(FP8X4), rhs_scale=xs, start=True, stop=True)
                    at = (e - leads[led_by[e]][0]) * HIDDEN + g * OPERAND
                    nc.scalar.activation(led_tile(led_by[e])[:, at:at + OPERAND].rearrange("p (n j) -> p n j", j=J),
                                         acc[:].rearrange("p t n -> p n t"), SILU)

        y_bank = {}
        load_of = [l for l, load in enumerate(W2_LOADS) for v in load]
        share = [v for load in W2_LOADS for v in load]
        pieces = []
        for b, widths in enumerate(W2_BATCHES):
            for n in widths:
                at = pieces[-1][2] if pieces else 0
                pieces.append((b, at, at + n))
        first_of = {b: min(a for i, a, z in pieces if i == b) // 2 for b in range(len(W2_BATCHES))}
        batch_of = [b for b, a, z in pieces for half in range(a, z) if half % 2 == 0]
        cut = [z // 2 for b, a, z in pieces if z % 2 and a < z - 1]
        staged = {}
        coded = {}

        def stage(b):
            if b not in staged:
                n = sum(W2_BATCHES[b]) * OPERAND // 2
                staged[b] = led_tile(late)[:, 0:HIDDEN + n] if b == LATE_BATCH else grouped_tile([P, n], BF16)[:]
            return staged[b]

        def empty(bank, engine):
            a, z = Y_BANKS[bank]
            copier[engine](out=y_all[:, a * C:z * C], in_=y_bank[bank][:].rearrange("p e n -> p (e n)"))

        def copy_load(l):
            first = load_of.index(l)
            for engine in "VS":
                slab = first
                while slab < first + len(W2_LOADS[l]):
                    n = 1
                    nxt = slab + 1
                    if nxt < first + len(W2_LOADS[l]) and (share[nxt], batch_of[nxt]) == (share[slab], batch_of[slab]):
                        n = 2
                    columns = (0, share[slab]) if engine == "V" else (share[slab], N)
                    if slab in cut and engine == "V":
                        columns = (0, N // 2, N)
                    for a, z in zip(columns, columns[1:]):
                        if a < z:
                            b = batch_of[slab]
                            at = (slab - first_of[b]) * OPERAND + (HIDDEN if b == LATE_BATCH else 0)
                            dst = stage(b)[:, at:at + n * OPERAND].rearrange("p (s c i j) -> p s c j i", c=N // 2, i=2, j=J)
                            src = w2_raw[l][:, slab - first:slab - first + n].rearrange("p s j (c i) -> p s c j i", i=2)
                            copier[engine](out=dst[:, :, a // 2:z // 2], in_=src[:, :, a // 2:z // 2])
                    slab += n

        def multiply(b, a, z):
            if b == LATE_BATCH:
                coded[b] = quantise(stage(b), leads[late])
            else:
                if b not in coded:
                    coded[b] = code_tiles(stage(b).shape[1] // J)
                values = slice((a - 2 * first_of[b]) * OPERAND // 2, (z - 2 * first_of[b]) * OPERAND // 2)
                words = slice(values.start // J, values.stop // J)
                nc.vector.quantize_mx(out=coded[b][0][:, words].bitcast(FP8X4), scales=coded[b][1][:, words], in_=stage(b)[:, values])
            codes, scales = coded[b]
            for slab in range(a // 2, z // 2):
                e, g = divmod(slab, G)
                bank = [i for i, (lo, hi) in enumerate(Y_BANKS) if lo <= e < hi][0]
                lo, hi = Y_BANKS[bank]
                if bank not in y_bank:
                    if bank < 2:
                        y_bank[bank] = psum.tile([N, hi - lo, C], F32, name="acc_y", tag="acc_y", bufs=2)
                    else:
                        y_bank[bank] = psum.tile([N, hi - lo, C], F32, name="acc_late", tag="acc", bufs=2 * G)
                hc, hs = h_q[e, g]
                s = slice((slab - first_of[b]) * N, (slab - first_of[b] + 1) * N)
                nc.tensor.matmul_mx(out=y_bank[bank][:, e - lo, :], lhsT=codes[:, s].bitcast(FP8X4), lhsT_scale=scales[:, s],
                                    rhs=hc.bitcast(FP8X4), rhs_scale=hs, start=(g == 0), stop=(g == G - 1))

        second = []

        def spread():
            banks = [psum.tile([P, 512], F32, name="second", tag="second", bufs=2) for b in range(2)]
            filled = [0, 0]
            for tokens, b in zip(chunks, CHUNK_BANKS):
                second.append(banks[b][:, filled[b]:filled[b] + tokens.stop - tokens.start])
                filled[b] += tokens.stop - tokens.start
                nc.tensor.matmul(second[-1], ones[:], row[:, tokens], start=True, stop=True)

        due = [max(load_of[s] + (share[s] < N) for s in range(a // 2, (z + 1) // 2)) for b, a, z in pieces]
        done = 0
        for l in range(len(W2_LOADS) + 1):
            if l < len(W2_LOADS):
                copy_load(l)
            if l == EARLY_LOAD:
                empty(0, "S")
            if l == ROW_BEFORE:
                spread()
            if l == len(W2_LOADS) - 2:
                issue(E)
            while done < len(due) and due[done] <= l:
                multiply(*pieces[done])
                done += 1
        for bank, engine in ((1, "S"), (2, "V"), (3, "S")):
            empty(bank, engine)

        terms = grouped_tile([P, 2, T], F32)

        def fetched(pos_t, tokens):
            return y_all[:].indirect(pos_t[:, tokens.start // LIST_ROWS:tokens.stop // LIST_ROWS])

        def add(engine, tokens):
            engine.tensor_tensor(terms[:, 0, tokens], terms[:, 0, tokens], terms[:, 1, tokens], ADD)
            nc.sync.dma_start(out=out[:, tokens], in_=terms[:, 0, tokens])

        nc.vector.tensor_tensor(terms[:, 0, :], fetched(pos1_t, slice(0, T)), gate_t[:], MULT)
        for tokens in chunks:
            nc.scalar.activation(terms[:, 1, tokens], fetched(pos2_t, tokens), COPY)
        for tokens, weight in zip(chunks, second):
            nc.vector.tensor_tensor(terms[:, 1, tokens], terms[:, 1, tokens], weight, MULT)
        add(nc.gpsimd, stores[0])
        for tokens in stores[1:]:
            add(nc.vector, tokens)
